import numpy as np
import ml_dtypes


def mxq(x, axis, fmt="e4m3"):
    dtype, down = {"e4m3": (ml_dtypes.float8_e4m3fn, 7), "e5m2": (ml_dtypes.float8_e5m2, 14)}[fmt]
    v = np.moveaxis(np.asarray(x, np.float32).astype(ml_dtypes.bfloat16).astype(np.float64), axis, -1)
    blocks = v.reshape(v.shape[:-1] + (-1, 32))
    amax = np.abs(blocks).max(-1, keepdims=True)
    byte = np.maximum(np.where(amax > 0, np.frexp(amax)[1] - 1 + 127, 0) - down, 1)
    scale = np.exp2(byte - 127.0)
    codes = (blocks / scale).astype(np.float32).astype(dtype).astype(np.float64)
    return np.moveaxis((codes * scale).reshape(v.shape), -1, axis)


WIDE = False


def mx_kscale(k):
    if not WIDE:
        return np.ones(k)
    levels = np.array([10, -10, 5, -5, 0])
    if k % 512:
        return np.exp2(np.random.permutation(np.resize(levels, k // 32))).repeat(32)
    a = np.empty((k // 512, 16))
    for p in range(k // 512):
        a[p, :8] = np.random.permutation(np.resize(levels, 8))
        for g in range(8):
            far = levels[np.abs(levels - a[p, g]) >= 10]
            a[p, g + 8] = far[np.random.randint(len(far))]
    return np.exp2(a.ravel()).repeat(32)


BF16 = ml_dtypes.bfloat16


def bf(x):
    return np.asarray(x, np.float32).astype(BF16)


def f64(x):
    return np.asarray(x).astype(np.float64)

def planes(Y):
    n, m = Y.shape
    b = f64(bf(Y)).reshape(n // 32, 32, m)
    amax = np.abs(b).max(1)
    byte = np.clip(np.where(amax > 0, np.frexp(amax)[1] - 1 + 127 - 7, 1), 1, 254)
    codes = (b * np.exp2(127.0 - byte)[:, None, :]).reshape(n, m).astype(np.float32).astype(ml_dtypes.float8_e4m3fn).view(np.uint8)
    words = codes.reshape(n // 512, 128, 4, m).transpose(0, 1, 3, 2)
    return np.ascontiguousarray(words), np.ascontiguousarray(byte.astype(np.uint8).reshape(n // 512, 16, m))


K, P, B, C, DL, DR = 2, 2, 4, 4, 512, 512

ENERGY = -1.0


def setup_inputs():
    s = mx_kscale(DL)
    t = mx_kscale(C * DR).reshape(C, DR)
    psi = np.random.standard_normal((K, P, DL, DR))
    gl = 1.0 + 0.1 * np.random.standard_normal(DL)
    lenv = np.random.standard_normal((B, DL, DL)) / np.sqrt(DL) + 0.25 * np.eye(DL)
    wmpo = (np.random.standard_normal((B, P, C, P)) + 1.0) * 0.7 / np.sqrt(B * P)
    gr = 1.0 + 0.1 * np.random.standard_normal((C, DR))
    renv = np.random.standard_normal((C, DR, DR)) / np.sqrt(C * DR) + 0.25 * np.eye(DR)
    d = np.random.uniform(0.5, 1.5, (P, DL, DR))
    return {
        "psi": bf(psi),
        "gl": bf(gl * s),
        "lenv": bf(lenv / s[None, None, :]),
        "wmpo": bf(wmpo),
        "gr": bf(gr * t),
        "renv": bf(renv / t[:, :, None]),
        "d": bf(d),
    }


def apply_effective_hamiltonian(psi, gl, lenv, wmpo, gr, renv):
    v = gl[None, None, :, None] * psi
    lq = mxq(lenv.reshape(B * DL, DL), 1, "e4m3")
    vq = mxq(v, 2, "e4m3")
    y = (lq @ vq).reshape(K, P, B, DL, DR)
    z = 0.0
    for b in range(B):
        for s in range(P):
            z = z + wmpo[b, s].T[None, :, :, None, None] * y[:, s, b][:, None, None, :, :]
    z = gr[None, None, :, None, :] * z
    z_joint = np.transpose(z, (0, 1, 3, 2, 4)).reshape(K, P, DL, C * DR)
    renv_joint = renv.reshape(C * DR, DR)
    return mxq(z_joint, 3, "e4m3") @ mxq(renv_joint, 0, "e4m3")


def core(psi, gl, lenv, wmpo, gr, renv, d):
    psi, gl, lenv, wmpo = f64(psi), f64(gl), f64(lenv), f64(wmpo)
    gr, renv, d = f64(gr), f64(renv), f64(d)
    h = apply_effective_hamiltonian(psi, gl, lenv, wmpo, gr, renv)
    q = (h - ENERGY * psi) / (ENERGY - d[None, :, :, :])
    ov = np.sum(psi * q, axis=(1, 2, 3)) / np.sum(psi * psi, axis=(1, 2, 3))
    corr = q - ov[:, None, None, None] * psi
    return corr


def reference(psi, gl, lenv, wmpo, gr, renv, d):
    R_out = core(psi, gl, lenv, wmpo, gr, renv, d)
    words, scales = planes(np.moveaxis(R_out, 3, 0).reshape(512, -1))
    return R_out, words, scales

@@ -1,0 +1,701 @@
+from contextlib import ExitStack
+
+import concourse.mybir as mybir
+from concourse.masks import make_identity
+
+F32 = mybir.dt.float32
+BF16 = mybir.dt.bfloat16
+U32 = mybir.dt.uint32
+I32 = mybir.dt.int32
+U8 = mybir.dt.uint8
+FP8X4 = mybir.dt.float8_e4m3fn_x4
+ALU = mybir.AluOpType
+ACT = mybir.ActivationFunctionType
+AX = mybir.AxisListType
+
+NK, NS, NB, NC, D = 2, 2, 4, 4, 512
+P = 128
+NG = NC * NS
+AB = 16
+NT = D // P
+NBLK = P // AB
+E_BLOCKS = (7, 6)
+
+FLOPS = 2 * 2 * 2048 * 2048 * 512 + 2 * 64 * 2 * 512 * 512
+
+
+def tile_dmrgsinglesitempodavidsoncorrection_x1_kernel(
+    tc, psi, gl, lenv, wmpo, gr, renv, d, out_0, out_1, out_2
+):
+    nc = tc.nc
+    with ExitStack() as ctx:
+        keep = ctx.enter_context(tc.tile_pool(name="keep", bufs=1))
+        work = ctx.enter_context(tc.tile_pool(name="work", bufs=2))
+        psum = ctx.enter_context(tc.psum_pool(name="psum", bufs=2))
+
+        def bank(tag):
+            return psum.tile([P, 512], F32, name="bank_" + tag, tag=tag, bufs=1 if tag in "ht" else 2)
+
+        glb = keep.tile([P, 4], BF16, name="glb")
+        nc.scalar.dma_start(out=glb[:], in_=gl.rearrange("(p j) -> p j", j=4))
+        wb = keep.tile([P, 64], BF16, name="wb")
+        nc.scalar.dma_start(
+            out=wb[:], in_=wmpo.rearrange("b s c t -> (b s c t)").partition_broadcast(P)
+        )
+        grb = keep.tile([P, NC, 4], BF16, name="grb")
+        nc.scalar.dma_start(out=grb[:], in_=gr.rearrange("c (p t) -> p c t", t=4))
+
+        def raw_tile(name):
+            return work.tile([P, 4, 512], BF16, name=name, tag="raw", bufs=8, align_bytes=64)
+
+        def load_lenv(i):
+            t = raw_tile("lnat%d" % i)
+            nc.sync.dma_start(
+                out=t[:], in_=lenv[:, P * i : P * (i + 1), :].rearrange("b a l -> a b l")
+            )
+            return t
+
+        def load_psik(k, s):
+            t = raw_tile("psik%d%d" % (k, s))
+            nc.sync.dma_start(out=t[:], in_=psi[k, s].rearrange("(p j) r -> p j r", j=4))
+            return t
+
+        lnat = {}
+        psik = {}
+        rnat = {}
+        dnat = {}
+        psin = {}
+        lnat[1] = load_lenv(1)
+        psik[0, 0] = load_psik(0, 0)
+        psik[0, 1] = load_psik(0, 1)
+        lnat[0] = load_lenv(0)
+        lnat[2] = load_lenv(2)
+
+        def load_renv(c):
+            rnat[c] = raw_tile("rnat%d" % c)
+            nc.sync.dma_start(out=rnat[c][:], in_=renv[c].rearrange("(p j) n -> p j n", j=4))
+
+        def load_psin(k, t):
+            psin[k, t] = keep.tile([P, NT, 512], BF16, name="psin%d%d" % (k, t))
+            nc.sync.dma_start(out=psin[k, t][:], in_=psi[k, t].rearrange("(i a) p -> a i p", a=P))
+
+        def load_d(t):
+            dnat[t] = raw_tile("dnat%d" % t)
+            nc.sync.dma_start(out=dnat[t][:], in_=d[t].rearrange("(i a) p -> a i p", a=P))
+
+        for c in range(3):
+            load_renv(c)
+
+        def later_loads():
+            load_renv(3)
+            lnat[3] = load_lenv(3)
+            for t in range(NS):
+                load_d(t)
+                load_psin(0, t)
+
+        def last_loads():
+            for s in range(NS):
+                psik[1, s] = load_psik(1, s)
+            for t in range(NS):
+                load_psin(1, t)
+
+
+        ident = keep.tile([P, P], F32, name="ident")
+        make_identity(nc, ident[:])
+        ones = keep.tile([P, P], F32, name="ones")
+        nc.gpsimd.memset(ones[:], 1.0)
+        onecol = keep.tile([P, 1], F32, name="onecol")
+        nc.vector.memset(onecol[:], 1.0)
+        tabl = keep.tile([P, 1], F32, name="tabl")
+        nc.scalar.activation(tabl[:], onecol[:], ACT.Abs_reciprocal_sqrt)
+
+        lcw, lsw = {}, {}
+        for i in (1, 2, 3):
+            lcw[i] = keep.tile([P, 9, P], U32, name="lcw%d" % i, align_bytes=64)
+            lsw[i] = keep.tile([P, 9, P], U8, name="lsw%d" % i, align_bytes=64)
+        lcw[0] = keep.tile([P, 3, P], U32, name="lcw0", align_bytes=64)
+        lsw[0] = keep.tile([P, 3, P], U8, name="lsw0", align_bytes=64)
+
+        def zero_windows(i):
+            nc.gpsimd.memset(lcw[i][:, :, 0:64], 0)
+            n = lsw[i].shape[1]
+            v = lsw[i][:].rearrange("p j w -> p (j w)").bitcast(I32)
+            nc.gpsimd.memset(v.rearrange("p (j w) -> p j w", j=n)[:, :, 0:16], 0)
+
+        for i in (1, 0, 2, 3):
+            zero_windows(i)
+
+        glf = keep.tile([P, 4], F32, name="glf")
+        wf = keep.tile([P, 64], F32, name="wf")
+        dmat = keep.tile([P, AB], F32, name="dmat")
+        sel = keep.tile([P, NG], F32, name="sel")
+        wprod = keep.tile([P, NG, NG], F32, name="wprod")
+        wcol = keep.tile([P, NG], F32, name="wcol")
+        wk = keep.tile([P, P], F32, name="wk")
+        grt = keep.tile([P, NG, 4], F32, name="grt")
+
+        def small_constants():
+            nc.vector.tensor_copy(out=glf[:], in_=glb[:])
+            nc.vector.tensor_copy(out=wf[:], in_=wb[:])
+            nc.vector.tensor_reduce(
+                out=dmat[:], in_=ident[:].rearrange("p (q a) -> p a q", a=AB), axis=AX.X, op=ALU.add
+            )
+            nc.vector.tensor_reduce(
+                out=sel[:], in_=ident[:].rearrange("p (q a) -> p q a", a=AB), axis=AX.X, op=ALU.add
+            )
+            nc.vector.tensor_copy(
+                out=grt[:].rearrange("p (c s) t -> p c s t", s=NS),
+                in_=grb[:].unsqueeze(2).to_broadcast([P, NC, NS, 4]),
+            )
+            nc.vector.tensor_tensor(
+                out=wprod[:].rearrange("p g (s b) -> p g s b", s=NS),
+                in0=wf[:].rearrange("p (b s g) -> p g s b", b=NB, s=NS),
+                in1=sel[:].rearrange("p (s b) -> p s b", s=NS).unsqueeze(1).to_broadcast([P, NG, NS, NB]),
+                op=ALU.mult,
+            )
+            nc.vector.tensor_reduce(out=wcol[:], in_=wprod[:], axis=AX.X, op=ALU.add)
+            nc.vector.tensor_tensor(
+                out=wk[:].rearrange("p (g a) -> p g a", a=AB),
+                in0=wcol[:].unsqueeze(2).to_broadcast([P, NG, AB]),
+                in1=dmat[:].unsqueeze(1).to_broadcast([P, NG, AB]),
+                op=ALU.mult,
+            )
+
+        def stage_tile(name):
+            return work.tile([P, 2048], BF16, name=name, tag="st", bufs=4, align_bytes=64)
+
+        def quant(codes, scales, src):
+            nc.vector.quantize_mx(out=codes.bitcast(FP8X4), scales=scales, in_=src)
+
+        lst = {}
+        xlen = {}
+
+        def lenv_pe(i):
+            words = lnat[i][:].rearrange("p b l -> p (b l)").bitcast(F32)
+            for h in range(2):
+                x = bank("ht"[h])
+                xlen[i, h] = x
+                for bb in range(2):
+                    b = 2 * h + bb
+                    for u in range(2):
+                        nc.tensor.transpose(
+                            x[:, (2 * bb + u) * P : (2 * bb + u + 1) * P],
+                            words[:, 256 * b + u : 256 * (b + 1) : 2],
+                            ident[:],
+                        )
+
+        def lenv_view(i, b):
+            return xlen[i, b // 2][:, (b % 2) * 256 : (b % 2) * 256 + 256]
+
+        def lenv_evac(i, engines):
+            lst[i] = stage_tile("lst%d" % i)
+            dst = lst[i][:].bitcast(F32).rearrange("p (k b a u) -> p k b a u", k=NBLK, b=NB, a=AB)
+            for b in range(NB):
+                src = lenv_view(i, b).rearrange("p (u k a) -> p k a u", u=2, k=NBLK)
+                if engines[b] == "s":
+                    nc.scalar.copy(out=dst[:, :, b], in_=src)
+                else:
+                    nc.vector.tensor_copy(out=dst[:, :, b], in_=src)
+
+        def lenv_quant(i, blks):
+            for j in blks:
+                quant(lcw[i][:, j, 64:128], lsw[i][:, j, 64:128], lst[i][:, 256 * j : 256 * (j + 1)])
+
+        lc0 = keep.tile([P, 512], U32, name="lc0", align_bytes=64)
+        ls0 = keep.tile([P, 512], U8, name="ls0", align_bytes=64)
+        lst0k = keep.tile([P, 2, 256], BF16, name="lst0k", align_bytes=64)
+
+        def lenv0_evac():
+            lst[0] = stage_tile("lst0")
+            dst = lst[0][:].bitcast(F32).rearrange("p (b a u) -> p b a u", b=NB, a=P)
+            dstk = lst0k[:].rearrange("p k w -> p (k w)").bitcast(F32).rearrange(
+                "p (k b a u) -> p k b a u", k=2, b=NB, a=AB
+            )
+            for b in range(NB):
+                v = lenv_view(0, b)
+                nc.scalar.copy(out=dst[:, b], in_=v.rearrange("p (u a) -> p a u", u=2))
+            for b in range(NB):
+                v = lenv_view(0, b)
+                nc.scalar.copy(
+                    out=dstk[:, :, b],
+                    in_=v.rearrange("p (u k a) -> p k a u", u=2, k=NBLK)[:, 6:8],
+                )
+
+        vc, vs, vst = {}, {}, {}
+        for k in range(NK):
+            for s in range(NS):
+                vc[k, s] = keep.tile([P, 512], U32, name="vc%d%d" % (k, s), align_bytes=64)
+                vs[k, s] = keep.tile([P, 512], U8, name="vs%d%d" % (k, s), align_bytes=64)
+
+        def v_on_vector(k, s):
+            vst[k, s] = stage_tile("vst%d%d" % (k, s))
+            nc.vector.tensor_tensor(
+                out=vst[k, s][:].rearrange("p (t q j) -> p t q j", t=4, j=4),
+                in0=psik[k, s][:].rearrange("p j (q t) -> p t q j", t=4),
+                in1=glb[:].unsqueeze(1).unsqueeze(1).to_broadcast([P, 4, P, 4]),
+                op=ALU.mult,
+            )
+
+        vsc = keep.tile([P, 4, 512], BF16, name="vsc")
+
+        def v_scale_on_scalar(k, s):
+            for j in range(4):
+                nc.scalar.activation(vsc[:, j, :], psik[k, s][:, j, :], ACT.Copy, scale=glf[:, j : j + 1])
+
+        def v_interleave(k, s):
+            vst[k, s] = stage_tile("vst%d%d" % (k, s))
+            nc.vector.tensor_copy(
+                out=vst[k, s][:].rearrange("p (t q j) -> p t q j", t=4, j=4),
+                in_=vsc[:].rearrange("p j (q t) -> p t q j", t=4),
+            )
+
+        def v_on_gpsimd(k, s, t):
+            if t == 0:
+                vst[k, s] = stage_tile("vst%d%d" % (k, s))
+            nc.gpsimd.tensor_tensor(
+                out=vst[k, s][:].rearrange("p (t q j) -> p t q j", t=4, j=4)[:, t],
+                in0=psik[k, s][:].rearrange("p j (q t) -> p t q j", t=4)[:, t],
+                in1=glb[:].unsqueeze(1).to_broadcast([P, P, 4]),
+                op=ALU.mult,
+            )
+
+        def v_quant(k, s):
+            quant(vc[k, s][:], vs[k, s][:], vst[k, s][:])
+
+        rc, rs, rst = {}, {}, {}
+        for c in range(NC):
+            rc[c] = keep.tile([P, 512], U32, name="rc%d" % c, align_bytes=64)
+            rs[c] = keep.tile([P, 512], U8, name="rs%d" % c, align_bytes=64)
+
+        def r_copy(c, part, eng):
+            if part == 0:
+                rst[c] = stage_tile("rst%d" % c)
+            dst = rst[c][:].rearrange("p (n j) -> p n j", j=4)[:, P * part : P * (part + 1)]
+            src = rnat[c][:].rearrange("p j n -> p n j")[:, P * part : P * (part + 1)]
+            if eng == "s":
+                nc.scalar.copy(out=dst, in_=src)
+            else:
+                nc.gpsimd.tensor_scalar(dst, src, 1.0, 0.0, ALU.mult, ALU.add)
+
+        def r_quant(c):
+            quant(rc[c][:], rs[c][:], rst[c][:])
+
+        rd = {}
+        rtmp = {}
+        for t in range(NS):
+            for i in range(NT):
+                rd[t, i] = keep.tile([P, 512], F32, name="rd%d%d" % (t, i))
+
+        def rd_s(t, i):
+            a = work.tile([P, 512], F32, name="ra", tag="ra", bufs=2)
+            g = work.tile([P, 512], F32, name="rg", tag="rg", bufs=2)
+            rtmp[t, i] = (a, g)
+            src = dnat[t][:, i, :]
+            return [
+                lambda: nc.scalar.activation(a[:], src, ACT.Abs_reciprocal_sqrt, bias=onecol[:, 0:1]),
+                lambda: nc.scalar.activation(g[:], src, ACT.Sign, bias=onecol[:, 0:1]),
+                lambda: nc.scalar.activation(a[:], a[:], ACT.Square),
+            ]
+
+        def rd_g(t, i):
+            a, g = rtmp[t, i]
+            nc.gpsimd.tensor_tensor(out=rd[t, i][:], in0=a[:], in1=g[:], op=ALU.mult)
+
+        stat = {}
+        for k in range(NK):
+            stat[k] = keep.tile([P, 2, NG], F32, name="stat%d" % k)
+
+        def psi_square(k, t, i):
+            junk = work.tile([P, 512], BF16, name="junk", tag="junk", bufs=2)
+            j = t * NT + i
+            nc.scalar.activation(
+                junk[:], psin[k, t][:, i, :], ACT.Square, accum_out=stat[k][:, 1, j : j + 1]
+            )
+
+        blocks = []
+        for k in range(NK):
+            order = [(1, j) for j in range(NBLK)] + [(2, j) for j in range(NBLK)]
+            order += [(0, j) for j in range(E_BLOCKS[k], NBLK)] + [(3, j) for j in range(NBLK)]
+            blocks += [(k, i, j) for i, j in order]
+        ybank, ysb, zbank, zst, zc, zs = {}, {}, {}, {}, {}, {}
+
+        def m1(n):
+            k, i, j = blocks[n]
+            ybank[n] = bank("y")
+            jj = j - 6 if i == 0 else j
+            cw = lcw[i][:].rearrange("p j w -> p (j w)")
+            sw = lsw[i][:].rearrange("p j w -> p (j w)")
+            for s in range(NS):
+                c0 = P * jj + 64 - 64 * s
+                nc.tensor.matmul_mx(
+                    out=ybank[n][:],
+                    lhsT=cw[:, c0 : c0 + P].bitcast(FP8X4),
+                    lhsT_scale=sw[:, c0 : c0 + P],
+                    rhs=vc[k, s][:].bitcast(FP8X4),
+                    rhs_scale=vs[k, s][:],
+                    start=(s == 0),
+                    stop=(s == 1),
+                )
+
+        def e1(n):
+            ysb[n] = work.tile([P, 512], F32, name="ysb", tag="ysb", bufs=3)
+            nc.scalar.copy(out=ysb[n][:], in_=ybank[n][:])
+
+        def m2(n):
+            zbank[n] = bank("z")
+            for t in range(4):
+                nc.tensor.matmul(
+                    zbank[n][:, P * t : P * (t + 1)],
+                    ysb[n][:, P * t : P * (t + 1)],
+                    wk[:],
+                    start=True,
+                    stop=True,
+                )
+
+        def zst_tile(k, i):
+            if (k, i) not in zst:
+                if i == 0:
+                    zst[k, i] = work.tile([P, NG, P, 4], BF16, name="zse", tag="zse", bufs=1, align_bytes=64)
+                else:
+                    zst[k, i] = work.tile([P, NG, P, 4], BF16, name="zst", tag="zst", bufs=2, align_bytes=64)
+            return zst[k, i]
+
+        def e2(n):
+            k, i, j = blocks[n]
+            nc.vector.tensor_tensor(
+                out=zst_tile(k, i)[:, :, AB * j : AB * (j + 1), :],
+                in0=zbank[n][:].rearrange("p (t g a) -> p g a t", t=4, g=NG),
+                in1=grt[:].unsqueeze(2).to_broadcast([P, NG, AB, 4]),
+                op=ALU.mult,
+            )
+
+        ebank, acc = {}, {}
+
+        def em(k, q):
+            b, s = divmod(q, NS)
+            ebank[k, q] = bank("e")
+            for t in range(4):
+                nc.tensor.matmul_mx(
+                    out=ebank[k, q][:, P * t : P * (t + 1)],
+                    lhsT=vc[k, s][:, P * t : P * (t + 1)].bitcast(FP8X4),
+                    lhsT_scale=vs[k, s][:, P * t : P * (t + 1)],
+                    rhs=lc0[:, P * b : P * (b + 1)].bitcast(FP8X4),
+                    rhs_scale=ls0[:, P * b : P * (b + 1)],
+                    start=True,
+                    stop=True,
+                )
+
+        def e_in(k, q):
+            na = AB * E_BLOCKS[k]
+            return ebank[k, q][:].rearrange("p (t a) -> p t a", t=4)[:, :, 0:na]
+
+        def fma(k, q, g):
+            w = wf[:, NG * q + g : NG * q + g + 1]
+            if q == 0:
+                na = AB * E_BLOCKS[k]
+                acc[k, g] = work.tile([P, 4, na], F32, name="acc%d" % g, tag="acc%d" % g, bufs=1)
+                nc.scalar.activation(acc[k, g][:], e_in(k, 0), ACT.Copy, scale=w)
+            else:
+                nc.vector.scalar_tensor_tensor(
+                    out=acc[k, g][:], in0=e_in(k, q), scalar=w, in1=acc[k, g][:], op0=ALU.mult, op1=ALU.add
+                )
+
+        def e_final(k, g):
+            na = AB * E_BLOCKS[k]
+            nc.gpsimd.tensor_tensor(
+                out=zst_tile(k, 0)[:, g, 0:na, :],
+                in0=acc[k, g][:].rearrange("p t a -> p a t"),
+                in1=grt[:, g : g + 1, :].to_broadcast([P, na, 4]),
+                op=ALU.mult,
+            )
+
+        hbank, qt = {}, {}
+
+        def z_quant(k, i):
+            zc[k, i] = work.tile([P, 1024], U32, name="zc", tag="zc", bufs=2, align_bytes=64)
+            zs[k, i] = work.tile([P, 1024], U8, name="zs", tag="zs", bufs=2, align_bytes=64)
+            quant(zc[k, i][:], zs[k, i][:], zst[k, i][:].rearrange("p g a t -> p (g a t)"))
+
+        def m3(k, i, t, tag):
+            hbank[k, i, t] = bank(tag)
+            for c in range(NC):
+                c0 = (NS * c + t) * P
+                nc.tensor.matmul_mx(
+                    out=hbank[k, i, t][:],
+                    lhsT=zc[k, i][:, c0 : c0 + P].bitcast(FP8X4),
+                    lhsT_scale=zs[k, i][:, c0 : c0 + P],
+                    rhs=rc[c][:].bitcast(FP8X4),
+                    rhs_scale=rs[c][:],
+                    start=(c == 0),
+                    stop=(c == NC - 1),
+                )
+
+        ut = {}
+
+        def ep_u(k, i, t):
+            ut[k, i, t] = work.tile([P, 512], F32, name="u", tag="u", bufs=2)
+            nc.vector.scalar_tensor_tensor(
+                out=ut[k, i, t][:],
+                in0=hbank[k, i, t][:],
+                scalar=-1.0,
+                in1=psin[k, t][:, i, :],
+                op0=ALU.mult,
+                op1=ALU.subtract,
+            )
+
+        def ep_q(k, i, t, eng):
+            qt[k, i, t] = work.tile([P, 512], F32, name="q", tag="q", bufs=10)
+            e = nc.gpsimd if eng == "g" else nc.vector
+            e.tensor_tensor(out=qt[k, i, t][:], in0=ut[k, i, t][:], in1=rd[t, i][:], op=ALU.mult)
+
+        pq = {}
+
+        def ep_p(k, i, t):
+            pq[k, i, t] = work.tile([P, 512], F32, name="pq", tag="pq", bufs=2)
+            nc.gpsimd.tensor_tensor(
+                out=pq[k, i, t][:], in0=qt[k, i, t][:], in1=psin[k, t][:, i, :], op=ALU.mult
+            )
+
+        def ep_sum(k, i, t):
+            j = t * NT + i
+            nc.scalar.activation(
+                pq[k, i, t][:], pq[k, i, t][:], ACT.Copy, accum_out=stat[k][:, 0, j : j + 1]
+            )
+
+        def ep_sum_v(k, i, t):
+            j = t * NT + i
+            p = work.tile([P, 512], F32, name="pq", tag="pq", bufs=2)
+            nc.vector.scalar_tensor_tensor(
+                out=p[:],
+                in0=qt[k, i, t][:],
+                scalar=1.0,
+                in1=psin[k, t][:, i, :],
+                op0=ALU.mult,
+                op1=ALU.mult,
+                accum_out=stat[k][:, 0, j : j + 1],
+            )
+
+        nov = {}
+        st2 = {}
+        sbank = {}
+
+        def overlap_v1(k):
+            st2[k] = keep.tile([P, 2], F32, name="st2%d" % k)
+            nc.vector.tensor_reduce(out=st2[k][:], in_=stat[k][:], axis=AX.X, op=ALU.add)
+
+        def overlap_pe(k):
+            sbank[k] = bank("t")
+            nc.tensor.matmul(sbank[k][:, 0:2], ones[:], st2[k][:], start=True, stop=True)
+
+        def overlap_v2(k):
+            rden = keep.tile([P, 1], F32, name="rden%d" % k)
+            nov[k] = keep.tile([P, 1], F32, name="nov%d" % k)
+            nc.vector.reciprocal(out=rden[:], in_=sbank[k][:, 1:2])
+            nc.vector.tensor_scalar(nov[k][:], sbank[k][:, 0:1], rden[:, 0:1], -1.0, ALU.mult, ALU.mult)
+
+        cor, cb, ost, xt, oc, osc = {}, {}, {}, {}, {}, {}
+        for k in range(NK):
+            osc[k] = keep.tile([P, 1024], U8, name="osc%d" % k, align_bytes=64)
+
+        def c_corr(k, t, i):
+            cor[k, t, i] = work.tile([P, 512], F32, name="cor", tag="cor", bufs=3)
+            nc.vector.scalar_tensor_tensor(
+                out=cor[k, t, i][:],
+                in0=psin[k, t][:, i, :],
+                scalar=nov[k][:, 0:1],
+                in1=qt[k, i, t][:],
+                op0=ALU.mult,
+                op1=ALU.add,
+            )
+            nc.sync.dma_start(out=out_0[k, t, P * i : P * (i + 1), :], in_=cor[k, t, i][:])
+
+        def c_cast(k, t, i):
+            cb[k, t, i] = work.tile([P, 512], BF16, name="cb", tag="cb", bufs=3)
+            nc.scalar.copy(out=cb[k, t, i][:], in_=cor[k, t, i][:])
+
+        def c_turn(k, t, i, tag):
+            if i % 2 == 0:
+                xt[k, t, i // 2] = bank(tag)
+            x = xt[k, t, i // 2]
+            words = cb[k, t, i][:].bitcast(F32)
+            for u in range(2):
+                c0 = (2 * (i % 2) + u) * P
+                nc.tensor.transpose(x[:, c0 : c0 + P], words[:, u:256:2], ident[:])
+
+        def c_evac(k, t, h, eng):
+            if h == 0:
+                ost[k, t] = stage_tile("ost%d%d" % (k, t))
+            dst = ost[k, t][:].bitcast(F32).rearrange("p (i a u) -> p i a u", i=NT, u=2)[:, 2 * h : 2 * h + 2]
+            src = xt[k, t, h][:].rearrange("p (i u a) -> p i a u", i=2, u=2)
+            if eng == "s":
+                nc.scalar.copy(out=dst, in_=src)
+            else:
+                nc.vector.tensor_copy(out=dst, in_=src)
+
+        def c_quant(k, t):
+            oc[k, t] = work.tile([P, 512], U32, name="oc", tag="oc", bufs=2, align_bytes=64)
+            quant(oc[k, t][:], osc[k][:, 512 * t : 512 * (t + 1)], ost[k, t][:])
+            m0 = k * 1024 + t * 512
+            words = out_1.rearrange("g p m t -> (g p) (m t)")[:, 4 * m0 : 4 * (m0 + 512)]
+            nc.sync.dma_start(out=words.bitcast(I32), in_=oc[k, t][:].bitcast(I32))
+
+        def c_scales(k):
+            rows = out_2.rearrange("g q m -> (g q) m")
+            for q in range(4):
+                nc.sync.dma_start(
+                    out=rows[4 * q : 4 * q + 4, 1024 * k : 1024 * (k + 1)].bitcast(I32),
+                    in_=osc[k][32 * q : 32 * q + 4, :].bitcast(I32),
+                )
+
+        lenv_pe(1)
+        small_constants()
+        lenv_evac(1, "ssss")
+        v_on_vector(0, 0)
+        v_scale_on_scalar(0, 1)
+        lenv_quant(1, range(2))
+        v_quant(0, 0)
+        lenv_pe(0)
+        v_interleave(0, 1)
+        v_quant(0, 1)
+        lenv_quant(1, range(2, NBLK))
+        lenv0_evac()
+        quant(lc0[:], ls0[:], lst[0][:])
+        for j in range(2):
+            quant(lcw[0][:, j, 64:128], lsw[0][:, j, 64:128], lst0k[:, j, :])
+
+        later_loads()
+
+        slots = {}
+
+        def at(step, slot, fn, *args):
+            slots.setdefault((step, slot), []).append((fn, args))
+
+        nblocks = len(blocks)
+        first = {0: 0, 1: sum(1 for x in blocks if x[0] == 0)}
+        last_of = {}
+        for n, (k, i, j) in enumerate(blocks):
+            last_of[k, i] = n
+
+        at(6, "v", last_loads)
+        at(1, "pe", lenv_pe, 2)
+        at(1, "s", lenv_evac, 2, "ssss")
+        at(3, "v", lenv_quant, 2, range(NBLK))
+        for c in range(NC):
+            eng = "s" if c % 2 == 0 else "g"
+            for part in range(4):
+                at(3 + c + part // 2, eng, r_copy, c, part, eng)
+            at(5 + c, "v", r_quant, c)
+        at(8, "pe", lenv_pe, 3)
+        at(8, "s", lenv_evac, 3, "ssss")
+        at(12, "v", lenv_quant, 3, range(NBLK))
+        for s in range(NS):
+            for t in range(4):
+                at(13 + 4 * s + t, "g", v_on_gpsimd, 1, s, t)
+            at(18 + 4 * s, "v", v_quant, 1, s)
+
+        def rd_queue(t, i, step):
+            def run():
+                for f in rd_s(t, i):
+                    f()
+            at(step, "s", run)
+            at(step, "g", rd_g, t, i)
+
+        for x, (t, i) in enumerate([(0, 1), (1, 1), (0, 2), (1, 2), (0, 0), (1, 0), (0, 3), (1, 3)]):
+            rd_queue(t, i, (8, 9, 11, 12, 15, 17, 19, 21)[x])
+        for t in range(NS):
+            for i in range(NT):
+                at(13 + t * NT + i, "s", psi_square, 0, t, i)
+                at(34 + t * NT + i, "s", psi_square, 1, t, i)
+
+        for k in range(NK):
+            s0 = first[k] + 2 * k
+            nsteps = 20 if k == 0 else 16
+            at(s0, "pe", em, k, 0)
+            for g in range(NG):
+                at(s0 + g // 4, "s", fma, k, 0, g)
+            for f in range(NG * (NG - 1)):
+                q, g = divmod(f, NG)
+                q += 1
+                step = s0 + 1 + f * nsteps // (NG * (NG - 1))
+                if g == 0:
+                    at(step - 1 if q > 1 else s0, "pe", em, k, q)
+                at(step, "fma", fma, k, q, g)
+                if q == NG - 1:
+                    at(step + 1, "g", e_final, k, g)
+
+        def stage(k, i, step):
+            at(step, "v", z_quant, k, i)
+            for t in range(NS):
+                at(step + 2 + 2 * t, "pe", m3, k, i, t, "h")
+                at(step + 3 + 2 * t, "v", ep_u, k, i, t)
+                at(step + 4 + 2 * t, "g", ep_q, k, i, t, "g")
+                at(step + 4 + 2 * t, "g", ep_p, k, i, t)
+                at(step + 5 + 2 * t, "s", ep_sum, k, i, t)
+
+        for k in range(NK):
+            for i in (1, 2, 3):
+                if (k, i) != (1, 3):
+                    stage(k, i, last_of[k, i] + 1)
+        stage(0, 0, last_of[0, 3] + 5)
+        stage(1, 0, first[1] + 2 + 1 + 16 + 2)
+
+        ov0 = last_of[0, 3] + 13
+        at(ov0, "v", overlap_v1, 0)
+        at(ov0 + 1, "pe", overlap_pe, 0)
+        at(ov0 + 1, "v", overlap_v2, 0)
+        for x in range(NG):
+            t, i = divmod(x, NT)
+            at(ov0 + 3 + x, "v", c_corr, 0, t, i)
+            at(ov0 + 4 + x, "s", c_cast, 0, t, i)
+            if i % 2 == 1:
+                at(ov0 + 6 + x, "pe", c_turn, 0, t, i - 1, "t")
+                at(ov0 + 6 + x, "pe", c_turn, 0, t, i, "t")
+                at(ov0 + 6 + x, "s", c_evac, 0, t, i // 2, "s")
+            if i == 3:
+                at(ov0 + 8 + x, "v", c_quant, 0, t)
+        at(ov0 + 9 + NG, "v", c_scales, 0)
+
+        def run(step, slot):
+            for fn, args in slots.pop((step, slot), []):
+                fn(*args)
+
+        m1(0)
+        e1(0)
+        for n in range(nblocks):
+            if n + 1 < nblocks:
+                m1(n + 1)
+            run(n, "pe")
+            m2(n)
+            if n + 1 < nblocks:
+                e1(n + 1)
+            run(n, "s")
+            if n > 0:
+                e2(n - 1)
+            run(n, "fma")
+            run(n, "g")
+            run(n, "v")
+        e2(nblocks - 1)
+        z_quant(1, 3)
+        for n in range(nblocks, nblocks + 20):
+            for slot in ("pe", "s", "fma", "g", "v"):
+                run(n, slot)
+        m3(1, 3, 0, "h")
+        m3(1, 3, 1, "y")
+        for t in range(NS):
+            ep_u(1, 3, t)
+            ep_q(1, 3, t, "v")
+        for t in range(NS):
+            ep_sum_v(1, 3, t)
+        overlap_v1(1)
+        overlap_pe(1)
+        overlap_v2(1)
+        assert not slots, sorted(slots)
+        for t in range(NS):
+            for i in range(NT):
+                c_corr(1, t, i)
+                c_cast(1, t, i)
+                c_turn(1, t, i, "ez"[t])
+                if i % 2 == 1:
+                    c_evac(1, t, i // 2, "sv"[i // 2])
+            c_quant(1, t)
+        c_scales(1)

@@ -20,8 +20,22 @@ AB = 16
 NT = D // P
 NBLK = P // AB
 E_BLOCKS = (7, 6)
+KMIN = NBLK - max(NBLK - x for x in E_BLOCKS)
 
 FLOPS = 2 * 2 * 2048 * 2048 * 512 + 2 * 64 * 2 * 512 * 512
+
+S_BUDGET = 1150
+V_BUDGET = 1700
+G_BUDGET = 1800
+LAG_M3 = 2
+LAG_U = 1
+LAG_Q = 1
+LAG_SUM = 3
+LAG_ZE = 2
+LAG_CAST = 1
+LAG_TURN = 2
+EM_AT = 6
+PACE = 2.75
 
 
 def tile_dmrgsinglesitempodavidsoncorrection_x1_kernel(
@@ -32,44 +46,27 @@ def tile_dmrgsinglesitempodavidsoncorrection_x1_kernel(
         keep = ctx.enter_context(tc.tile_pool(name="keep", bufs=1))
         work = ctx.enter_context(tc.tile_pool(name="work", bufs=2))
         psum = ctx.enter_context(tc.psum_pool(name="psum", bufs=2))
+        ctx.enter_context(tc.manual_schedule())
+
+        bank_bufs = {"y": 2, "z": 2, "e": 2, "h": 1, "t": 1}
 
         def bank(tag):
-            return psum.tile([P, 512], F32, name="bank_" + tag, tag=tag, bufs=1 if tag in "ht" else 2)
+            return psum.tile([P, 512], F32, name="bank_" + tag, tag=tag, bufs=bank_bufs[tag])
 
-        glb = keep.tile([P, 4], BF16, name="glb")
-        nc.scalar.dma_start(out=glb[:], in_=gl.rearrange("(p j) -> p j", j=4))
-        wb = keep.tile([P, 64], BF16, name="wb")
-        nc.scalar.dma_start(
-            out=wb[:], in_=wmpo.rearrange("b s c t -> (b s c t)").partition_broadcast(P)
-        )
-        grb = keep.tile([P, NC, 4], BF16, name="grb")
-        nc.scalar.dma_start(out=grb[:], in_=gr.rearrange("c (p t) -> p c t", t=4))
+        lnat, psik, rnat, dnat, psin = {}, {}, {}, {}, {}
 
         def raw_tile(name):
             return work.tile([P, 4, 512], BF16, name=name, tag="raw", bufs=8, align_bytes=64)
 
         def load_lenv(i):
-            t = raw_tile("lnat%d" % i)
+            lnat[i] = raw_tile("lnat%d" % i)
             nc.sync.dma_start(
-                out=t[:], in_=lenv[:, P * i : P * (i + 1), :].rearrange("b a l -> a b l")
+                out=lnat[i][:], in_=lenv[:, P * i : P * (i + 1), :].rearrange("b a l -> a b l")
             )
-            return t
 
         def load_psik(k, s):
-            t = raw_tile("psik%d%d" % (k, s))
-            nc.sync.dma_start(out=t[:], in_=psi[k, s].rearrange("(p j) r -> p j r", j=4))
-            return t
-
-        lnat = {}
-        psik = {}
-        rnat = {}
-        dnat = {}
-        psin = {}
-        lnat[1] = load_lenv(1)
-        psik[0, 0] = load_psik(0, 0)
-        psik[0, 1] = load_psik(0, 1)
-        lnat[0] = load_lenv(0)
-        lnat[2] = load_lenv(2)
+            psik[k, s] = raw_tile("psik%d%d" % (k, s))
+            nc.sync.dma_start(out=psik[k, s][:], in_=psi[k, s].rearrange("(p j) r -> p j r", j=4))
 
         def load_renv(c):
             rnat[c] = raw_tile("rnat%d" % c)
@@ -83,38 +80,48 @@ def tile_dmrgsinglesitempodavidsoncorrection_x1_kernel(
             dnat[t] = raw_tile("dnat%d" % t)
             nc.sync.dma_start(out=dnat[t][:], in_=d[t].rearrange("(i a) p -> a i p", a=P))
 
+        glb = keep.tile([P, 4], BF16, name="glb")
+        nc.scalar.dma_start(out=glb[:], in_=gl.rearrange("(p j) -> p j", j=4))
+        load_psik(0, 0)
+        load_psik(0, 1)
+        load_lenv(1)
+        wb = keep.tile([P, 64], BF16, name="wb")
+        nc.scalar.dma_start(
+            out=wb[:], in_=wmpo.rearrange("b s c t -> (b s c t)").partition_broadcast(P)
+        )
+        grb = keep.tile([P, NC, 4], BF16, name="grb")
+        nc.scalar.dma_start(out=grb[:], in_=gr.rearrange("c (p t) -> p c t", t=4))
+        load_lenv(0)
+        load_lenv(2)
         for c in range(3):
             load_renv(c)
 
         def later_loads():
             load_renv(3)
-            lnat[3] = load_lenv(3)
+            load_lenv(3)
             for t in range(NS):
                 load_d(t)
                 load_psin(0, t)
 
         def last_loads():
             for s in range(NS):
-                psik[1, s] = load_psik(1, s)
+                load_psik(1, s)
             for t in range(NS):
                 load_psin(1, t)
 
-
         ident = keep.tile([P, P], F32, name="ident")
         make_identity(nc, ident[:])
-        ones = keep.tile([P, P], F32, name="ones")
-        nc.gpsimd.memset(ones[:], 1.0)
         onecol = keep.tile([P, 1], F32, name="onecol")
         nc.vector.memset(onecol[:], 1.0)
         tabl = keep.tile([P, 1], F32, name="tabl")
         nc.scalar.activation(tabl[:], onecol[:], ACT.Abs_reciprocal_sqrt)
+        ones = keep.tile([P, P], F32, name="ones")
 
         lcw, lsw = {}, {}
-        for i in (1, 2, 3):
-            lcw[i] = keep.tile([P, 9, P], U32, name="lcw%d" % i, align_bytes=64)
-            lsw[i] = keep.tile([P, 9, P], U8, name="lsw%d" % i, align_bytes=64)
-        lcw[0] = keep.tile([P, 3, P], U32, name="lcw0", align_bytes=64)
-        lsw[0] = keep.tile([P, 3, P], U8, name="lsw0", align_bytes=64)
+        for i in (1, 0, 2, 3):
+            n = 3 if i == 0 else 9
+            lcw[i] = keep.tile([P, n, P], U32, name="lcw%d" % i, align_bytes=64)
+            lsw[i] = keep.tile([P, n, P], U8, name="lsw%d" % i, align_bytes=64)
 
         def zero_windows(i):
             nc.gpsimd.memset(lcw[i][:, :, 0:64], 0)
@@ -122,11 +129,7 @@ def tile_dmrgsinglesitempodavidsoncorrection_x1_kernel(
             v = lsw[i][:].rearrange("p j w -> p (j w)").bitcast(I32)
             nc.gpsimd.memset(v.rearrange("p (j w) -> p j w", j=n)[:, :, 0:16], 0)
 
-        for i in (1, 0, 2, 3):
-            zero_windows(i)
-
-        glf = keep.tile([P, 4], F32, name="glf")
-        wf = keep.tile([P, 64], F32, name="wf")
+        wf = keep.tile([P, NG, NG], F32, name="wf")
         dmat = keep.tile([P, AB], F32, name="dmat")
         sel = keep.tile([P, NG], F32, name="sel")
         wprod = keep.tile([P, NG, NG], F32, name="wprod")
@@ -135,23 +138,25 @@ def tile_dmrgsinglesitempodavidsoncorrection_x1_kernel(
         grt = keep.tile([P, NG, 4], F32, name="grt")
 
         def small_constants():
-            nc.vector.tensor_copy(out=glf[:], in_=glb[:])
-            nc.vector.tensor_copy(out=wf[:], in_=wb[:])
+            nc.vector.tensor_copy(
+                out=wf[:].rearrange("p q (t c) -> p q t c", t=NS),
+                in_=wb[:].rearrange("p (q c t) -> p q t c", q=NG, t=NS),
+            )
             nc.vector.tensor_reduce(
                 out=dmat[:], in_=ident[:].rearrange("p (q a) -> p a q", a=AB), axis=AX.X, op=ALU.add
             )
             nc.vector.tensor_reduce(
                 out=sel[:], in_=ident[:].rearrange("p (q a) -> p q a", a=AB), axis=AX.X, op=ALU.add
             )
-            nc.vector.tensor_copy(
-                out=grt[:].rearrange("p (c s) t -> p c s t", s=NS),
-                in_=grb[:].unsqueeze(2).to_broadcast([P, NC, NS, 4]),
-            )
             nc.vector.tensor_tensor(
                 out=wprod[:].rearrange("p g (s b) -> p g s b", s=NS),
-                in0=wf[:].rearrange("p (b s g) -> p g s b", b=NB, s=NS),
+                in0=wf[:].rearrange("p (b s) g -> p g s b", s=NS),
                 in1=sel[:].rearrange("p (s b) -> p s b", s=NS).unsqueeze(1).to_broadcast([P, NG, NS, NB]),
                 op=ALU.mult,
+            )
+            nc.vector.tensor_copy(
+                out=grt[:].rearrange("p (s c) t -> p s (c t)", s=NS),
+                in_=grb[:].rearrange("p c t -> p (c t)").unsqueeze(1).to_broadcast([P, NS, 4 * NC]),
             )
             nc.vector.tensor_reduce(out=wcol[:], in_=wprod[:], axis=AX.X, op=ALU.add)
             nc.vector.tensor_tensor(
@@ -167,8 +172,7 @@ def tile_dmrgsinglesitempodavidsoncorrection_x1_kernel(
         def quant(codes, scales, src):
             nc.vector.quantize_mx(out=codes.bitcast(FP8X4), scales=scales, in_=src)
 
-        lst = {}
-        xlen = {}
+        lst, xlen = {}, {}
 
         def lenv_pe(i):
             words = lnat[i][:].rearrange("p b l -> p (b l)").bitcast(F32)
@@ -187,15 +191,13 @@ def tile_dmrgsinglesitempodavidsoncorrection_x1_kernel(
         def lenv_view(i, b):
             return xlen[i, b // 2][:, (b % 2) * 256 : (b % 2) * 256 + 256]
 
-        def lenv_evac(i, engines):
+        def lenv_evac(i):
             lst[i] = stage_tile("lst%d" % i)
             dst = lst[i][:].bitcast(F32).rearrange("p (k b a u) -> p k b a u", k=NBLK, b=NB, a=AB)
             for b in range(NB):
-                src = lenv_view(i, b).rearrange("p (u k a) -> p k a u", u=2, k=NBLK)
-                if engines[b] == "s":
-                    nc.scalar.copy(out=dst[:, :, b], in_=src)
-                else:
-                    nc.vector.tensor_copy(out=dst[:, :, b], in_=src)
+                nc.scalar.copy(
+                    out=dst[:, :, b], in_=lenv_view(i, b).rearrange("p (u k a) -> p k a u", u=2, k=NBLK)
+                )
 
         def lenv_quant(i, blks):
             for j in blks:
@@ -203,23 +205,25 @@ def tile_dmrgsinglesitempodavidsoncorrection_x1_kernel(
 
         lc0 = keep.tile([P, 512], U32, name="lc0", align_bytes=64)
         ls0 = keep.tile([P, 512], U8, name="ls0", align_bytes=64)
-        lst0k = keep.tile([P, 2, 256], BF16, name="lst0k", align_bytes=64)
+        lst0k = keep.tile([P, NBLK - KMIN, 256], BF16, name="lst0k", align_bytes=64)
 
         def lenv0_evac():
             lst[0] = stage_tile("lst0")
             dst = lst[0][:].bitcast(F32).rearrange("p (b a u) -> p b a u", b=NB, a=P)
             dstk = lst0k[:].rearrange("p k w -> p (k w)").bitcast(F32).rearrange(
-                "p (k b a u) -> p k b a u", k=2, b=NB, a=AB
+                "p (k b a u) -> p k b a u", b=NB, a=AB, u=2
             )
             for b in range(NB):
-                v = lenv_view(0, b)
-                nc.scalar.copy(out=dst[:, b], in_=v.rearrange("p (u a) -> p a u", u=2))
+                nc.scalar.copy(out=dst[:, b], in_=lenv_view(0, b).rearrange("p (u a) -> p a u", u=2))
             for b in range(NB):
-                v = lenv_view(0, b)
                 nc.scalar.copy(
                     out=dstk[:, :, b],
-                    in_=v.rearrange("p (u k a) -> p k a u", u=2, k=NBLK)[:, 6:8],
+                    in_=lenv_view(0, b).rearrange("p (u k a) -> p k a u", u=2, k=NBLK)[:, KMIN:NBLK],
                 )
+
+        def lenv0_quant():
+            for j in range(NBLK - KMIN):
+                quant(lcw[0][:, j, 64:128], lsw[0][:, j, 64:128], lst0k[:, j, :])
 
         vc, vs, vst = {}, {}, {}
         for k in range(NK):
@@ -227,37 +231,24 @@ def tile_dmrgsinglesitempodavidsoncorrection_x1_kernel(
                 vc[k, s] = keep.tile([P, 512], U32, name="vc%d%d" % (k, s), align_bytes=64)
                 vs[k, s] = keep.tile([P, 512], U8, name="vs%d%d" % (k, s), align_bytes=64)
 
-        def v_on_vector(k, s):
-            vst[k, s] = stage_tile("vst%d%d" % (k, s))
-            nc.vector.tensor_tensor(
-                out=vst[k, s][:].rearrange("p (t q j) -> p t q j", t=4, j=4),
-                in0=psik[k, s][:].rearrange("p j (q t) -> p t q j", t=4),
-                in1=glb[:].unsqueeze(1).unsqueeze(1).to_broadcast([P, 4, P, 4]),
-                op=ALU.mult,
-            )
-
-        vsc = keep.tile([P, 4, 512], BF16, name="vsc")
-
-        def v_scale_on_scalar(k, s):
-            for j in range(4):
-                nc.scalar.activation(vsc[:, j, :], psik[k, s][:, j, :], ACT.Copy, scale=glf[:, j : j + 1])
-
-        def v_interleave(k, s):
-            vst[k, s] = stage_tile("vst%d%d" % (k, s))
-            nc.vector.tensor_copy(
-                out=vst[k, s][:].rearrange("p (t q j) -> p t q j", t=4, j=4),
-                in_=vsc[:].rearrange("p j (q t) -> p t q j", t=4),
-            )
-
-        def v_on_gpsimd(k, s, t):
-            if t == 0:
+        def v_part(k, s, t0, t1, engine):
+            if (k, s) not in vst:
                 vst[k, s] = stage_tile("vst%d%d" % (k, s))
-            nc.gpsimd.tensor_tensor(
-                out=vst[k, s][:].rearrange("p (t q j) -> p t q j", t=4, j=4)[:, t],
-                in0=psik[k, s][:].rearrange("p j (q t) -> p t q j", t=4)[:, t],
-                in1=glb[:].unsqueeze(1).to_broadcast([P, P, 4]),
-                op=ALU.mult,
-            )
+            for t in range(t0, t1) if engine == "g" else (t0,):
+                n = 1 if engine == "g" else t1 - t0
+                e = nc.gpsimd if engine == "g" else nc.vector
+                out = vst[k, s][:].rearrange("p (t q j) -> p t q j", t=4, j=4)
+                src = psik[k, s][:].rearrange("p j (q t) -> p t q j", t=4)
+                if engine == "g":
+                    e.tensor_tensor(
+                        out=out[:, t], in0=src[:, t],
+                        in1=glb[:].unsqueeze(1).to_broadcast([P, P, 4]), op=ALU.mult,
+                    )
+                else:
+                    e.tensor_tensor(
+                        out=out[:, t0:t1], in0=src[:, t0:t1],
+                        in1=glb[:].unsqueeze(1).unsqueeze(1).to_broadcast([P, n, P, 4]), op=ALU.mult,
+                    )
 
         def v_quant(k, s):
             quant(vc[k, s][:], vs[k, s][:], vst[k, s][:])
@@ -280,30 +271,31 @@ def tile_dmrgsinglesitempodavidsoncorrection_x1_kernel(
         def r_quant(c):
             quant(rc[c][:], rs[c][:], rst[c][:])
 
-        rd = {}
-        rtmp = {}
+        rd, rtmp = {}, {}
         for t in range(NS):
             for i in range(NT):
                 rd[t, i] = keep.tile([P, 512], F32, name="rd%d%d" % (t, i))
 
-        def rd_s(t, i):
-            a = work.tile([P, 512], F32, name="ra", tag="ra", bufs=2)
-            g = work.tile([P, 512], F32, name="rg", tag="rg", bufs=2)
-            rtmp[t, i] = (a, g)
-            src = dnat[t][:, i, :]
-            return [
-                lambda: nc.scalar.activation(a[:], src, ACT.Abs_reciprocal_sqrt, bias=onecol[:, 0:1]),
-                lambda: nc.scalar.activation(g[:], src, ACT.Sign, bias=onecol[:, 0:1]),
-                lambda: nc.scalar.activation(a[:], a[:], ACT.Square),
-            ]
+        def rd_first(t, i):
+            nc.scalar.activation(
+                rd[t, i][:], dnat[t][:, i, :], ACT.Abs_reciprocal_sqrt, bias=onecol[:, 0:1]
+            )
+
+        def rd_second(t, i):
+            rtmp[t, i] = work.tile([P, 512], BF16, name="rg", tag="rg", bufs=8)
+            nc.scalar.activation(rtmp[t, i][:], dnat[t][:, i, :], ACT.Sign, bias=onecol[:, 0:1])
+
+        def rd_third(t, i):
+            nc.scalar.activation(rd[t, i][:], rd[t, i][:], ACT.Square)
 
         def rd_g(t, i):
-            a, g = rtmp[t, i]
-            nc.gpsimd.tensor_tensor(out=rd[t, i][:], in0=a[:], in1=g[:], op=ALU.mult)
+            nc.gpsimd.tensor_tensor(out=rd[t, i][:], in0=rd[t, i][:], in1=rtmp[t, i][:], op=ALU.mult)
 
-        stat = {}
+        stat, sones, nov = {}, {}, {}
         for k in range(NK):
             stat[k] = keep.tile([P, 2, NG], F32, name="stat%d" % k)
+            sones[k] = keep.tile([P, P], F32, name="sones%d" % k)
+            nov[k] = keep.tile([P, 1], F32, name="nov%d" % k)
 
         def psi_square(k, t, i):
             junk = work.tile([P, 512], BF16, name="junk", tag="junk", bufs=2)
@@ -312,17 +304,35 @@ def tile_dmrgsinglesitempodavidsoncorrection_x1_kernel(
                 junk[:], psin[k, t][:, i, :], ACT.Square, accum_out=stat[k][:, 1, j : j + 1]
             )
 
+        norm = {}
+
+        def norm_a(k):
+            norm[k] = keep.tile([P, 2], F32, name="norm%d" % k)
+            nc.vector.tensor_reduce(out=norm[k][:, 0:1], in_=stat[k][:, 1, :], axis=AX.X, op=ALU.add)
+
+        def norm_b(k):
+            norm[k, "bank"] = bank("t")
+            nc.tensor.matmul(norm[k, "bank"][:, 0:1], ones[:], norm[k][:, 0:1], start=True, stop=True)
+
+        def norm_c(k):
+            nc.vector.reciprocal(out=norm[k][:, 1:2], in_=norm[k, "bank"][:, 0:1])
+            nc.vector.tensor_scalar(sones[k][:], ones[:], norm[k][:, 1:2], -1.0, ALU.mult, ALU.mult)
+
         blocks = []
         for k in range(NK):
             order = [(1, j) for j in range(NBLK)] + [(2, j) for j in range(NBLK)]
             order += [(0, j) for j in range(E_BLOCKS[k], NBLK)] + [(3, j) for j in range(NBLK)]
             blocks += [(k, i, j) for i, j in order]
+        nblocks = len(blocks)
+        last_of = {}
+        for n, (k, i, j) in enumerate(blocks):
+            last_of[k, i] = n
         ybank, ysb, zbank, zst, zc, zs = {}, {}, {}, {}, {}, {}
 
         def m1(n):
             k, i, j = blocks[n]
             ybank[n] = bank("y")
-            jj = j - 6 if i == 0 else j
+            jj = j - KMIN if i == 0 else j
             cw = lcw[i][:].rearrange("p j w -> p (j w)")
             sw = lsw[i][:].rearrange("p j w -> p (j w)")
             for s in range(NS):
@@ -390,7 +400,7 @@ def tile_dmrgsinglesitempodavidsoncorrection_x1_kernel(
             return ebank[k, q][:].rearrange("p (t a) -> p t a", t=4)[:, :, 0:na]
 
         def fma(k, q, g):
-            w = wf[:, NG * q + g : NG * q + g + 1]
+            w = wf[:, q, g : g + 1]
             if q == 0:
                 na = AB * E_BLOCKS[k]
                 acc[k, g] = work.tile([P, 4, na], F32, name="acc%d" % g, tag="acc%d" % g, bufs=1)
@@ -400,26 +410,30 @@ def tile_dmrgsinglesitempodavidsoncorrection_x1_kernel(
                     out=acc[k, g][:], in0=e_in(k, q), scalar=w, in1=acc[k, g][:], op0=ALU.mult, op1=ALU.add
                 )
 
-        def e_final(k, g):
+        def e_final(k, g, engine):
             na = AB * E_BLOCKS[k]
-            nc.gpsimd.tensor_tensor(
+            e = nc.gpsimd if engine == "g" else nc.vector
+            e.tensor_tensor(
                 out=zst_tile(k, 0)[:, g, 0:na, :],
                 in0=acc[k, g][:].rearrange("p t a -> p a t"),
                 in1=grt[:, g : g + 1, :].to_broadcast([P, na, 4]),
                 op=ALU.mult,
             )
 
-        hbank, qt = {}, {}
+        hbank, qt, ut, pq = {}, {}, {}, {}
 
-        def z_quant(k, i):
+        def z_tiles(k, i):
             zc[k, i] = work.tile([P, 1024], U32, name="zc", tag="zc", bufs=2, align_bytes=64)
             zs[k, i] = work.tile([P, 1024], U8, name="zs", tag="zs", bufs=2, align_bytes=64)
-            quant(zc[k, i][:], zs[k, i][:], zst[k, i][:].rearrange("p g a t -> p (g a t)"))
+
+        def z_quant(k, i, c0, c1):
+            flat = zst[k, i][:].rearrange("p g a t -> p (g a t)")
+            quant(zc[k, i][:, c0:c1], zs[k, i][:, c0:c1], flat[:, 4 * c0 : 4 * c1])
 
         def m3(k, i, t, tag):
             hbank[k, i, t] = bank(tag)
             for c in range(NC):
-                c0 = (NS * c + t) * P
+                c0 = (NC * t + c) * P
                 nc.tensor.matmul_mx(
                     out=hbank[k, i, t][:],
                     lhsT=zc[k, i][:, c0 : c0 + P].bitcast(FP8X4),
@@ -430,10 +444,8 @@ def tile_dmrgsinglesitempodavidsoncorrection_x1_kernel(
                     stop=(c == NC - 1),
                 )
 
-        ut = {}
-
         def ep_u(k, i, t):
-            ut[k, i, t] = work.tile([P, 512], F32, name="u", tag="u", bufs=2)
+            ut[k, i, t] = work.tile([P, 512], F32, name="u", tag="u", bufs=3)
             nc.vector.scalar_tensor_tensor(
                 out=ut[k, i, t][:],
                 in0=hbank[k, i, t][:],
@@ -447,8 +459,6 @@ def tile_dmrgsinglesitempodavidsoncorrection_x1_kernel(
             qt[k, i, t] = work.tile([P, 512], F32, name="q", tag="q", bufs=10)
             e = nc.gpsimd if eng == "g" else nc.vector
             e.tensor_tensor(out=qt[k, i, t][:], in0=ut[k, i, t][:], in1=rd[t, i][:], op=ALU.mult)
-
-        pq = {}
 
         def ep_p(k, i, t):
             pq[k, i, t] = work.tile([P, 512], F32, name="pq", tag="pq", bufs=2)
@@ -464,9 +474,9 @@ def tile_dmrgsinglesitempodavidsoncorrection_x1_kernel(
 
         def ep_sum_v(k, i, t):
             j = t * NT + i
-            p = work.tile([P, 512], F32, name="pq", tag="pq", bufs=2)
+            pv = work.tile([P, 512], F32, name="pq", tag="pq", bufs=2)
             nc.vector.scalar_tensor_tensor(
-                out=p[:],
+                out=pv[:],
                 in0=qt[k, i, t][:],
                 scalar=1.0,
                 in1=psin[k, t][:, i, :],
@@ -475,30 +485,25 @@ def tile_dmrgsinglesitempodavidsoncorrection_x1_kernel(
                 accum_out=stat[k][:, 0, j : j + 1],
             )
 
-        nov = {}
-        st2 = {}
-        sbank = {}
+        snum, sbank = {}, {}
 
         def overlap_v1(k):
-            st2[k] = keep.tile([P, 2], F32, name="st2%d" % k)
-            nc.vector.tensor_reduce(out=st2[k][:], in_=stat[k][:], axis=AX.X, op=ALU.add)
+            snum[k] = keep.tile([P, 1], F32, name="snum%d" % k)
+            nc.vector.tensor_reduce(out=snum[k][:], in_=stat[k][:, 0, :], axis=AX.X, op=ALU.add)
 
         def overlap_pe(k):
             sbank[k] = bank("t")
-            nc.tensor.matmul(sbank[k][:, 0:2], ones[:], st2[k][:], start=True, stop=True)
+            nc.tensor.matmul(sbank[k][:, 0:1], sones[k][:], snum[k][:], start=True, stop=True)
 
         def overlap_v2(k):
-            rden = keep.tile([P, 1], F32, name="rden%d" % k)
-            nov[k] = keep.tile([P, 1], F32, name="nov%d" % k)
-            nc.vector.reciprocal(out=rden[:], in_=sbank[k][:, 1:2])
-            nc.vector.tensor_scalar(nov[k][:], sbank[k][:, 0:1], rden[:, 0:1], -1.0, ALU.mult, ALU.mult)
+            nc.vector.tensor_copy(out=nov[k][:], in_=sbank[k][:, 0:1])
 
         cor, cb, ost, xt, oc, osc = {}, {}, {}, {}, {}, {}
         for k in range(NK):
             osc[k] = keep.tile([P, 1024], U8, name="osc%d" % k, align_bytes=64)
 
         def c_corr(k, t, i):
-            cor[k, t, i] = work.tile([P, 512], F32, name="cor", tag="cor", bufs=3)
+            cor[k, t, i] = work.tile([P, 512], F32, name="cor", tag="cor", bufs=4)
             nc.vector.scalar_tensor_tensor(
                 out=cor[k, t, i][:],
                 in0=psin[k, t][:, i, :],
@@ -511,7 +516,10 @@ def tile_dmrgsinglesitempodavidsoncorrection_x1_kernel(
 
         def c_cast(k, t, i):
             cb[k, t, i] = work.tile([P, 512], BF16, name="cb", tag="cb", bufs=3)
-            nc.scalar.copy(out=cb[k, t, i][:], in_=cor[k, t, i][:])
+            nc.scalar.copy(
+                out=cb[k, t, i][:].rearrange("a (u w e) -> a u w e", u=2, e=2),
+                in_=cor[k, t, i][:].rearrange("a (w u e) -> a u w e", u=2, e=2),
+            )
 
         def c_turn(k, t, i, tag):
             if i % 2 == 0:
@@ -520,7 +528,7 @@ def tile_dmrgsinglesitempodavidsoncorrection_x1_kernel(
             words = cb[k, t, i][:].bitcast(F32)
             for u in range(2):
                 c0 = (2 * (i % 2) + u) * P
-                nc.tensor.transpose(x[:, c0 : c0 + P], words[:, u:256:2], ident[:])
+                nc.tensor.transpose(x[:, c0 : c0 + P], words[:, P * u : P * (u + 1)], ident[:])
 
         def c_evac(k, t, h, eng):
             if h == 0:
@@ -532,12 +540,18 @@ def tile_dmrgsinglesitempodavidsoncorrection_x1_kernel(
             else:
                 nc.vector.tensor_copy(out=dst, in_=src)
 
-        def c_quant(k, t):
-            oc[k, t] = work.tile([P, 512], U32, name="oc", tag="oc", bufs=2, align_bytes=64)
-            quant(oc[k, t][:], osc[k][:, 512 * t : 512 * (t + 1)], ost[k, t][:])
-            m0 = k * 1024 + t * 512
-            words = out_1.rearrange("g p m t -> (g p) (m t)")[:, 4 * m0 : 4 * (m0 + 512)]
-            nc.sync.dma_start(out=words.bitcast(I32), in_=oc[k, t][:].bitcast(I32))
+        def c_quant(k, t, h0, h1):
+            if h0 == 0:
+                oc[k, t] = work.tile([P, 512], U32, name="oc", tag="oc", bufs=2, align_bytes=64)
+            quant(
+                oc[k, t][:, 256 * h0 : 256 * h1],
+                osc[k][:, 512 * t + 256 * h0 : 512 * t + 256 * h1],
+                ost[k, t][:, 1024 * h0 : 1024 * h1],
+            )
+            if h1 == 2:
+                m0 = k * 1024 + t * 512
+                words = out_1.rearrange("g p m t -> (g p) (m t)")[:, 4 * m0 : 4 * (m0 + 512)]
+                nc.sync.dma_start(out=words.bitcast(I32), in_=oc[k, t][:].bitcast(I32))
 
         def c_scales(k):
             rows = out_2.rearrange("g q m -> (g q) m")
@@ -547,155 +561,258 @@ def tile_dmrgsinglesitempodavidsoncorrection_x1_kernel(
                     in_=osc[k][32 * q : 32 * q + 4, :].bitcast(I32),
                 )
 
-        lenv_pe(1)
-        small_constants()
-        lenv_evac(1, "ssss")
-        v_on_vector(0, 0)
-        v_scale_on_scalar(0, 1)
-        lenv_quant(1, range(2))
+        v_part(0, 0, 0, 3, "v")
+        v_part(0, 0, 3, 4, "g")
+        zero_windows(1)
+        v_part(0, 1, 2, 4, "g")
         v_quant(0, 0)
-        lenv_pe(0)
-        v_interleave(0, 1)
+        v_part(0, 1, 0, 2, "v")
+        lenv_pe(1)
+        lenv_evac(1)
+        small_constants()
+        lenv_quant(1, range(1))
         v_quant(0, 1)
-        lenv_quant(1, range(2, NBLK))
+        lenv_quant(1, range(1, 3))
+        nc.gpsimd.memset(ones[:], 1.0)
+        for i in (0, 2, 3):
+            zero_windows(i)
+        lenv_pe(0)
         lenv0_evac()
-        quant(lc0[:], ls0[:], lst[0][:])
-        for j in range(2):
-            quant(lcw[0][:, j, 64:128], lsw[0][:, j, 64:128], lst0k[:, j, :])
-
         later_loads()
 
-        slots = {}
+        waiting = {"pe": [], "s": [], "g0": [], "g": [], "v": []}
+        state = {"round": 0, "h": True, "f": 0, "em": 0, "final": 0}
+        hq = []
 
-        def at(step, slot, fn, *args):
-            slots.setdefault((step, slot), []).append((fn, args))
+        def push(engine, delay, cost, fn, *args):
+            waiting[engine].append((state["round"] + delay, cost, fn, args))
 
-        nblocks = len(blocks)
-        first = {0: 0, 1: sum(1 for x in blocks if x[0] == 0)}
-        last_of = {}
-        for n, (k, i, j) in enumerate(blocks):
-            last_of[k, i] = n
+        def drain(engine, budget):
+            for item in list(waiting[engine]):
+                if budget <= 0:
+                    break
+                if item[0] <= state["round"]:
+                    waiting[engine].remove(item)
+                    item[2](*item[3])
+                    budget -= item[1]
+            return budget
 
-        at(6, "v", last_loads)
-        at(1, "pe", lenv_pe, 2)
-        at(1, "s", lenv_evac, 2, "ssss")
-        at(3, "v", lenv_quant, 2, range(NBLK))
-        for c in range(NC):
-            eng = "s" if c % 2 == 0 else "g"
-            for part in range(4):
-                at(3 + c + part // 2, eng, r_copy, c, part, eng)
-            at(5 + c, "v", r_quant, c)
-        at(8, "pe", lenv_pe, 3)
-        at(8, "s", lenv_evac, 3, "ssss")
-        at(12, "v", lenv_quant, 3, range(NBLK))
-        for s in range(NS):
-            for t in range(4):
-                at(13 + 4 * s + t, "g", v_on_gpsimd, 1, s, t)
-            at(18 + 4 * s, "v", v_quant, 1, s)
+        def stage_end(k, i):
+            z_tiles(k, i)
+            z_quant(k, i, 0, 1024)
+            push("pe", LAG_M3, 1, product_request, k, i)
 
-        def rd_queue(t, i, step):
-            def run():
-                for f in rd_s(t, i):
-                    f()
-            at(step, "s", run)
-            at(step, "g", rd_g, t, i)
+        def product_request(k, i):
+            hq.extend([(k, i, 0), (k, i, 1)])
 
-        for x, (t, i) in enumerate([(0, 1), (1, 1), (0, 2), (1, 2), (0, 0), (1, 0), (0, 3), (1, 3)]):
-            rd_queue(t, i, (8, 9, 11, 12, 15, 17, 19, 21)[x])
-        for t in range(NS):
-            for i in range(NT):
-                at(13 + t * NT + i, "s", psi_square, 0, t, i)
-                at(34 + t * NT + i, "s", psi_square, 1, t, i)
+        def product():
+            if hq and state["h"]:
+                k, i, t = hq.pop(0)
+                m3(k, i, t, "h")
+                state["h"] = False
+                push("v", LAG_U, 450, u_and_more, k, i, t)
 
-        for k in range(NK):
-            s0 = first[k] + 2 * k
-            nsteps = 20 if k == 0 else 16
-            at(s0, "pe", em, k, 0)
-            for g in range(NG):
-                at(s0 + g // 4, "s", fma, k, 0, g)
-            for f in range(NG * (NG - 1)):
-                q, g = divmod(f, NG)
-                q += 1
-                step = s0 + 1 + f * nsteps // (NG * (NG - 1))
-                if g == 0:
-                    at(step - 1 if q > 1 else s0, "pe", em, k, q)
-                at(step, "fma", fma, k, q, g)
-                if q == NG - 1:
-                    at(step + 1, "g", e_final, k, g)
+        def u_and_more(k, i, t):
+            ep_u(k, i, t)
+            state["h"] = True
+            push("g", LAG_Q, 960, ep_q, k, i, t, "g")
+            push("g", LAG_Q, 960, p_and_more, k, i, t)
 
-        def stage(k, i, step):
-            at(step, "v", z_quant, k, i)
-            for t in range(NS):
-                at(step + 2 + 2 * t, "pe", m3, k, i, t, "h")
-                at(step + 3 + 2 * t, "v", ep_u, k, i, t)
-                at(step + 4 + 2 * t, "g", ep_q, k, i, t, "g")
-                at(step + 4 + 2 * t, "g", ep_p, k, i, t)
-                at(step + 5 + 2 * t, "s", ep_sum, k, i, t)
+        def p_and_more(k, i, t):
+            ep_p(k, i, t)
+            push("s", LAG_SUM, 450, sum_and_more, k, i, t)
 
-        for k in range(NK):
-            for i in (1, 2, 3):
-                if (k, i) != (1, 3):
-                    stage(k, i, last_of[k, i] + 1)
-        stage(0, 0, last_of[0, 3] + 5)
-        stage(1, 0, first[1] + 2 + 1 + 16 + 2)
+        done = {0: 0, 1: 0}
 
-        ov0 = last_of[0, 3] + 13
-        at(ov0, "v", overlap_v1, 0)
-        at(ov0 + 1, "pe", overlap_pe, 0)
-        at(ov0 + 1, "v", overlap_v2, 0)
-        for x in range(NG):
+        def sum_and_more(k, i, t):
+            ep_sum(k, i, t)
+            done[k] += 1
+            if k == 0 and done[0] == NG:
+                push("v", 2, 100, overlap_a)
+
+        def overlap_a():
+            overlap_v1(0)
+            push("pe", 1, 50, overlap_b)
+
+        def overlap_b():
+            overlap_pe(0)
+            push("v", 0, 300, overlap_c)
+
+        def overlap_c():
+            overlap_v2(0)
+            for x in range(NG):
+                push("v", 1 + x, 450, corr_and_more, x)
+
+        def corr_and_more(x):
             t, i = divmod(x, NT)
-            at(ov0 + 3 + x, "v", c_corr, 0, t, i)
-            at(ov0 + 4 + x, "s", c_cast, 0, t, i)
-            if i % 2 == 1:
-                at(ov0 + 6 + x, "pe", c_turn, 0, t, i - 1, "t")
-                at(ov0 + 6 + x, "pe", c_turn, 0, t, i, "t")
-                at(ov0 + 6 + x, "s", c_evac, 0, t, i // 2, "s")
-            if i == 3:
-                at(ov0 + 8 + x, "v", c_quant, 0, t)
-        at(ov0 + 9 + NG, "v", c_scales, 0)
+            c_corr(0, t, i)
+            push("s", LAG_CAST, 450, cast_and_more, t, i)
 
-        def run(step, slot):
-            for fn, args in slots.pop((step, slot), []):
-                fn(*args)
+        def cast_and_more(t, i):
+            c_cast(0, t, i)
+            if i % 2 == 1:
+                push("pe", LAG_TURN, 420, turn_and_more, t, i // 2)
+
+        def turn_and_more(t, h):
+            c_turn(0, t, 2 * h, "t")
+            c_turn(0, t, 2 * h + 1, "t")
+            c_evac(0, t, h, "s")
+            if h == 1:
+                push("v", 2, 470, c_quant, 0, t, 0, 2)
+                if t == 1:
+                    push("v", 3, 50, c_scales, 0)
+
+        fmas = [(k, q, g) for k in range(NK) for q in range(NB * NS) for g in range(NG)]
+        ems = [(k, q) for k in range(NK) for q in range(NB * NS)]
+
+        def em_ahead():
+            at = state["f"] // NG
+            into = state["f"] % NG
+            allowed = at + (2 if into >= EM_AT or at % NG == 0 else 1)
+            if state["round"] > 0 and state["em"] < min(len(ems), allowed):
+                em(*ems[state["em"]])
+                state["em"] += 1
+
+        def fma_next():
+            k, q, g = fmas[state["f"]]
+            if NB * NS * k + q >= state["em"] or (q == 0 and state["final"] < NG * k and state["final"] <= g):
+                return False
+            fma(k, q, g)
+            state["f"] += 1
+            if q == NB * NS - 1:
+                if k == 1 and g % 2 == 1:
+                    push("v", 1, 340, e_last, k, g, "v")
+                else:
+                    push("g0", 1, 850, e_last, k, g, "g")
+            return True
+
+        def e_last(k, g, engine):
+            e_final(k, g, engine)
+            state["final"] += 1
+            if state["final"] == NG * (k + 1):
+                push("v", LAG_ZE, 900, stage_end, k, 0)
+
+        def rd_all(t, i):
+            push("s", 0, 450, rd_first, t, i)
+            push("s", 0, 450, rd_second, t, i)
+            push("s", 0, 450, rd_and_more, t, i)
+
+        def rd_and_more(t, i):
+            rd_third(t, i)
+            push("g", 2, 960, rd_g, t, i)
+
+        def prep(i):
+            lenv_pe(i)
+            lenv_evac(i)
+            push("v", 2, 450, lenv_quant, i, range(0, 4))
+            push("v", 3, 450, lenv_quant, i, range(4, NBLK))
+
+        def r_prep(c, eng):
+            for part in range(4):
+                push(eng, 0, 520, r_copy, c, part, eng)
+            push("v", 4, 470, r_quant, c)
+
+        def v_prep(s):
+            for t in range(4):
+                push("g", 0, 960, v_part, 1, s, t, t + 1, "g")
+            push("v", 6, 470, v_quant, 1, s)
+
+        def norm_all(k):
+            norm_a(k)
+            push("pe", 1, 50, norm_pe, k)
+
+        def norm_pe(k):
+            norm_b(k)
+            push("v", 0, 200, norm_c, k)
+
+        ready = {}
+
+        def at(step, fn, *args):
+            ready.setdefault(step, []).append((fn, args))
+
+        at(0, push, "v", 0, 480, quant, lc0[:], ls0[:], lst[0][:])
+        at(0, push, "v", 0, 350, lenv_quant, 1, range(3, 6))
+        at(1, push, "v", 0, 230, lenv_quant, 1, range(6, 8))
+        at(3, push, "v", 0, 230, lenv0_quant)
+        at(1, prep, 2)
+        at(2, r_prep, 0, "g")
+        at(3, r_prep, 1, "s")
+        at(5, r_prep, 2, "g")
+        at(6, r_prep, 3, "s")
+        at(6, last_loads)
+        at(8, prep, 3)
+        for x, (t, i) in enumerate([(0, 1), (1, 1), (0, 2), (1, 2), (0, 3), (1, 3), (0, 0), (1, 0)]):
+            at((10, 11, 14, 15, 18, 19, 20, 21)[x], rd_all, t, i)
+        at(12, v_prep, 0)
+        at(16, v_prep, 1)
+        for k in range(NK):
+            for t in range(NS):
+                for i in range(NT):
+                    at(22 + 8 * k + t * NT + i, push, "s", 0, 450, psi_square, k, t, i)
+        at(31, push, "v", 0, 100, norm_all, 0)
+        at(40, push, "v", 0, 100, norm_all, 1)
 
         m1(0)
         e1(0)
         for n in range(nblocks):
+            state["round"] = n
             if n + 1 < nblocks:
                 m1(n + 1)
-            run(n, "pe")
+            product()
+            em_ahead()
+            for fn, args in ready.pop(n, []):
+                fn(*args)
+            drain("pe", 500)
             m2(n)
             if n + 1 < nblocks:
                 e1(n + 1)
-            run(n, "s")
+            sb = S_BUDGET
+            while sb > 0 and state["f"] < len(fmas) and fmas[state["f"]][1] == 0 and fma_next():
+                sb -= 450
+            drain("s", sb)
+            left = V_BUDGET
             if n > 0:
                 e2(n - 1)
-            run(n, "fma")
-            run(n, "g")
-            run(n, "v")
+                left -= 450
+                k, i, j = blocks[n - 1]
+                if i > 0 and last_of[k, i] == n - 1 and (k, i) != (1, 3):
+                    push("v", 0, 900, stage_end, k, i)
+            left = drain("v", left)
+            while (
+                left > 0
+                and state["f"] < min(len(fmas), int(PACE * (n - 1)) + NG)
+                and fmas[state["f"]][1] > 0
+                and fma_next()
+            ):
+                left -= 380
+            drain("g", drain("g0", G_BUDGET))
+        assert state["f"] == len(fmas), state["f"]
         e2(nblocks - 1)
-        z_quant(1, 3)
-        for n in range(nblocks, nblocks + 20):
-            for slot in ("pe", "s", "fma", "g", "v"):
-                run(n, slot)
-        m3(1, 3, 0, "h")
+        z_tiles(1, 3)
+        z_quant(1, 3, 0, 512)
+        z_quant(1, 3, 512, 1024)
+        for n in range(nblocks, nblocks + 14):
+            state["round"] = n
+            product()
+            for engine in ("pe", "s", "g0", "g", "v"):
+                drain(engine, 5000)
+        m3(1, 3, 0, "y")
         m3(1, 3, 1, "y")
         for t in range(NS):
             ep_u(1, 3, t)
             ep_q(1, 3, t, "v")
-        for t in range(NS):
             ep_sum_v(1, 3, t)
         overlap_v1(1)
         overlap_pe(1)
         overlap_v2(1)
-        assert not slots, sorted(slots)
         for t in range(NS):
             for i in range(NT):
                 c_corr(1, t, i)
                 c_cast(1, t, i)
                 c_turn(1, t, i, "ez"[t])
-                if i % 2 == 1:
-                    c_evac(1, t, i // 2, "sv"[i // 2])
-            c_quant(1, t)
+            c_evac(1, t, 0, "s")
+            c_quant(1, t, 0, 1)
+            c_evac(1, t, 1, "v")
+            c_quant(1, t, 1, 2)
         c_scales(1)
+        assert not any(waiting.values()) and not hq and not ready

@@ -24,18 +24,34 @@ KMIN = NBLK - max(NBLK - x for x in E_BLOCKS)
 
 FLOPS = 2 * 2 * 2048 * 2048 * 512 + 2 * 64 * 2 * 512 * 512
 
-S_BUDGET = 1150
+S_BUDGET = 700
 V_BUDGET = 1700
 G_BUDGET = 1800
 LAG_M3 = 2
 LAG_U = 1
-LAG_Q = 1
-LAG_SUM = 3
+LAG_Q = 0
+LAG_SUM = 1
 LAG_ZE = 2
 LAG_CAST = 1
 LAG_TURN = 2
-EM_AT = 6
-PACE = 2.75
+EM_AT = 5
+SG_INPUTS = 1
+AHEAD = 1
+DMA_FROM = 99
+XBUFS = 3
+PACE = 3.1
+FINAL = ("g", "g")
+SQ = (14, 26)
+LAG_R = 3
+EM_FROM = 1
+LAST_AT = 6
+PREP_AT = (1, 7)
+V_AT = 12
+R_AT = (1, 2, 3, 4)
+TAIL_CAST = "ssssssss"
+CORR = ("v", 450)
+CAST = ("s", 450)
+R_ENG = ("g", "s", "g", "g")
 
 
 def tile_dmrgsinglesitempodavidsoncorrection_x1_kernel(
@@ -80,24 +96,26 @@ def tile_dmrgsinglesitempodavidsoncorrection_x1_kernel(
             dnat[t] = raw_tile("dnat%d" % t)
             nc.sync.dma_start(out=dnat[t][:], in_=d[t].rearrange("(i a) p -> a i p", a=P))
 
+        wb = keep.tile([P, 64], BF16, name="wb")
+        nc.vector.memset(wb[:], 0.0)
+        nc.scalar.dma_start(out=wb[0:1, :], in_=wmpo.rearrange("b s c t -> (b s c t)").unsqueeze(0))
         glb = keep.tile([P, 4], BF16, name="glb")
         nc.scalar.dma_start(out=glb[:], in_=gl.rearrange("(p j) -> p j", j=4))
         load_psik(0, 0)
         load_psik(0, 1)
         load_lenv(1)
-        wb = keep.tile([P, 64], BF16, name="wb")
-        nc.scalar.dma_start(
-            out=wb[:], in_=wmpo.rearrange("b s c t -> (b s c t)").partition_broadcast(P)
-        )
         grb = keep.tile([P, NC, 4], BF16, name="grb")
         nc.scalar.dma_start(out=grb[:], in_=gr.rearrange("c (p t) -> p c t", t=4))
         load_lenv(0)
         load_lenv(2)
-        for c in range(3):
-            load_renv(c)
+        load_renv(0)
 
         def later_loads():
+            load_renv(1)
+            load_renv(2)
             load_renv(3)
+
+        def more_loads():
             load_lenv(3)
             for t in range(NS):
                 load_d(t)
@@ -116,55 +134,64 @@ def tile_dmrgsinglesitempodavidsoncorrection_x1_kernel(
         tabl = keep.tile([P, 1], F32, name="tabl")
         nc.scalar.activation(tabl[:], onecol[:], ACT.Abs_reciprocal_sqrt)
         ones = keep.tile([P, P], F32, name="ones")
+        onesb = keep.tile([P, P], BF16, name="onesb")
+        nc.vector.memset(onesb[:], 1.0)
 
         lcw, lsw = {}, {}
-        for i in (1, 0, 2, 3):
-            n = 3 if i == 0 else 9
-            lcw[i] = keep.tile([P, n, P], U32, name="lcw%d" % i, align_bytes=64)
-            lsw[i] = keep.tile([P, n, P], U8, name="lsw%d" % i, align_bytes=64)
-
-        def zero_windows(i):
-            nc.gpsimd.memset(lcw[i][:, :, 0:64], 0)
-            n = lsw[i].shape[1]
-            v = lsw[i][:].rearrange("p j w -> p (j w)").bitcast(I32)
-            nc.gpsimd.memset(v.rearrange("p (j w) -> p j w", j=n)[:, :, 0:16], 0)
+        for i in range(NT):
+            n = 3 * 64 if i == 0 else 4 * 3 * 64
+            lcw[i] = keep.tile([P, n], U32, name="lcw%d" % i, align_bytes=64)
+            lsw[i] = keep.tile([P, n], U8, name="lsw%d" % i, align_bytes=64)
 
         wf = keep.tile([P, NG, NG], F32, name="wf")
         dmat = keep.tile([P, AB], F32, name="dmat")
-        sel = keep.tile([P, NG], F32, name="sel")
-        wprod = keep.tile([P, NG, NG], F32, name="wprod")
-        wcol = keep.tile([P, NG], F32, name="wcol")
-        wk = keep.tile([P, P], F32, name="wk")
+        sel = [keep.tile([P, NG], F32, name="sel%d" % h) for h in range(2)]
+        wprod = [keep.tile([P, NG, NG], F32, name="wprod%d" % h) for h in range(2)]
+        wcol = [keep.tile([P, NG], F32, name="wcol%d" % h) for h in range(2)]
+        wk = [keep.tile([P, P], F32, name="wk%d" % h) for h in range(2)]
         grt = keep.tile([P, NG, 4], F32, name="grt")
 
         def small_constants():
+            wbank = bank("e")
+            nc.tensor.matmul(wbank[:, 0:64], onesb[:], wb[:], start=True, stop=True)
             nc.vector.tensor_copy(
                 out=wf[:].rearrange("p q (t c) -> p q t c", t=NS),
-                in_=wb[:].rearrange("p (q c t) -> p q t c", q=NG, t=NS),
+                in_=wbank[:, 0:64].rearrange("p (q c t) -> p q t c", q=NG, t=NS),
             )
+
+        def small_constants_0():
             nc.vector.tensor_reduce(
                 out=dmat[:], in_=ident[:].rearrange("p (q a) -> p a q", a=AB), axis=AX.X, op=ALU.add
             )
             nc.vector.tensor_reduce(
-                out=sel[:], in_=ident[:].rearrange("p (q a) -> p q a", a=AB), axis=AX.X, op=ALU.add
+                out=sel[0][:], in_=ident[:].rearrange("p (q a) -> p q a", a=AB), axis=AX.X, op=ALU.add
             )
-            nc.vector.tensor_tensor(
-                out=wprod[:].rearrange("p g (s b) -> p g s b", s=NS),
-                in0=wf[:].rearrange("p (b s) g -> p g s b", s=NS),
-                in1=sel[:].rearrange("p (s b) -> p s b", s=NS).unsqueeze(1).to_broadcast([P, NG, NS, NB]),
-                op=ALU.mult,
-            )
+            for s in range(NS):
+                nc.vector.tensor_copy(
+                    out=sel[1][:, NB * s : NB * (s + 1)], in_=sel[0][:, NB * (1 - s) : NB * (2 - s)]
+                )
+
+        def small_constants_2():
             nc.vector.tensor_copy(
                 out=grt[:].rearrange("p (s c) t -> p s (c t)", s=NS),
                 in_=grb[:].rearrange("p c t -> p (c t)").unsqueeze(1).to_broadcast([P, NS, 4 * NC]),
             )
-            nc.vector.tensor_reduce(out=wcol[:], in_=wprod[:], axis=AX.X, op=ALU.add)
-            nc.vector.tensor_tensor(
-                out=wk[:].rearrange("p (g a) -> p g a", a=AB),
-                in0=wcol[:].unsqueeze(2).to_broadcast([P, NG, AB]),
-                in1=dmat[:].unsqueeze(1).to_broadcast([P, NG, AB]),
-                op=ALU.mult,
-            )
+            for h in range(2):
+                nc.vector.tensor_tensor(
+                    out=wprod[h][:].rearrange("p g (s b) -> p g s b", s=NS),
+                    in0=wf[:].rearrange("p (b s) g -> p g s b", s=NS),
+                    in1=sel[h][:].rearrange("p (s b) -> p s b", s=NS).unsqueeze(1).to_broadcast([P, NG, NS, NB]),
+                    op=ALU.mult,
+                )
+            for h in range(2):
+                nc.vector.tensor_reduce(out=wcol[h][:], in_=wprod[h][:], axis=AX.X, op=ALU.add)
+            for h in range(2):
+                nc.vector.tensor_tensor(
+                    out=wk[h][:].rearrange("p (g a) -> p g a", a=AB),
+                    in0=wcol[h][:].unsqueeze(2).to_broadcast([P, NG, AB]),
+                    in1=dmat[:].unsqueeze(1).to_broadcast([P, NG, AB]),
+                    op=ALU.mult,
+                )
 
         def stage_tile(name):
             return work.tile([P, 2048], BF16, name=name, tag="st", bufs=4, align_bytes=64)
@@ -192,38 +219,35 @@ def tile_dmrgsinglesitempodavidsoncorrection_x1_kernel(
             return xlen[i, b // 2][:, (b % 2) * 256 : (b % 2) * 256 + 256]
 
         def lenv_evac(i):
-            lst[i] = stage_tile("lst%d" % i)
-            dst = lst[i][:].bitcast(F32).rearrange("p (k b a u) -> p k b a u", k=NBLK, b=NB, a=AB)
+            lst[i] = work.tile([P, 4096], BF16, name="lst%d" % i, tag="zst", bufs=2, align_bytes=64)
+            dst = lst[i][:, 0:3072].bitcast(F32).rearrange("p (k z b a u) -> p k z b a u", z=3, b=NB, a=AB, u=2)
             for b in range(NB):
-                nc.scalar.copy(
-                    out=dst[:, :, b], in_=lenv_view(i, b).rearrange("p (u k a) -> p k a u", u=2, k=NBLK)
-                )
+                src = lenv_view(i, b).rearrange("p (u k h a) -> p k h a u", u=2, h=2, a=AB)
+                nc.scalar.copy(out=dst[:, :, 0:2, b], in_=src)
+                nc.scalar.copy(out=dst[:, :, 2, b], in_=src[:, :, 0])
 
-        def lenv_quant(i, blks):
-            for j in blks:
-                quant(lcw[i][:, j, 64:128], lsw[i][:, j, 64:128], lst[i][:, 256 * j : 256 * (j + 1)])
+        def lenv_quant(i, c0, c1):
+            quant(lcw[i][:, c0:c1], lsw[i][:, c0:c1], lst[i][:, 4 * c0 : 4 * c1])
 
         lc0 = keep.tile([P, 512], U32, name="lc0", align_bytes=64)
         ls0 = keep.tile([P, 512], U8, name="ls0", align_bytes=64)
-        lst0k = keep.tile([P, NBLK - KMIN, 256], BF16, name="lst0k", align_bytes=64)
+        lst0k = keep.tile([P, 768], BF16, name="lst0k", align_bytes=64)
 
         def lenv0_evac():
             lst[0] = stage_tile("lst0")
             dst = lst[0][:].bitcast(F32).rearrange("p (b a u) -> p b a u", b=NB, a=P)
-            dstk = lst0k[:].rearrange("p k w -> p (k w)").bitcast(F32).rearrange(
-                "p (k b a u) -> p k b a u", b=NB, a=AB, u=2
-            )
             for b in range(NB):
                 nc.scalar.copy(out=dst[:, b], in_=lenv_view(0, b).rearrange("p (u a) -> p a u", u=2))
-            for b in range(NB):
-                nc.scalar.copy(
-                    out=dstk[:, :, b],
-                    in_=lenv_view(0, b).rearrange("p (u k a) -> p k a u", u=2, k=NBLK)[:, KMIN:NBLK],
-                )
+
+        def lenv0_pair():
+            dst = lst0k[:].rearrange("p (z b x) -> p z b x", z=3, b=NB)
+            src = lst[0][:].rearrange("p (b k x) -> p k b x", b=NB, k=NBLK)
+            nc.gpsimd.tensor_copy(out=dst[:, 0:2], in_=src[:, NBLK - 2 :])
+            nc.gpsimd.tensor_copy(out=dst[:, 2], in_=src[:, NBLK - 2])
 
         def lenv0_quant():
-            for j in range(NBLK - KMIN):
-                quant(lcw[0][:, j, 64:128], lsw[0][:, j, 64:128], lst0k[:, j, :])
+            for c0, c1 in ((0, 128), (128, 192)):
+                quant(lcw[0][:, c0:c1], lsw[0][:, c0:c1], lst0k[:, 4 * c0 : 4 * c1])
 
         vc, vs, vst = {}, {}, {}
         for k in range(NK):
@@ -320,8 +344,8 @@ def tile_dmrgsinglesitempodavidsoncorrection_x1_kernel(
 
         blocks = []
         for k in range(NK):
-            order = [(1, j) for j in range(NBLK)] + [(2, j) for j in range(NBLK)]
-            order += [(0, j) for j in range(E_BLOCKS[k], NBLK)] + [(3, j) for j in range(NBLK)]
+            order = [(i, j ^ 1) for i in (1, 2, 0, 3) for j in range(NBLK)]
+            order = [(i, j) for i, j in order if i > 0 or j >= E_BLOCKS[k]]
             blocks += [(k, i, j) for i, j in order]
         nblocks = len(blocks)
         last_of = {}
@@ -329,27 +353,53 @@ def tile_dmrgsinglesitempodavidsoncorrection_x1_kernel(
             last_of[k, i] = n
         ybank, ysb, zbank, zst, zc, zs = {}, {}, {}, {}, {}, {}
 
-        def m1(n):
-            k, i, j = blocks[n]
-            ybank[n] = bank("y")
-            jj = j - KMIN if i == 0 else j
-            cw = lcw[i][:].rearrange("p j w -> p (j w)")
-            sw = lsw[i][:].rearrange("p j w -> p (j w)")
+        pairs, members = [], []
+        for n, (k, i, j) in enumerate(blocks):
+            if not pairs or pairs[-1] != (k, i, j // 2):
+                pairs.append((k, i, j // 2))
+                members.append([])
+            members[-1].append(n)
+
+        def m1(x):
+            k, i, pp = pairs[x]
             for s in range(NS):
-                c0 = P * jj + 64 - 64 * s
+                ybank[x, s] = bank("y")
+                c0 = 64 * s + (0 if i == 0 else 192 * pp)
                 nc.tensor.matmul_mx(
-                    out=ybank[n][:],
-                    lhsT=cw[:, c0 : c0 + P].bitcast(FP8X4),
-                    lhsT_scale=sw[:, c0 : c0 + P],
+                    out=ybank[x, s][:],
+                    lhsT=lcw[i][:, c0 : c0 + P].bitcast(FP8X4),
+                    lhsT_scale=lsw[i][:, c0 : c0 + P],
                     rhs=vc[k, s][:].bitcast(FP8X4),
                     rhs_scale=vs[k, s][:],
-                    start=(s == 0),
-                    stop=(s == 1),
+                    start=True,
+                    stop=True,
                 )
 
-        def e1(n):
-            ysb[n] = work.tile([P, 512], F32, name="ysb", tag="ysb", bufs=3)
-            nc.scalar.copy(out=ysb[n][:], in_=ybank[n][:])
+        xs = {}
+
+        def by_dma(x):
+            return x >= DMA_FROM
+
+        def e1(x, part):
+            if by_dma(x):
+                if part == 0:
+                    for s in range(NS):
+                        xs[x, s] = work.tile([P, 512], F32, name="xs", tag="xs%d" % s, bufs=(XBUFS, 2)[s])
+                        nc.scalar.copy(out=xs[x, s][:], in_=ybank[x, s][:])
+                    xs[x, 2] = work.tile([P, 512], F32, name="xw", tag="xw", bufs=XBUFS)
+                    nc.scalar.dma_start(out=xs[x, 2][64:128, :], in_=xs[x, 0][64:128, :])
+                    nc.scalar.dma_start(out=xs[x, 2][0:64, :], in_=xs[x, 1][0:64, :])
+                elif len(members[x]) == 2:
+                    nc.scalar.dma_start(out=xs[x, 0][64:128, :], in_=xs[x, 1][64:128, :])
+                for n in members[x]:
+                    ysb[n] = xs[x, 2 if blocks[n][2] % 2 else 0]
+            elif part < len(members[x]):
+                n = members[x][part]
+                h = blocks[n][2] % 2
+                tag = "xw" if h else "xs0"
+                ysb[n] = work.tile([P, 512], F32, name="ysb", tag=tag, bufs=XBUFS)
+                nc.scalar.copy(out=ysb[n][0:64, :], in_=ybank[x, h][0:64, :])
+                nc.scalar.copy(out=ysb[n][64:128, :], in_=ybank[x, 1 - h][64:128, :])
 
         def m2(n):
             zbank[n] = bank("z")
@@ -357,7 +407,7 @@ def tile_dmrgsinglesitempodavidsoncorrection_x1_kernel(
                 nc.tensor.matmul(
                     zbank[n][:, P * t : P * (t + 1)],
                     ysb[n][:, P * t : P * (t + 1)],
-                    wk[:],
+                    wk[blocks[n][2] % 2][:],
                     start=True,
                     stop=True,
                 )
@@ -401,8 +451,12 @@ def tile_dmrgsinglesitempodavidsoncorrection_x1_kernel(
 
         def fma(k, q, g):
             w = wf[:, q, g : g + 1]
+            na = AB * E_BLOCKS[k]
+            if 0 < q < SG_INPUTS:
+                part = work.tile([P, 4, na], F32, name="part", tag="part", bufs=2)
+                nc.scalar.activation(part[:], e_in(k, q), ACT.Copy, scale=w)
+                return part
             if q == 0:
-                na = AB * E_BLOCKS[k]
                 acc[k, g] = work.tile([P, 4, na], F32, name="acc%d" % g, tag="acc%d" % g, bufs=1)
                 nc.scalar.activation(acc[k, g][:], e_in(k, 0), ACT.Copy, scale=w)
             else:
@@ -410,8 +464,17 @@ def tile_dmrgsinglesitempodavidsoncorrection_x1_kernel(
                     out=acc[k, g][:], in0=e_in(k, q), scalar=w, in1=acc[k, g][:], op0=ALU.mult, op1=ALU.add
                 )
 
+        def fma_add(k, g, part):
+            nc.gpsimd.tensor_tensor(out=acc[k, g][:], in0=acc[k, g][:], in1=part[:], op=ALU.add)
+
         def e_final(k, g, engine):
             na = AB * E_BLOCKS[k]
+            if engine == "s":
+                for t in range(4):
+                    nc.scalar.activation(
+                        zst_tile(k, 0)[:, g, 0:na, t], acc[k, g][:, t, :], ACT.Copy, scale=grt[:, g, t : t + 1]
+                    )
+                return
             e = nc.gpsimd if engine == "g" else nc.vector
             e.tensor_tensor(
                 out=zst_tile(k, 0)[:, g, 0:na, :],
@@ -445,7 +508,7 @@ def tile_dmrgsinglesitempodavidsoncorrection_x1_kernel(
                 )
 
         def ep_u(k, i, t):
-            ut[k, i, t] = work.tile([P, 512], F32, name="u", tag="u", bufs=3)
+            ut[k, i, t] = work.tile([P, 512], F32, name="u", tag="u", bufs=4)
             nc.vector.scalar_tensor_tensor(
                 out=ut[k, i, t][:],
                 in0=hbank[k, i, t][:],
@@ -456,7 +519,7 @@ def tile_dmrgsinglesitempodavidsoncorrection_x1_kernel(
             )
 
         def ep_q(k, i, t, eng):
-            qt[k, i, t] = work.tile([P, 512], F32, name="q", tag="q", bufs=10)
+            qt[k, i, t] = work.tile([P, 512], F32, name="q", tag="q", bufs=8) if k == 0 else rd[t, i]
             e = nc.gpsimd if eng == "g" else nc.vector
             e.tensor_tensor(out=qt[k, i, t][:], in0=ut[k, i, t][:], in1=rd[t, i][:], op=ALU.mult)
 
@@ -474,9 +537,8 @@ def tile_dmrgsinglesitempodavidsoncorrection_x1_kernel(
 
         def ep_sum_v(k, i, t):
             j = t * NT + i
-            pv = work.tile([P, 512], F32, name="pq", tag="pq", bufs=2)
             nc.vector.scalar_tensor_tensor(
-                out=pv[:],
+                out=ut[k, i, t][:],
                 in0=qt[k, i, t][:],
                 scalar=1.0,
                 in1=psin[k, t][:, i, :],
@@ -502,24 +564,33 @@ def tile_dmrgsinglesitempodavidsoncorrection_x1_kernel(
         for k in range(NK):
             osc[k] = keep.tile([P, 1024], U8, name="osc%d" % k, align_bytes=64)
 
-        def c_corr(k, t, i):
+        def c_corr(k, t, i, engine):
             cor[k, t, i] = work.tile([P, 512], F32, name="cor", tag="cor", bufs=4)
-            nc.vector.scalar_tensor_tensor(
-                out=cor[k, t, i][:],
-                in0=psin[k, t][:, i, :],
-                scalar=nov[k][:, 0:1],
-                in1=qt[k, i, t][:],
-                op0=ALU.mult,
-                op1=ALU.add,
-            )
+            c = cor[k, t, i]
+            if engine == "g":
+                nc.gpsimd.tensor_scalar(c[:], psin[k, t][:, i, :], nov[k][:, 0:1], 0.0, ALU.mult, ALU.add)
+                nc.gpsimd.tensor_tensor(out=c[:], in0=c[:], in1=qt[k, i, t][:], op=ALU.add)
+            else:
+                nc.vector.scalar_tensor_tensor(
+                    out=c[:],
+                    in0=psin[k, t][:, i, :],
+                    scalar=nov[k][:, 0:1],
+                    in1=qt[k, i, t][:],
+                    op0=ALU.mult,
+                    op1=ALU.add,
+                )
             nc.sync.dma_start(out=out_0[k, t, P * i : P * (i + 1), :], in_=cor[k, t, i][:])
 
-        def c_cast(k, t, i):
-            cb[k, t, i] = work.tile([P, 512], BF16, name="cb", tag="cb", bufs=3)
-            nc.scalar.copy(
-                out=cb[k, t, i][:].rearrange("a (u w e) -> a u w e", u=2, e=2),
-                in_=cor[k, t, i][:].rearrange("a (w u e) -> a u w e", u=2, e=2),
-            )
+        def c_cast(k, t, i, engine):
+            cb[k, t, i] = work.tile([P, 512], BF16, name="cb", tag="cb", bufs=4)
+            dst = cb[k, t, i][:].rearrange("a (u w e) -> a u w e", u=2, e=2)
+            src = cor[k, t, i][:].rearrange("a (w u e) -> a u w e", u=2, e=2)
+            if engine == "s":
+                nc.scalar.copy(out=dst, in_=src)
+            elif engine == "g":
+                nc.gpsimd.tensor_copy(out=dst, in_=src)
+            else:
+                nc.vector.tensor_copy(out=dst, in_=src)
 
         def c_turn(k, t, i, tag):
             if i % 2 == 0:
@@ -561,27 +632,28 @@ def tile_dmrgsinglesitempodavidsoncorrection_x1_kernel(
                     in_=osc[k][32 * q : 32 * q + 4, :].bitcast(I32),
                 )
 
-        v_part(0, 0, 0, 3, "v")
-        v_part(0, 0, 3, 4, "g")
-        zero_windows(1)
-        v_part(0, 1, 2, 4, "g")
+        small_constants_0()
+        v_part(0, 0, 0, 4, "v")
+        small_constants()
         v_quant(0, 0)
-        v_part(0, 1, 0, 2, "v")
+        v_part(0, 1, 0, 4, "v")
         lenv_pe(1)
         lenv_evac(1)
-        small_constants()
-        lenv_quant(1, range(1))
+        small_constants_2()
+        lenv_quant(1, 0, 128)
+        lenv_quant(1, 128, 192)
         v_quant(0, 1)
-        lenv_quant(1, range(1, 3))
+        lenv_quant(1, 192, 704)
+        lenv_quant(1, 704, 768)
         nc.gpsimd.memset(ones[:], 1.0)
-        for i in (0, 2, 3):
-            zero_windows(i)
         lenv_pe(0)
         lenv0_evac()
+        quant(lc0[:], ls0[:], lst[0][:])
+        lenv0_pair()
         later_loads()
 
-        waiting = {"pe": [], "s": [], "g0": [], "g": [], "v": []}
-        state = {"round": 0, "h": True, "f": 0, "em": 0, "final": 0}
+        waiting = {"pe": [], "s0": [], "s": [], "g0": [], "g": [], "v0": [], "v": []}
+        state = {"round": 0, "h": True, "f": 0, "em": 0, "final": 0, "turned": 0, "t": True, "r": 0, "v": 0, "tail": False}
         hq = []
 
         def push(engine, delay, cost, fn, *args):
@@ -591,9 +663,8 @@ def tile_dmrgsinglesitempodavidsoncorrection_x1_kernel(
             for item in list(waiting[engine]):
                 if budget <= 0:
                     break
-                if item[0] <= state["round"]:
+                if item[0] <= state["round"] and item[2](*item[3]) != "wait":
                     waiting[engine].remove(item)
-                    item[2](*item[3])
                     budget -= item[1]
             return budget
 
@@ -606,19 +677,35 @@ def tile_dmrgsinglesitempodavidsoncorrection_x1_kernel(
             hq.extend([(k, i, 0), (k, i, 1)])
 
         def product():
-            if hq and state["h"]:
+            if hq and state["h"] and state["r"] == NC:
                 k, i, t = hq.pop(0)
                 m3(k, i, t, "h")
                 state["h"] = False
                 push("v", LAG_U, 450, u_and_more, k, i, t)
 
+        free = {"u": 3, "pq": 2, "cb": 4, "part": 2}
+
         def u_and_more(k, i, t):
+            if free["u"] == 0:
+                return "wait"
             ep_u(k, i, t)
             state["h"] = True
-            push("g", LAG_Q, 960, ep_q, k, i, t, "g")
-            push("g", LAG_Q, 960, p_and_more, k, i, t)
+            if state["tail"]:
+                ep_q(k, i, t, "v")
+                ep_sum_v(k, i, t)
+                return
+            free["u"] -= 1
+            push("g", LAG_Q, 960, q_and_more, k, i, t)
+
+        def q_and_more(k, i, t):
+            ep_q(k, i, t, "g")
+            free["u"] += 1
+            push("g", 0, 960, p_and_more, k, i, t)
 
         def p_and_more(k, i, t):
+            if free["pq"] == 0:
+                return "wait"
+            free["pq"] -= 1
             ep_p(k, i, t)
             push("s", LAG_SUM, 450, sum_and_more, k, i, t)
 
@@ -626,6 +713,7 @@ def tile_dmrgsinglesitempodavidsoncorrection_x1_kernel(
 
         def sum_and_more(k, i, t):
             ep_sum(k, i, t)
+            free["pq"] += 1
             done[k] += 1
             if k == 0 and done[0] == NG:
                 push("v", 2, 100, overlap_a)
@@ -635,27 +723,36 @@ def tile_dmrgsinglesitempodavidsoncorrection_x1_kernel(
             push("pe", 1, 50, overlap_b)
 
         def overlap_b():
+            if not state["t"]:
+                return "wait"
+            state["t"] = False
             overlap_pe(0)
             push("v", 0, 300, overlap_c)
 
         def overlap_c():
             overlap_v2(0)
+            state["t"] = True
             for x in range(NG):
-                push("v", 1 + x, 450, corr_and_more, x)
+                push(CORR[0], 1 + x, CORR[1], corr_and_more, x)
 
         def corr_and_more(x):
             t, i = divmod(x, NT)
-            c_corr(0, t, i)
-            push("s", LAG_CAST, 450, cast_and_more, t, i)
+            c_corr(0, t, i, CORR[0])
+            push(CAST[0], LAG_CAST, CAST[1], cast_and_more, t, i)
 
         def cast_and_more(t, i):
-            c_cast(0, t, i)
+            if NT // 2 * t + i // 2 > state["turned"] + 1:
+                return "wait"
+            c_cast(0, t, i, CAST[0])
             if i % 2 == 1:
                 push("pe", LAG_TURN, 420, turn_and_more, t, i // 2)
 
         def turn_and_more(t, h):
+            if not state["t"]:
+                return "wait"
             c_turn(0, t, 2 * h, "t")
             c_turn(0, t, 2 * h + 1, "t")
+            state["turned"] += 1
             c_evac(0, t, h, "s")
             if h == 1:
                 push("v", 2, 470, c_quant, 0, t, 0, 2)
@@ -669,25 +766,41 @@ def tile_dmrgsinglesitempodavidsoncorrection_x1_kernel(
             at = state["f"] // NG
             into = state["f"] % NG
             allowed = at + (2 if into >= EM_AT or at % NG == 0 else 1)
-            if state["round"] > 0 and state["em"] < min(len(ems), allowed):
+            if (
+                state["round"] >= EM_FROM
+                and state["em"] < min(len(ems), allowed)
+                and (ems[state["em"]][0] == 0 or state["v"] == NS)
+            ):
                 em(*ems[state["em"]])
                 state["em"] += 1
 
         def fma_next():
             k, q, g = fmas[state["f"]]
-            if NB * NS * k + q >= state["em"] or (q == 0 and state["final"] < NG * k and state["final"] <= g):
+            if NB * NS * k + q >= state["em"] or (
+                q == 0 and k == 1 and (0, g) not in finals
+            ):
                 return False
-            fma(k, q, g)
+            if 0 < q < SG_INPUTS:
+                if free["part"] == 0:
+                    return False
+                free["part"] -= 1
+            part = fma(k, q, g)
+            if part is not None:
+                push("g0", 0, 860, part_end, k, g, part)
             state["f"] += 1
             if q == NB * NS - 1:
-                if k == 1 and g % 2 == 1:
-                    push("v", 1, 340, e_last, k, g, "v")
-                else:
-                    push("g0", 1, 850, e_last, k, g, "g")
+                push(FINAL[g % 2][0] + "0", 1, 850, e_last, k, g, FINAL[g % 2])
             return True
+
+        finals = set()
+
+        def part_end(k, g, part):
+            fma_add(k, g, part)
+            free["part"] += 1
 
         def e_last(k, g, engine):
             e_final(k, g, engine)
+            finals.add((k, g))
             state["final"] += 1
             if state["final"] == NG * (k + 1):
                 push("v", LAG_ZE, 900, stage_end, k, 0)
@@ -702,74 +815,111 @@ def tile_dmrgsinglesitempodavidsoncorrection_x1_kernel(
             push("g", 2, 960, rd_g, t, i)
 
         def prep(i):
+            if not (state["h"] and state["t"]):
+                return "wait"
             lenv_pe(i)
             lenv_evac(i)
-            push("v", 2, 450, lenv_quant, i, range(0, 4))
-            push("v", 3, 450, lenv_quant, i, range(4, NBLK))
+            push("v", 2, 480, lenv_quant, i, 0, 512)
+            push("v", 2, 250, lenv_quant, i, 512, 768)
 
         def r_prep(c, eng):
             for part in range(4):
-                push(eng, 0, 520, r_copy, c, part, eng)
-            push("v", 4, 470, r_quant, c)
+                push(eng, 0, 520, r_part, c, part, eng)
+
+        def r_part(c, part, eng):
+            r_copy(c, part, eng)
+            if part == 3:
+                push("v", LAG_R, 470, r_end, c)
+
+        def r_end(c):
+            r_quant(c)
+            state["r"] += 1
 
         def v_prep(s):
             for t in range(4):
-                push("g", 0, 960, v_part, 1, s, t, t + 1, "g")
-            push("v", 6, 470, v_quant, 1, s)
+                push("g", 0, 960, v_next, s, t)
+
+        def v_next(s, t):
+            v_part(1, s, t, t + 1, "g")
+            if t == 3:
+                push("v", 2, 470, v_end, s)
+
+        def v_end(s):
+            v_quant(1, s)
+            state["v"] += 1
+
+        def square_and_more(k, t, i):
+            psi_square(k, t, i)
+            if (t, i) == (NS - 1, NT - 1):
+                push("v", 3, 100, norm_all, k)
 
         def norm_all(k):
             norm_a(k)
             push("pe", 1, 50, norm_pe, k)
 
         def norm_pe(k):
+            if not state["t"]:
+                return "wait"
+            state["t"] = False
             norm_b(k)
-            push("v", 0, 200, norm_c, k)
+            push("v", 0, 200, norm_end, k)
+
+        def norm_end(k):
+            norm_c(k)
+            state["t"] = True
 
         ready = {}
 
         def at(step, fn, *args):
             ready.setdefault(step, []).append((fn, args))
 
-        at(0, push, "v", 0, 480, quant, lc0[:], ls0[:], lst[0][:])
-        at(0, push, "v", 0, 350, lenv_quant, 1, range(3, 6))
-        at(1, push, "v", 0, 230, lenv_quant, 1, range(6, 8))
         at(3, push, "v", 0, 230, lenv0_quant)
-        at(1, prep, 2)
-        at(2, r_prep, 0, "g")
-        at(3, r_prep, 1, "s")
-        at(5, r_prep, 2, "g")
-        at(6, r_prep, 3, "s")
-        at(6, last_loads)
-        at(8, prep, 3)
+        at(PREP_AT[0], push, "pe", 0, 840, prep, 2)
+        for c in range(NC):
+            at(R_AT[c], r_prep, c, R_ENG[c])
+        at(3, more_loads)
+        at(LAST_AT, last_loads)
+        at(PREP_AT[1], push, "pe", 0, 840, prep, 3)
         for x, (t, i) in enumerate([(0, 1), (1, 1), (0, 2), (1, 2), (0, 3), (1, 3), (0, 0), (1, 0)]):
             at((10, 11, 14, 15, 18, 19, 20, 21)[x], rd_all, t, i)
-        at(12, v_prep, 0)
-        at(16, v_prep, 1)
+        at(V_AT, v_prep, 0)
+        at(V_AT, v_prep, 1)
         for k in range(NK):
             for t in range(NS):
                 for i in range(NT):
-                    at(22 + 8 * k + t * NT + i, push, "s", 0, 450, psi_square, k, t, i)
-        at(31, push, "v", 0, 100, norm_all, 0)
-        at(40, push, "v", 0, 100, norm_all, 1)
+                    at(SQ[k] + t * NT + i, push, "s", 0, 450, square_and_more, k, t, i)
 
+        pair_of = {n: x for x, m in enumerate(members) for n in m}
         m1(0)
-        e1(0)
+        e1(0, 0)
+        e1(0, 1)
+        issued, half = 1, []
         for n in range(nblocks):
             state["round"] = n
-            if n + 1 < nblocks:
-                m1(n + 1)
+            x = pair_of[n]
+            if x >= issued:
+                m1(x)
+                e1(x, 0)
+                e1(x, 1)
+                issued += 1
             product()
             em_ahead()
             for fn, args in ready.pop(n, []):
                 fn(*args)
             drain("pe", 500)
             m2(n)
-            if n + 1 < nblocks:
-                e1(n + 1)
+            for y in half:
+                e1(y, 1)
+            half = []
+            if issued < len(pairs) and issued <= x + AHEAD:
+                m1(issued)
+                e1(issued, 0)
+                half = [issued]
+                issued += 1
             sb = S_BUDGET
-            while sb > 0 and state["f"] < len(fmas) and fmas[state["f"]][1] == 0 and fma_next():
+            while sb > 0 and state["f"] < len(fmas) and fmas[state["f"]][1] < SG_INPUTS and fma_next():
                 sb -= 450
-            drain("s", sb)
+            drain("s", drain("s0", sb))
             left = V_BUDGET
             if n > 0:
                 e2(n - 1)
@@ -777,42 +927,57 @@ def tile_dmrgsinglesitempodavidsoncorrection_x1_kernel(
                 k, i, j = blocks[n - 1]
                 if i > 0 and last_of[k, i] == n - 1 and (k, i) != (1, 3):
                     push("v", 0, 900, stage_end, k, i)
-            left = drain("v", left)
+            left = drain("v", drain("v0", left))
             while (
                 left > 0
                 and state["f"] < min(len(fmas), int(PACE * (n - 1)) + NG)
-                and fmas[state["f"]][1] > 0
+                and fmas[state["f"]][1] >= SG_INPUTS
                 and fma_next()
             ):
                 left -= 380
             drain("g", drain("g0", G_BUDGET))
         assert state["f"] == len(fmas), state["f"]
+        state["round"], state["tail"] = nblocks + 20, True
         e2(nblocks - 1)
         z_tiles(1, 3)
         z_quant(1, 3, 0, 512)
         z_quant(1, 3, 512, 1024)
-        for n in range(nblocks, nblocks + 14):
-            state["round"] = n
-            product()
-            for engine in ("pe", "s", "g0", "g", "v"):
-                drain(engine, 5000)
-        m3(1, 3, 0, "y")
-        m3(1, 3, 1, "y")
-        for t in range(NS):
-            ep_u(1, 3, t)
-            ep_q(1, 3, t, "v")
-            ep_sum_v(1, 3, t)
+        drain("pe", 2)
+        rest = hq + [(1, 3, 0), (1, 3, 1)]
+        assert len(rest) < 5
+        for x, (k, i, t) in enumerate(rest):
+            m3(k, i, t, "yyzz"[x + 4 - len(rest)])
+        drain("v0", 9999)
+        for item in list(waiting["v"]):
+            if item[2] == u_and_more:
+                waiting["v"].remove(item)
+                item[2](*item[3])
+        for k, i, t in rest:
+            ep_u(k, i, t)
+            ep_q(k, i, t, "v")
+            ep_sum_v(k, i, t)
+        for n in range(8):
+            state["round"] += 10
+            for engine in ("pe", "s0", "g0", "g", "s"):
+                drain(engine, 9999)
         overlap_v1(1)
         overlap_pe(1)
         overlap_v2(1)
-        for t in range(NS):
-            for i in range(NT):
-                c_corr(1, t, i)
-                c_cast(1, t, i)
-                c_turn(1, t, i, "ez"[t])
-            c_evac(1, t, 0, "s")
-            c_quant(1, t, 0, 1)
-            c_evac(1, t, 1, "v")
-            c_quant(1, t, 1, 2)
+        order = [(t, i) for t in range(NS) for i in range(NT)]
+        for x, (t, i) in enumerate(order):
+            c_corr(1, t, i, "v")
+            c_cast(1, t, i, TAIL_CAST[x])
+            c_turn(1, t, i, "ez"[t])
+            if x == 4:
+                c_evac(1, 0, 0, "s")
+        state["round"] += 10
+        drain("v", 9999)
+        drain("v", 9999)
+        c_evac(1, 0, 1, "v")
+        c_evac(1, 1, 0, "s")
+        c_quant(1, 0, 0, 2)
+        c_evac(1, 1, 1, "v")
+        c_quant(1, 1, 0, 1)
+        c_quant(1, 1, 1, 2)
         c_scales(1)
-        assert not any(waiting.values()) and not hq and not ready
+        assert not any(waiting.values()) and not ready, waiting

@@ -13,45 +13,15 @@ ALU = mybir.AluOpType
 ACT = mybir.ActivationFunctionType
 AX = mybir.AxisListType
 
-NK, NS, NB, NC, D = 2, 2, 4, 4, 512
 P = 128
+NK, NS, NB, NC, D = 2, 2, 4, 4, 512
 NG = NC * NS
-AB = 16
-NT = D // P
-NBLK = P // AB
-E_BLOCKS = (7, 6)
-KMIN = NBLK - max(NBLK - x for x in E_BLOCKS)
+TILES = D // P
+STRIP = 16
+STRIPS = P // STRIP
+V_STRIPS = (7, 6)
 
 FLOPS = 2 * 2 * 2048 * 2048 * 512 + 2 * 64 * 2 * 512 * 512
-
-S_BUDGET = 700
-V_BUDGET = 1700
-G_BUDGET = 1800
-LAG_M3 = 2
-LAG_U = 1
-LAG_Q = 0
-LAG_SUM = 1
-LAG_ZE = 2
-LAG_CAST = 1
-LAG_TURN = 2
-EM_AT = 5
-SG_INPUTS = 1
-AHEAD = 1
-DMA_FROM = 99
-XBUFS = 3
-PACE = 3.1
-FINAL = ("g", "g")
-SQ = (14, 26)
-LAG_R = 3
-EM_FROM = 1
-LAST_AT = 6
-PREP_AT = (1, 7)
-V_AT = 12
-R_AT = (1, 2, 3, 4)
-TAIL_CAST = "ssssssss"
-CORR = ("v", 450)
-CAST = ("s", 450)
-R_ENG = ("g", "s", "g", "g")
 
 
 def tile_dmrgsinglesitempodavidsoncorrection_x1_kernel(
@@ -64,920 +34,793 @@ def tile_dmrgsinglesitempodavidsoncorrection_x1_kernel(
         psum = ctx.enter_context(tc.psum_pool(name="psum", bufs=2))
         ctx.enter_context(tc.manual_schedule())
 
-        bank_bufs = {"y": 2, "z": 2, "e": 2, "h": 1, "t": 1}
+        banks_of = {"y": 2, "z": 2, "e": 2, "h": 1, "turn": 1}
 
         def bank(tag):
-            return psum.tile([P, 512], F32, name="bank_" + tag, tag=tag, bufs=bank_bufs[tag])
+            return psum.tile([P, 512], F32, name="bank_" + tag, tag=tag, bufs=banks_of[tag])
 
-        lnat, psik, rnat, dnat, psin = {}, {}, {}, {}, {}
+        lenv_in, psi_lr, renv_in, d_in, psi_ap = {}, {}, {}, {}, {}
 
-        def raw_tile(name):
-            return work.tile([P, 4, 512], BF16, name=name, tag="raw", bufs=8, align_bytes=64)
+        def input_tile(name):
+            return work.tile([P, 4, 512], BF16, name=name, tag="input", bufs=8, align_bytes=64)
 
         def load_lenv(i):
-            lnat[i] = raw_tile("lnat%d" % i)
+            lenv_in[i] = input_tile("lenv_in%d" % i)
             nc.sync.dma_start(
-                out=lnat[i][:], in_=lenv[:, P * i : P * (i + 1), :].rearrange("b a l -> a b l")
+                out=lenv_in[i][:], in_=lenv[:, P * i : P * (i + 1), :].rearrange("b a l -> a b l")
             )
 
-        def load_psik(k, s):
-            psik[k, s] = raw_tile("psik%d%d" % (k, s))
-            nc.sync.dma_start(out=psik[k, s][:], in_=psi[k, s].rearrange("(p j) r -> p j r", j=4))
+        def load_psi_lr(k, s):
+            psi_lr[k, s] = input_tile("psi_lr%d%d" % (k, s))
+            nc.sync.dma_start(out=psi_lr[k, s][:], in_=psi[k, s].rearrange("(q e) r -> q e r", e=4))
 
         def load_renv(c):
-            rnat[c] = raw_tile("rnat%d" % c)
-            nc.sync.dma_start(out=rnat[c][:], in_=renv[c].rearrange("(p j) n -> p j n", j=4))
+            renv_in[c] = input_tile("renv_in%d" % c)
+            nc.sync.dma_start(out=renv_in[c][:], in_=renv[c].rearrange("(q e) p -> q e p", e=4))
 
-        def load_psin(k, t):
-            psin[k, t] = keep.tile([P, NT, 512], BF16, name="psin%d%d" % (k, t))
-            nc.sync.dma_start(out=psin[k, t][:], in_=psi[k, t].rearrange("(i a) p -> a i p", a=P))
+        def load_psi_ap(k, t):
+            psi_ap[k, t] = keep.tile([P, TILES, 512], BF16, name="psi_ap%d%d" % (k, t))
+            nc.sync.dma_start(out=psi_ap[k, t][:], in_=psi[k, t].rearrange("(i a) p -> a i p", a=P))
 
         def load_d(t):
-            dnat[t] = raw_tile("dnat%d" % t)
-            nc.sync.dma_start(out=dnat[t][:], in_=d[t].rearrange("(i a) p -> a i p", a=P))
+            d_in[t] = input_tile("d_in%d" % t)
+            nc.sync.dma_start(out=d_in[t][:], in_=d[t].rearrange("(i a) p -> a i p", a=P))
 
-        wb = keep.tile([P, 64], BF16, name="wb")
-        nc.vector.memset(wb[:], 0.0)
-        nc.scalar.dma_start(out=wb[0:1, :], in_=wmpo.rearrange("b s c t -> (b s c t)").unsqueeze(0))
-        glb = keep.tile([P, 4], BF16, name="glb")
-        nc.scalar.dma_start(out=glb[:], in_=gl.rearrange("(p j) -> p j", j=4))
-        load_psik(0, 0)
-        load_psik(0, 1)
+        w_row = keep.tile([P, NG * NG], BF16, name="w_row")
+        nc.vector.memset(w_row[:], 0.0)
+        gl_in = keep.tile([P, 4], BF16, name="gl_in")
+        nc.sync.dma_start(out=gl_in[:], in_=gl.rearrange("(q e) -> q e", e=4))
+        load_psi_lr(0, 0)
+        nc.sync.dma_start(out=w_row[0:1, :], in_=wmpo.rearrange("b s c t -> (b s c t)").unsqueeze(0))
+        load_psi_lr(0, 1)
         load_lenv(1)
-        grb = keep.tile([P, NC, 4], BF16, name="grb")
-        nc.scalar.dma_start(out=grb[:], in_=gr.rearrange("c (p t) -> p c t", t=4))
+        gr_in = keep.tile([P, NC, 4], BF16, name="gr_in")
+        nc.sync.dma_start(out=gr_in[:], in_=gr.rearrange("c (q e) -> q c e", e=4))
         load_lenv(0)
         load_lenv(2)
         load_renv(0)
 
-        def later_loads():
-            load_renv(1)
-            load_renv(2)
-            load_renv(3)
-
-        def more_loads():
+        def load_second_part():
+            for c in range(1, NC):
+                load_renv(c)
             load_lenv(3)
             for t in range(NS):
                 load_d(t)
-                load_psin(0, t)
+                load_psi_ap(0, t)
 
-        def last_loads():
+        def load_third_part():
             for s in range(NS):
-                load_psik(1, s)
+                load_psi_lr(1, s)
             for t in range(NS):
-                load_psin(1, t)
+                load_psi_ap(1, t)
 
         ident = keep.tile([P, P], F32, name="ident")
         make_identity(nc, ident[:])
-        onecol = keep.tile([P, 1], F32, name="onecol")
-        nc.vector.memset(onecol[:], 1.0)
-        tabl = keep.tile([P, 1], F32, name="tabl")
-        nc.scalar.activation(tabl[:], onecol[:], ACT.Abs_reciprocal_sqrt)
-        ones = keep.tile([P, P], F32, name="ones")
-        onesb = keep.tile([P, P], BF16, name="onesb")
-        nc.vector.memset(onesb[:], 1.0)
+        one = keep.tile([P, 1], F32, name="one")
+        nc.vector.memset(one[:], 1.0)
+        table_load = keep.tile([P, 1], F32, name="table_load")
+        nc.scalar.activation(table_load[:], one[:], ACT.Abs_reciprocal_sqrt)
+        minus_ones = keep.tile([P, P], F32, name="minus_ones")
+        ones = keep.tile([P, P], BF16, name="ones")
+        nc.vector.memset(ones[:], 1.0)
 
-        lcw, lsw = {}, {}
-        for i in range(NT):
-            n = 3 * 64 if i == 0 else 4 * 3 * 64
-            lcw[i] = keep.tile([P, n], U32, name="lcw%d" % i, align_bytes=64)
-            lsw[i] = keep.tile([P, n], U8, name="lsw%d" % i, align_bytes=64)
+        gl_f = keep.tile([P, 4], F32, name="gl_f")
+        w_all = keep.tile([P, NG, NG], F32, name="w_all")
+        same_a = keep.tile([P, STRIP], F32, name="same_a")
+        same_sb = keep.tile([P, NG], F32, name="same_sb")
+        w_pick = keep.tile([P, NG, NG], F32, name="w_pick")
+        w_own = keep.tile([P, NG], F32, name="w_own")
+        mixer = keep.tile([P, P], F32, name="mixer")
+        gr_all = keep.tile([P, NG, 4], F32, name="gr_all")
 
-        wf = keep.tile([P, NG, NG], F32, name="wf")
-        dmat = keep.tile([P, AB], F32, name="dmat")
-        sel = [keep.tile([P, NG], F32, name="sel%d" % h) for h in range(2)]
-        wprod = [keep.tile([P, NG, NG], F32, name="wprod%d" % h) for h in range(2)]
-        wcol = [keep.tile([P, NG], F32, name="wcol%d" % h) for h in range(2)]
-        wk = [keep.tile([P, P], F32, name="wk%d" % h) for h in range(2)]
-        grt = keep.tile([P, NG, 4], F32, name="grt")
-
-        def small_constants():
-            wbank = bank("e")
-            nc.tensor.matmul(wbank[:, 0:64], onesb[:], wb[:], start=True, stop=True)
-            nc.vector.tensor_copy(
-                out=wf[:].rearrange("p q (t c) -> p q t c", t=NS),
-                in_=wbank[:, 0:64].rearrange("p (q c t) -> p q t c", q=NG, t=NS),
-            )
-
-        def small_constants_0():
+        def make_selectors():
+            split = ident[:].rearrange("x (sb a) -> x sb a", a=STRIP)
             nc.vector.tensor_reduce(
-                out=dmat[:], in_=ident[:].rearrange("p (q a) -> p a q", a=AB), axis=AX.X, op=ALU.add
+                out=same_a[:], in_=split.rearrange("x sb a -> x a sb"), axis=AX.X, op=ALU.add
             )
-            nc.vector.tensor_reduce(
-                out=sel[0][:], in_=ident[:].rearrange("p (q a) -> p q a", a=AB), axis=AX.X, op=ALU.add
-            )
-            for s in range(NS):
-                nc.vector.tensor_copy(
-                    out=sel[1][:, NB * s : NB * (s + 1)], in_=sel[0][:, NB * (1 - s) : NB * (2 - s)]
-                )
+            nc.vector.tensor_reduce(out=same_sb[:], in_=split, axis=AX.X, op=ALU.add)
 
-        def small_constants_2():
+        def spread_w():
+            spread = bank("e")
+            nc.tensor.matmul(spread[:, 0 : NG * NG], ones[:], w_row[:], start=True, stop=True)
             nc.vector.tensor_copy(
-                out=grt[:].rearrange("p (s c) t -> p s (c t)", s=NS),
-                in_=grb[:].rearrange("p c t -> p (c t)").unsqueeze(1).to_broadcast([P, NS, 4 * NC]),
+                out=w_all[:].rearrange("x bs (t c) -> x bs t c", t=NS),
+                in_=spread[:, 0 : NG * NG].rearrange("x (bs c t) -> x bs t c", bs=NG, t=NS),
             )
-            for h in range(2):
-                nc.vector.tensor_tensor(
-                    out=wprod[h][:].rearrange("p g (s b) -> p g s b", s=NS),
-                    in0=wf[:].rearrange("p (b s) g -> p g s b", s=NS),
-                    in1=sel[h][:].rearrange("p (s b) -> p s b", s=NS).unsqueeze(1).to_broadcast([P, NG, NS, NB]),
-                    op=ALU.mult,
-                )
-            for h in range(2):
-                nc.vector.tensor_reduce(out=wcol[h][:], in_=wprod[h][:], axis=AX.X, op=ALU.add)
-            for h in range(2):
-                nc.vector.tensor_tensor(
-                    out=wk[h][:].rearrange("p (g a) -> p g a", a=AB),
-                    in0=wcol[h][:].unsqueeze(2).to_broadcast([P, NG, AB]),
-                    in1=dmat[:].unsqueeze(1).to_broadcast([P, NG, AB]),
-                    op=ALU.mult,
-                )
+
+        def make_mixer():
+            nc.vector.tensor_copy(
+                out=gr_all[:].rearrange("q (t c) e -> q t (c e)", t=NS),
+                in_=gr_in[:].rearrange("q c e -> q (c e)").unsqueeze(1).to_broadcast([P, NS, 4 * NC]),
+            )
+            nc.vector.tensor_tensor(
+                out=w_pick[:].rearrange("x g (s b) -> x g s b", s=NS),
+                in0=w_all[:].rearrange("x (b s) g -> x g s b", s=NS),
+                in1=same_sb[:].rearrange("x (s b) -> x s b", s=NS).unsqueeze(1).to_broadcast([P, NG, NS, NB]),
+                op=ALU.mult,
+            )
+            nc.vector.tensor_reduce(out=w_own[:], in_=w_pick[:], axis=AX.X, op=ALU.add)
+            nc.vector.tensor_tensor(
+                out=mixer[:].rearrange("x (g a) -> x g a", a=STRIP),
+                in0=w_own[:].unsqueeze(2).to_broadcast([P, NG, STRIP]),
+                in1=same_a[:].unsqueeze(1).to_broadcast([P, NG, STRIP]),
+                op=ALU.mult,
+            )
 
         def stage_tile(name):
-            return work.tile([P, 2048], BF16, name=name, tag="st", bufs=4, align_bytes=64)
+            return work.tile([P, 2048], BF16, name=name, tag="stage", bufs=4, align_bytes=64)
 
-        def quant(codes, scales, src):
-            nc.vector.quantize_mx(out=codes.bitcast(FP8X4), scales=scales, in_=src)
+        def quantise(codes, scales, values):
+            nc.vector.quantize_mx(out=codes.bitcast(FP8X4), scales=scales, in_=values)
 
-        lst, xlen = {}, {}
+        HELD = (2, STRIPS, STRIPS, STRIPS)
+        lenv_codes, lenv_scales, lenv_stage, lenv_banks = {}, {}, {}, {}
+        for i in range(TILES):
+            n = 64 + P * HELD[i]
+            lenv_codes[i] = keep.tile([P, n], U32, name="lenv_codes%d" % i, align_bytes=64)
+            lenv_scales[i] = keep.tile([P, n], U8, name="lenv_scales%d" % i, align_bytes=64)
+        lenv0_codes = keep.tile([P, 512], U32, name="lenv0_codes", align_bytes=64)
+        lenv0_scales = keep.tile([P, 512], U8, name="lenv0_scales", align_bytes=64)
+        lenv0_strips = keep.tile([P, 2, 2, 256], BF16, name="lenv0_strips", align_bytes=64)
 
-        def lenv_pe(i):
-            words = lnat[i][:].rearrange("p b l -> p (b l)").bitcast(F32)
-            for h in range(2):
-                x = bank("ht"[h])
-                xlen[i, h] = x
-                for bb in range(2):
-                    b = 2 * h + bb
-                    for u in range(2):
-                        nc.tensor.transpose(
-                            x[:, (2 * bb + u) * P : (2 * bb + u + 1) * P],
-                            words[:, 256 * b + u : 256 * (b + 1) : 2],
-                            ident[:],
-                        )
+        def zero_first_columns(i):
+            nc.gpsimd.memset(lenv_codes[i][:, 0:64], 0)
+            nc.gpsimd.memset(lenv_scales[i][:, 0:64].bitcast(I32), 0)
 
-        def lenv_view(i, b):
-            return xlen[i, b // 2][:, (b % 2) * 256 : (b % 2) * 256 + 256]
+        def zero_halves(values, strips):
+            words = values.rearrange("q k z x -> q (k z x)").bitcast(U32)
+            nc.gpsimd.memset(words.rearrange("q (k z x) -> q k z x", k=strips, z=2)[:, :, 1], 0)
 
-        def lenv_evac(i):
-            lst[i] = work.tile([P, 4096], BF16, name="lst%d" % i, tag="zst", bufs=2, align_bytes=64)
-            dst = lst[i][:, 0:3072].bitcast(F32).rearrange("p (k z b a u) -> p k z b a u", z=3, b=NB, a=AB, u=2)
+        def lenv_zeros(i):
+            lenv_stage[i] = work.tile(
+                [P, STRIPS, 2, 256], BF16, name="lenv_stage%d" % i, tag="z_stage", bufs=2, align_bytes=64
+            )
+            zero_halves(lenv_stage[i][:], STRIPS)
+
+        def lenv_turn(i):
+            words = lenv_in[i][:].rearrange("a b l -> a (b l)").bitcast(F32)
+            for half, tag in enumerate(("h", "turn")):
+                lenv_banks[i, half] = bank(tag)
+                for x in range(4):
+                    b, u = 2 * half + x // 2, x % 2
+                    nc.tensor.transpose(
+                        lenv_banks[i, half][:, P * x : P * (x + 1)],
+                        words[:, 256 * b + u : 256 * (b + 1) : 2],
+                        ident[:],
+                    )
+
+        def lenv_bank(i, b):
+            return lenv_banks[i, b // 2][:, 256 * (b % 2) : 256 * (b % 2 + 1)]
+
+        def lenv_copy(i):
+            words = lenv_stage[i][:].rearrange("q k z x -> q (k z x)").bitcast(F32)
+            out = words.rearrange("q (k z b a u) -> q k z b a u", k=STRIPS, z=2, b=NB, a=STRIP)
             for b in range(NB):
-                src = lenv_view(i, b).rearrange("p (u k h a) -> p k h a u", u=2, h=2, a=AB)
-                nc.scalar.copy(out=dst[:, :, 0:2, b], in_=src)
-                nc.scalar.copy(out=dst[:, :, 2, b], in_=src[:, :, 0])
+                nc.scalar.copy(
+                    out=out[:, :, 0, b], in_=lenv_bank(i, b).rearrange("q (u k a) -> q k a u", u=2, k=STRIPS)
+                )
 
-        def lenv_quant(i, c0, c1):
-            quant(lcw[i][:, c0:c1], lsw[i][:, c0:c1], lst[i][:, 4 * c0 : 4 * c1])
+        def lenv_quantise(i, strip_0, strip_1):
+            x0, x1 = 64 + P * strip_0, 64 + P * strip_1
+            values = lenv_stage[i][:].rearrange("q k z x -> q (k z x)")
+            quantise(lenv_codes[i][:, x0:x1], lenv_scales[i][:, x0:x1], values[:, 512 * strip_0 : 512 * strip_1])
 
-        lc0 = keep.tile([P, 512], U32, name="lc0", align_bytes=64)
-        ls0 = keep.tile([P, 512], U8, name="ls0", align_bytes=64)
-        lst0k = keep.tile([P, 768], BF16, name="lst0k", align_bytes=64)
-
-        def lenv0_evac():
-            lst[0] = stage_tile("lst0")
-            dst = lst[0][:].bitcast(F32).rearrange("p (b a u) -> p b a u", b=NB, a=P)
+        def lenv0_copy():
+            lenv_stage[0] = stage_tile("lenv_stage0")
+            out = lenv_stage[0][:].bitcast(F32).rearrange("q (b a u) -> q b a u", b=NB, a=P)
             for b in range(NB):
-                nc.scalar.copy(out=dst[:, b], in_=lenv_view(0, b).rearrange("p (u a) -> p a u", u=2))
+                nc.scalar.copy(out=out[:, b], in_=lenv_bank(0, b).rearrange("q (u a) -> q a u", u=2))
 
-        def lenv0_pair():
-            dst = lst0k[:].rearrange("p (z b x) -> p z b x", z=3, b=NB)
-            src = lst[0][:].rearrange("p (b k x) -> p k b x", b=NB, k=NBLK)
-            nc.gpsimd.tensor_copy(out=dst[:, 0:2], in_=src[:, NBLK - 2 :])
-            nc.gpsimd.tensor_copy(out=dst[:, 2], in_=src[:, NBLK - 2])
+        def lenv0_strips_copy():
+            zero_halves(lenv0_strips[:], 2)
+            out = lenv0_strips[:].rearrange("q k z (b x) -> q k z b x", b=NB)[:, :, 0]
+            values = lenv_stage[0][:].rearrange("q (b k x) -> q k b x", b=NB, k=STRIPS)
+            nc.gpsimd.tensor_copy(out=out, in_=values[:, STRIPS - 2 :])
 
-        def lenv0_quant():
-            for c0, c1 in ((0, 128), (128, 192)):
-                quant(lcw[0][:, c0:c1], lsw[0][:, c0:c1], lst0k[:, 4 * c0 : 4 * c1])
+        def lenv0_strips_quantise():
+            values = lenv0_strips[:].rearrange("q k z x -> q (k z x)")
+            quantise(lenv_codes[0][:, 64 : 64 + 2 * P], lenv_scales[0][:, 64 : 64 + 2 * P], values)
 
-        vc, vs, vst = {}, {}, {}
+        v_codes, v_scales, v_stage, scaled = {}, {}, {}, {}
         for k in range(NK):
             for s in range(NS):
-                vc[k, s] = keep.tile([P, 512], U32, name="vc%d%d" % (k, s), align_bytes=64)
-                vs[k, s] = keep.tile([P, 512], U8, name="vs%d%d" % (k, s), align_bytes=64)
+                v_codes[k, s] = keep.tile([P, 512], U32, name="v_codes%d%d" % (k, s), align_bytes=64)
+                v_scales[k, s] = keep.tile([P, 512], U8, name="v_scales%d%d" % (k, s), align_bytes=64)
 
-        def v_part(k, s, t0, t1, engine):
-            if (k, s) not in vst:
-                vst[k, s] = stage_tile("vst%d%d" % (k, s))
-            for t in range(t0, t1) if engine == "g" else (t0,):
-                n = 1 if engine == "g" else t1 - t0
-                e = nc.gpsimd if engine == "g" else nc.vector
-                out = vst[k, s][:].rearrange("p (t q j) -> p t q j", t=4, j=4)
-                src = psik[k, s][:].rearrange("p j (q t) -> p t q j", t=4)
-                if engine == "g":
-                    e.tensor_tensor(
-                        out=out[:, t], in0=src[:, t],
-                        in1=glb[:].unsqueeze(1).to_broadcast([P, P, 4]), op=ALU.mult,
-                    )
-                else:
-                    e.tensor_tensor(
-                        out=out[:, t0:t1], in0=src[:, t0:t1],
-                        in1=glb[:].unsqueeze(1).unsqueeze(1).to_broadcast([P, n, P, 4]), op=ALU.mult,
-                    )
+        def v_out(k, s):
+            return v_stage[k, s][:].rearrange("m (e q f) -> m e q f", e=4, f=4)
 
-        def v_quant(k, s):
-            quant(vc[k, s][:], vs[k, s][:], vst[k, s][:])
+        def v_in(k, s):
+            return psi_lr[k, s][:].rearrange("m f (q e) -> m e q f", e=4)
 
-        rc, rs, rst = {}, {}, {}
-        for c in range(NC):
-            rc[c] = keep.tile([P, 512], U32, name="rc%d" % c, align_bytes=64)
-            rs[c] = keep.tile([P, 512], U8, name="rs%d" % c, align_bytes=64)
-
-        def r_copy(c, part, eng):
-            if part == 0:
-                rst[c] = stage_tile("rst%d" % c)
-            dst = rst[c][:].rearrange("p (n j) -> p n j", j=4)[:, P * part : P * (part + 1)]
-            src = rnat[c][:].rearrange("p j n -> p n j")[:, P * part : P * (part + 1)]
-            if eng == "s":
-                nc.scalar.copy(out=dst, in_=src)
-            else:
-                nc.gpsimd.tensor_scalar(dst, src, 1.0, 0.0, ALU.mult, ALU.add)
-
-        def r_quant(c):
-            quant(rc[c][:], rs[c][:], rst[c][:])
-
-        rd, rtmp = {}, {}
-        for t in range(NS):
-            for i in range(NT):
-                rd[t, i] = keep.tile([P, 512], F32, name="rd%d%d" % (t, i))
-
-        def rd_first(t, i):
-            nc.scalar.activation(
-                rd[t, i][:], dnat[t][:, i, :], ACT.Abs_reciprocal_sqrt, bias=onecol[:, 0:1]
+        def v_on_vector(k, s):
+            v_stage[k, s] = stage_tile("v_stage%d%d" % (k, s))
+            nc.vector.tensor_tensor(
+                out=v_out(k, s),
+                in0=v_in(k, s),
+                in1=gl_in[:].unsqueeze(1).unsqueeze(1).to_broadcast([P, 4, P, 4]),
+                op=ALU.mult,
             )
 
-        def rd_second(t, i):
-            rtmp[t, i] = work.tile([P, 512], BF16, name="rg", tag="rg", bufs=8)
-            nc.scalar.activation(rtmp[t, i][:], dnat[t][:, i, :], ACT.Sign, bias=onecol[:, 0:1])
+        def v_on_gpsimd(k, s, e):
+            if e == 0:
+                v_stage[k, s] = stage_tile("v_stage%d%d" % (k, s))
+            nc.gpsimd.tensor_tensor(
+                out=v_out(k, s)[:, e],
+                in0=v_in(k, s)[:, e],
+                in1=gl_in[:].unsqueeze(1).to_broadcast([P, P, 4]),
+                op=ALU.mult,
+            )
 
-        def rd_third(t, i):
-            nc.scalar.activation(rd[t, i][:], rd[t, i][:], ACT.Square)
+        def v_on_scalar(k, s):
+            scaled[k, s] = stage_tile("scaled")
+            for f in range(4):
+                nc.scalar.activation(
+                    scaled[k, s][:, 512 * f : 512 * (f + 1)], psi_lr[k, s][:, f, :], ACT.Copy, scale=gl_f[:, f : f + 1]
+                )
 
-        def rd_g(t, i):
-            nc.gpsimd.tensor_tensor(out=rd[t, i][:], in0=rd[t, i][:], in1=rtmp[t, i][:], op=ALU.mult)
+        def v_interleave(k, s):
+            v_stage[k, s] = stage_tile("v_stage%d%d" % (k, s))
+            nc.vector.tensor_copy(
+                out=v_out(k, s), in_=scaled[k, s][:].rearrange("m (f q e) -> m e q f", f=4, e=4)
+            )
 
-        stat, sones, nov = {}, {}, {}
+        def v_quantise(k, s):
+            quantise(v_codes[k, s][:], v_scales[k, s][:], v_stage[k, s][:])
+
+        renv_codes, renv_scales, renv_stage = {}, {}, {}
+        for c in range(NC):
+            renv_codes[c] = keep.tile([P, 512], U32, name="renv_codes%d" % c, align_bytes=64)
+            renv_scales[c] = keep.tile([P, 512], U8, name="renv_scales%d" % c, align_bytes=64)
+
+        def renv_interleave(c, part, engine):
+            if part == 0:
+                renv_stage[c] = stage_tile("renv_stage%d" % c)
+            cols = slice(P * part, P * (part + 1))
+            out = renv_stage[c][:].rearrange("q (p e) -> q p e", e=4)[:, cols]
+            values = renv_in[c][:].rearrange("q e p -> q p e")[:, cols]
+            if engine == "scalar":
+                nc.scalar.copy(out=out, in_=values)
+            else:
+                nc.gpsimd.tensor_scalar(out, values, 1.0, 0.0, ALU.mult, ALU.add)
+
+        def renv_quantise(c):
+            quantise(renv_codes[c][:], renv_scales[c][:], renv_stage[c][:])
+
+        inverse, sign = {}, {}
+        for t in range(NS):
+            for i in range(TILES):
+                inverse[t, i] = keep.tile([P, 512], F32, name="inverse%d%d" % (t, i))
+
+        def inverse_root(t, i):
+            nc.scalar.activation(
+                inverse[t, i][:], d_in[t][:, i, :], ACT.Abs_reciprocal_sqrt, bias=one[:, 0:1]
+            )
+
+        def inverse_sign(t, i):
+            sign[t, i] = work.tile([P, 512], BF16, name="sign", tag="sign", bufs=8)
+            nc.scalar.activation(sign[t, i][:], d_in[t][:, i, :], ACT.Sign, bias=one[:, 0:1])
+
+        def inverse_square(t, i):
+            nc.scalar.activation(inverse[t, i][:], inverse[t, i][:], ACT.Square)
+
+        def inverse_join(t, i):
+            nc.gpsimd.tensor_tensor(out=inverse[t, i][:], in0=inverse[t, i][:], in1=sign[t, i][:], op=ALU.mult)
+
+        sums, norm, norm_bank, scaled_ones = {}, {}, {}, {}
         for k in range(NK):
-            stat[k] = keep.tile([P, 2, NG], F32, name="stat%d" % k)
-            sones[k] = keep.tile([P, P], F32, name="sones%d" % k)
-            nov[k] = keep.tile([P, 1], F32, name="nov%d" % k)
+            sums[k] = keep.tile([P, 2, NG], F32, name="sums%d" % k)
+            norm[k] = keep.tile([P, 2], F32, name="norm%d" % k)
+            scaled_ones[k] = keep.tile([P, P], F32, name="scaled_ones%d" % k)
 
         def psi_square(k, t, i):
-            junk = work.tile([P, 512], BF16, name="junk", tag="junk", bufs=2)
-            j = t * NT + i
-            nc.scalar.activation(
-                junk[:], psin[k, t][:, i, :], ACT.Square, accum_out=stat[k][:, 1, j : j + 1]
-            )
+            unused = work.tile([P, 512], BF16, name="unused", tag="unused", bufs=2)
+            j = t * TILES + i
+            nc.scalar.activation(unused[:], psi_ap[k, t][:, i, :], ACT.Square, accum_out=sums[k][:, 1, j : j + 1])
 
-        norm = {}
+        def norm_partial(k):
+            nc.vector.tensor_reduce(out=norm[k][:, 0:1], in_=sums[k][:, 1, :], axis=AX.X, op=ALU.add)
 
-        def norm_a(k):
-            norm[k] = keep.tile([P, 2], F32, name="norm%d" % k)
-            nc.vector.tensor_reduce(out=norm[k][:, 0:1], in_=stat[k][:, 1, :], axis=AX.X, op=ALU.add)
+        def norm_total(k):
+            norm_bank[k] = bank("turn")
+            nc.tensor.matmul(norm_bank[k][:, 0:1], minus_ones[:], norm[k][:, 0:1], start=True, stop=True)
 
-        def norm_b(k):
-            norm[k, "bank"] = bank("t")
-            nc.tensor.matmul(norm[k, "bank"][:, 0:1], ones[:], norm[k][:, 0:1], start=True, stop=True)
+        def norm_inverse(k):
+            nc.vector.reciprocal(out=norm[k][:, 1:2], in_=norm_bank[k][:, 0:1])
 
-        def norm_c(k):
-            nc.vector.reciprocal(out=norm[k][:, 1:2], in_=norm[k, "bank"][:, 0:1])
-            nc.vector.tensor_scalar(sones[k][:], ones[:], norm[k][:, 1:2], -1.0, ALU.mult, ALU.mult)
+        def norm_spread(k):
+            nc.scalar.activation(scaled_ones[k][:], ones[:], ACT.Copy, scale=norm[k][:, 1:2])
 
-        blocks = []
-        for k in range(NK):
-            order = [(i, j ^ 1) for i in (1, 2, 0, 3) for j in range(NBLK)]
-            order = [(i, j) for i, j in order if i > 0 or j >= E_BLOCKS[k]]
-            blocks += [(k, i, j) for i, j in order]
-        nblocks = len(blocks)
-        last_of = {}
-        for n, (k, i, j) in enumerate(blocks):
-            last_of[k, i] = n
-        ybank, ysb, zbank, zst, zc, zs = {}, {}, {}, {}, {}, {}
+        strips = [
+            (k, i, j)
+            for k in range(NK)
+            for i in (1, 2, 0, 3)
+            for j in range(STRIPS)
+            if i > 0 or j >= V_STRIPS[k]
+        ]
+        y_bank, y_sb, z_bank, z_stage, z_codes, z_scales = {}, {}, {}, {}, {}, {}
 
-        pairs, members = [], []
-        for n, (k, i, j) in enumerate(blocks):
-            if not pairs or pairs[-1] != (k, i, j // 2):
-                pairs.append((k, i, j // 2))
-                members.append([])
-            members[-1].append(n)
-
-        def m1(x):
-            k, i, pp = pairs[x]
+        def strip_y(n):
+            k, i, j = strips[n]
+            y_bank[n] = bank("y")
             for s in range(NS):
-                ybank[x, s] = bank("y")
-                c0 = 64 * s + (0 if i == 0 else 192 * pp)
+                x0 = 64 + P * (j - STRIPS + HELD[i]) - 64 * s
                 nc.tensor.matmul_mx(
-                    out=ybank[x, s][:],
-                    lhsT=lcw[i][:, c0 : c0 + P].bitcast(FP8X4),
-                    lhsT_scale=lsw[i][:, c0 : c0 + P],
-                    rhs=vc[k, s][:].bitcast(FP8X4),
-                    rhs_scale=vs[k, s][:],
-                    start=True,
-                    stop=True,
+                    out=y_bank[n][:],
+                    lhsT=lenv_codes[i][:, x0 : x0 + P].bitcast(FP8X4),
+                    lhsT_scale=lenv_scales[i][:, x0 : x0 + P],
+                    rhs=v_codes[k, s][:].bitcast(FP8X4),
+                    rhs_scale=v_scales[k, s][:],
+                    start=(s == 0),
+                    stop=(s == NS - 1),
                 )
 
-        xs = {}
+        def strip_copy(n):
+            y_sb[n] = work.tile([P, 512], F32, name="y_sb", tag="y_sb", bufs=4)
+            nc.scalar.copy(out=y_sb[n][:], in_=y_bank[n][:])
 
-        def by_dma(x):
-            return x >= DMA_FROM
-
-        def e1(x, part):
-            if by_dma(x):
-                if part == 0:
-                    for s in range(NS):
-                        xs[x, s] = work.tile([P, 512], F32, name="xs", tag="xs%d" % s, bufs=(XBUFS, 2)[s])
-                        nc.scalar.copy(out=xs[x, s][:], in_=ybank[x, s][:])
-                    xs[x, 2] = work.tile([P, 512], F32, name="xw", tag="xw", bufs=XBUFS)
-                    nc.scalar.dma_start(out=xs[x, 2][64:128, :], in_=xs[x, 0][64:128, :])
-                    nc.scalar.dma_start(out=xs[x, 2][0:64, :], in_=xs[x, 1][0:64, :])
-                elif len(members[x]) == 2:
-                    nc.scalar.dma_start(out=xs[x, 0][64:128, :], in_=xs[x, 1][64:128, :])
-                for n in members[x]:
-                    ysb[n] = xs[x, 2 if blocks[n][2] % 2 else 0]
-            elif part < len(members[x]):
-                n = members[x][part]
-                h = blocks[n][2] % 2
-                tag = "xw" if h else "xs0"
-                ysb[n] = work.tile([P, 512], F32, name="ysb", tag=tag, bufs=XBUFS)
-                nc.scalar.copy(out=ysb[n][0:64, :], in_=ybank[x, h][0:64, :])
-                nc.scalar.copy(out=ysb[n][64:128, :], in_=ybank[x, 1 - h][64:128, :])
-
-        def m2(n):
-            zbank[n] = bank("z")
-            for t in range(4):
+        def strip_mix(n):
+            z_bank[n] = bank("z")
+            for e in range(4):
                 nc.tensor.matmul(
-                    zbank[n][:, P * t : P * (t + 1)],
-                    ysb[n][:, P * t : P * (t + 1)],
-                    wk[blocks[n][2] % 2][:],
-                    start=True,
-                    stop=True,
+                    z_bank[n][:, P * e : P * (e + 1)], y_sb[n][:, P * e : P * (e + 1)], mixer[:], start=True, stop=True
                 )
 
-        def zst_tile(k, i):
-            if (k, i) not in zst:
-                if i == 0:
-                    zst[k, i] = work.tile([P, NG, P, 4], BF16, name="zse", tag="zse", bufs=1, align_bytes=64)
-                else:
-                    zst[k, i] = work.tile([P, NG, P, 4], BF16, name="zst", tag="zst", bufs=2, align_bytes=64)
-            return zst[k, i]
+        def z_tile(k, i):
+            if (k, i) not in z_stage:
+                tag, bufs = ("z_stage", 2) if i else ("z_stage0", 1)
+                z_stage[k, i] = work.tile([P, NG, P, 4], BF16, name=tag, tag=tag, bufs=bufs, align_bytes=64)
+            return z_stage[k, i]
 
-        def e2(n):
-            k, i, j = blocks[n]
+        def strip_z(n):
+            k, i, j = strips[n]
             nc.vector.tensor_tensor(
-                out=zst_tile(k, i)[:, :, AB * j : AB * (j + 1), :],
-                in0=zbank[n][:].rearrange("p (t g a) -> p g a t", t=4, g=NG),
-                in1=grt[:].unsqueeze(2).to_broadcast([P, NG, AB, 4]),
+                out=z_tile(k, i)[:, :, STRIP * j : STRIP * (j + 1), :],
+                in0=z_bank[n][:].rearrange("q (e g a) -> q g a e", e=4, g=NG),
+                in1=gr_all[:].unsqueeze(2).to_broadcast([P, NG, STRIP, 4]),
                 op=ALU.mult,
             )
 
-        ebank, acc = {}, {}
+        e_bank, acc = {}, {}
 
-        def em(k, q):
-            b, s = divmod(q, NS)
-            ebank[k, q] = bank("e")
-            for t in range(4):
+        def input_y(k, n):
+            b, s = divmod(n, NS)
+            e_bank[k, n] = bank("e")
+            for e in range(4):
                 nc.tensor.matmul_mx(
-                    out=ebank[k, q][:, P * t : P * (t + 1)],
-                    lhsT=vc[k, s][:, P * t : P * (t + 1)].bitcast(FP8X4),
-                    lhsT_scale=vs[k, s][:, P * t : P * (t + 1)],
-                    rhs=lc0[:, P * b : P * (b + 1)].bitcast(FP8X4),
-                    rhs_scale=ls0[:, P * b : P * (b + 1)],
+                    out=e_bank[k, n][:, P * e : P * (e + 1)],
+                    lhsT=v_codes[k, s][:, P * e : P * (e + 1)].bitcast(FP8X4),
+                    lhsT_scale=v_scales[k, s][:, P * e : P * (e + 1)],
+                    rhs=lenv0_codes[:, P * b : P * (b + 1)].bitcast(FP8X4),
+                    rhs_scale=lenv0_scales[:, P * b : P * (b + 1)],
                     start=True,
                     stop=True,
                 )
 
-        def e_in(k, q):
-            na = AB * E_BLOCKS[k]
-            return ebank[k, q][:].rearrange("p (t a) -> p t a", t=4)[:, :, 0:na]
-
-        def fma(k, q, g):
-            w = wf[:, q, g : g + 1]
-            na = AB * E_BLOCKS[k]
-            if 0 < q < SG_INPUTS:
-                part = work.tile([P, 4, na], F32, name="part", tag="part", bufs=2)
-                nc.scalar.activation(part[:], e_in(k, q), ACT.Copy, scale=w)
-                return part
-            if q == 0:
-                acc[k, g] = work.tile([P, 4, na], F32, name="acc%d" % g, tag="acc%d" % g, bufs=1)
-                nc.scalar.activation(acc[k, g][:], e_in(k, 0), ACT.Copy, scale=w)
+        def add_input(k, n, g):
+            width = STRIP * V_STRIPS[k]
+            y = e_bank[k, n][:].rearrange("q (e a) -> q e a", e=4)[:, :, 0:width]
+            w = w_all[:, n, g : g + 1]
+            if n == 0:
+                acc[k, g] = work.tile([P, 4, width], F32, name="acc%d" % g, tag="acc%d" % g, bufs=1)
+                nc.scalar.activation(acc[k, g][:], y, ACT.Copy, scale=w)
             else:
                 nc.vector.scalar_tensor_tensor(
-                    out=acc[k, g][:], in0=e_in(k, q), scalar=w, in1=acc[k, g][:], op0=ALU.mult, op1=ALU.add
+                    out=acc[k, g][:], in0=y, scalar=w, in1=acc[k, g][:], op0=ALU.mult, op1=ALU.add
                 )
 
-        def fma_add(k, g, part):
-            nc.gpsimd.tensor_tensor(out=acc[k, g][:], in0=acc[k, g][:], in1=part[:], op=ALU.add)
+        def finish_output(k, g, engine):
+            width = STRIP * V_STRIPS[k]
+            out = z_tile(k, 0)[:, g, 0:width, :]
+            if engine == "scalar":
+                for e in range(4):
+                    nc.scalar.activation(out[:, :, e], acc[k, g][:, e, :], ACT.Copy, scale=gr_all[:, g, e : e + 1])
+            else:
+                nc.gpsimd.tensor_tensor(
+                    out=out,
+                    in0=acc[k, g][:].rearrange("q e a -> q a e"),
+                    in1=gr_all[:, g : g + 1, :].to_broadcast([P, width, 4]),
+                    op=ALU.mult,
+                )
 
-        def e_final(k, g, engine):
-            na = AB * E_BLOCKS[k]
-            if engine == "s":
-                for t in range(4):
-                    nc.scalar.activation(
-                        zst_tile(k, 0)[:, g, 0:na, t], acc[k, g][:, t, :], ACT.Copy, scale=grt[:, g, t : t + 1]
-                    )
-                return
-            e = nc.gpsimd if engine == "g" else nc.vector
-            e.tensor_tensor(
-                out=zst_tile(k, 0)[:, g, 0:na, :],
-                in0=acc[k, g][:].rearrange("p t a -> p a t"),
-                in1=grt[:, g : g + 1, :].to_broadcast([P, na, 4]),
-                op=ALU.mult,
-            )
+        h_bank, minus_u, q_tile, psi_q = {}, {}, {}, {}
 
-        hbank, qt, ut, pq = {}, {}, {}, {}
+        def z_code_tiles(k, i):
+            z_codes[k, i] = work.tile([P, NG * P], U32, name="z_codes", tag="z_codes", bufs=2, align_bytes=64)
+            z_scales[k, i] = work.tile([P, NG * P], U8, name="z_scales", tag="z_scales", bufs=2, align_bytes=64)
 
-        def z_tiles(k, i):
-            zc[k, i] = work.tile([P, 1024], U32, name="zc", tag="zc", bufs=2, align_bytes=64)
-            zs[k, i] = work.tile([P, 1024], U8, name="zs", tag="zs", bufs=2, align_bytes=64)
+        def z_quantise(k, i, x0, x1):
+            values = z_stage[k, i][:].rearrange("q g a e -> q (g a e)")
+            quantise(z_codes[k, i][:, x0:x1], z_scales[k, i][:, x0:x1], values[:, 4 * x0 : 4 * x1])
 
-        def z_quant(k, i, c0, c1):
-            flat = zst[k, i][:].rearrange("p g a t -> p (g a t)")
-            quant(zc[k, i][:, c0:c1], zs[k, i][:, c0:c1], flat[:, 4 * c0 : 4 * c1])
+        def z_quantise_tile(k, i):
+            z_code_tiles(k, i)
+            z_quantise(k, i, 0, NG * P)
 
-        def m3(k, i, t, tag):
-            hbank[k, i, t] = bank(tag)
+        def h_product(k, i, t, tag):
+            h_bank[k, i, t] = bank(tag)
             for c in range(NC):
-                c0 = (NC * t + c) * P
+                x0 = (NC * t + c) * P
                 nc.tensor.matmul_mx(
-                    out=hbank[k, i, t][:],
-                    lhsT=zc[k, i][:, c0 : c0 + P].bitcast(FP8X4),
-                    lhsT_scale=zs[k, i][:, c0 : c0 + P],
-                    rhs=rc[c][:].bitcast(FP8X4),
-                    rhs_scale=rs[c][:],
+                    out=h_bank[k, i, t][:],
+                    lhsT=z_codes[k, i][:, x0 : x0 + P].bitcast(FP8X4),
+                    lhsT_scale=z_scales[k, i][:, x0 : x0 + P],
+                    rhs=renv_codes[c][:].bitcast(FP8X4),
+                    rhs_scale=renv_scales[c][:],
                     start=(c == 0),
                     stop=(c == NC - 1),
                 )
 
-        def ep_u(k, i, t):
-            ut[k, i, t] = work.tile([P, 512], F32, name="u", tag="u", bufs=4)
+        def residual(k, i, t):
+            minus_u[k, i, t] = work.tile([P, 512], F32, name="minus_u", tag="minus_u", bufs=4)
             nc.vector.scalar_tensor_tensor(
-                out=ut[k, i, t][:],
-                in0=hbank[k, i, t][:],
+                out=minus_u[k, i, t][:],
+                in0=h_bank[k, i, t][:],
                 scalar=-1.0,
-                in1=psin[k, t][:, i, :],
+                in1=psi_ap[k, t][:, i, :],
                 op0=ALU.mult,
                 op1=ALU.subtract,
             )
 
-        def ep_q(k, i, t, eng):
-            qt[k, i, t] = work.tile([P, 512], F32, name="q", tag="q", bufs=8) if k == 0 else rd[t, i]
-            e = nc.gpsimd if eng == "g" else nc.vector
-            e.tensor_tensor(out=qt[k, i, t][:], in0=ut[k, i, t][:], in1=rd[t, i][:], op=ALU.mult)
+        def precondition(k, i, t, engine):
+            q_tile[k, i, t] = inverse[t, i] if k else work.tile([P, 512], F32, name="q", tag="q", bufs=8)
+            e = nc.vector if engine == "vector" else nc.gpsimd
+            e.tensor_tensor(out=q_tile[k, i, t][:], in0=minus_u[k, i, t][:], in1=inverse[t, i][:], op=ALU.mult)
 
-        def ep_p(k, i, t):
-            pq[k, i, t] = work.tile([P, 512], F32, name="pq", tag="pq", bufs=2)
+        def overlap_product(k, i, t):
+            psi_q[k, i, t] = work.tile([P, 512], F32, name="psi_q", tag="psi_q", bufs=2)
             nc.gpsimd.tensor_tensor(
-                out=pq[k, i, t][:], in0=qt[k, i, t][:], in1=psin[k, t][:, i, :], op=ALU.mult
+                out=psi_q[k, i, t][:], in0=q_tile[k, i, t][:], in1=psi_ap[k, t][:, i, :], op=ALU.mult
             )
 
-        def ep_sum(k, i, t):
-            j = t * NT + i
+        def overlap_sum(k, i, t):
+            j = t * TILES + i
             nc.scalar.activation(
-                pq[k, i, t][:], pq[k, i, t][:], ACT.Copy, accum_out=stat[k][:, 0, j : j + 1]
+                psi_q[k, i, t][:], psi_q[k, i, t][:], ACT.Copy, accum_out=sums[k][:, 0, j : j + 1]
             )
 
-        def ep_sum_v(k, i, t):
-            j = t * NT + i
+        def overlap_on_vector(k, i, t):
+            j = t * TILES + i
             nc.vector.scalar_tensor_tensor(
-                out=ut[k, i, t][:],
-                in0=qt[k, i, t][:],
+                out=minus_u[k, i, t][:],
+                in0=q_tile[k, i, t][:],
                 scalar=1.0,
-                in1=psin[k, t][:, i, :],
+                in1=psi_ap[k, t][:, i, :],
                 op0=ALU.mult,
                 op1=ALU.mult,
-                accum_out=stat[k][:, 0, j : j + 1],
+                accum_out=sums[k][:, 0, j : j + 1],
             )
 
-        snum, sbank = {}, {}
-
-        def overlap_v1(k):
-            snum[k] = keep.tile([P, 1], F32, name="snum%d" % k)
-            nc.vector.tensor_reduce(out=snum[k][:], in_=stat[k][:, 0, :], axis=AX.X, op=ALU.add)
-
-        def overlap_pe(k):
-            sbank[k] = bank("t")
-            nc.tensor.matmul(sbank[k][:, 0:1], sones[k][:], snum[k][:], start=True, stop=True)
-
-        def overlap_v2(k):
-            nc.vector.tensor_copy(out=nov[k][:], in_=sbank[k][:, 0:1])
-
-        cor, cb, ost, xt, oc, osc = {}, {}, {}, {}, {}, {}
+        partial, ov_bank, minus_ov = {}, {}, {}
+        corr, corr_bf, turn_bank, plane_stage, plane_codes, plane_scales = {}, {}, {}, {}, {}, {}
         for k in range(NK):
-            osc[k] = keep.tile([P, 1024], U8, name="osc%d" % k, align_bytes=64)
+            plane_scales[k] = keep.tile([P, NS * D], U8, name="plane_scales%d" % k, align_bytes=64)
 
-        def c_corr(k, t, i, engine):
-            cor[k, t, i] = work.tile([P, 512], F32, name="cor", tag="cor", bufs=4)
-            c = cor[k, t, i]
-            if engine == "g":
-                nc.gpsimd.tensor_scalar(c[:], psin[k, t][:, i, :], nov[k][:, 0:1], 0.0, ALU.mult, ALU.add)
-                nc.gpsimd.tensor_tensor(out=c[:], in0=c[:], in1=qt[k, i, t][:], op=ALU.add)
-            else:
-                nc.vector.scalar_tensor_tensor(
-                    out=c[:],
-                    in0=psin[k, t][:, i, :],
-                    scalar=nov[k][:, 0:1],
-                    in1=qt[k, i, t][:],
-                    op0=ALU.mult,
-                    op1=ALU.add,
-                )
-            nc.sync.dma_start(out=out_0[k, t, P * i : P * (i + 1), :], in_=cor[k, t, i][:])
+        def overlap_partial(k):
+            partial[k] = keep.tile([P, 1], F32, name="partial%d" % k)
+            nc.vector.tensor_reduce(out=partial[k][:], in_=sums[k][:, 0, :], axis=AX.X, op=ALU.add)
 
-        def c_cast(k, t, i, engine):
-            cb[k, t, i] = work.tile([P, 512], BF16, name="cb", tag="cb", bufs=4)
-            dst = cb[k, t, i][:].rearrange("a (u w e) -> a u w e", u=2, e=2)
-            src = cor[k, t, i][:].rearrange("a (w u e) -> a u w e", u=2, e=2)
-            if engine == "s":
-                nc.scalar.copy(out=dst, in_=src)
-            elif engine == "g":
-                nc.gpsimd.tensor_copy(out=dst, in_=src)
-            else:
-                nc.vector.tensor_copy(out=dst, in_=src)
+        def overlap_total(k):
+            ov_bank[k] = bank("turn")
+            nc.tensor.matmul(ov_bank[k][:, 0:1], scaled_ones[k][:], partial[k][:], start=True, stop=True)
+            minus_ov[k] = ov_bank[k][:, 0:1]
 
-        def c_turn(k, t, i, tag):
-            if i % 2 == 0:
-                xt[k, t, i // 2] = bank(tag)
-            x = xt[k, t, i // 2]
-            words = cb[k, t, i][:].bitcast(F32)
-            for u in range(2):
-                c0 = (2 * (i % 2) + u) * P
-                nc.tensor.transpose(x[:, c0 : c0 + P], words[:, P * u : P * (u + 1)], ident[:])
+        def overlap_copy(k):
+            minus_ov[k] = keep.tile([P, 1], F32, name="minus_ov%d" % k)
+            nc.vector.tensor_copy(out=minus_ov[k][:], in_=ov_bank[k][:, 0:1])
 
-        def c_evac(k, t, h, eng):
-            if h == 0:
-                ost[k, t] = stage_tile("ost%d%d" % (k, t))
-            dst = ost[k, t][:].bitcast(F32).rearrange("p (i a u) -> p i a u", i=NT, u=2)[:, 2 * h : 2 * h + 2]
-            src = xt[k, t, h][:].rearrange("p (i u a) -> p i a u", i=2, u=2)
-            if eng == "s":
-                nc.scalar.copy(out=dst, in_=src)
-            else:
-                nc.vector.tensor_copy(out=dst, in_=src)
-
-        def c_quant(k, t, h0, h1):
-            if h0 == 0:
-                oc[k, t] = work.tile([P, 512], U32, name="oc", tag="oc", bufs=2, align_bytes=64)
-            quant(
-                oc[k, t][:, 256 * h0 : 256 * h1],
-                osc[k][:, 512 * t + 256 * h0 : 512 * t + 256 * h1],
-                ost[k, t][:, 1024 * h0 : 1024 * h1],
+        def correct(k, t, i):
+            corr[k, t, i] = work.tile([P, 512], F32, name="corr", tag="corr", bufs=4)
+            nc.vector.scalar_tensor_tensor(
+                out=corr[k, t, i][:],
+                in0=psi_ap[k, t][:, i, :],
+                scalar=minus_ov[k][:, 0:1],
+                in1=q_tile[k, i, t][:],
+                op0=ALU.mult,
+                op1=ALU.add,
             )
-            if h1 == 2:
-                m0 = k * 1024 + t * 512
-                words = out_1.rearrange("g p m t -> (g p) (m t)")[:, 4 * m0 : 4 * (m0 + 512)]
-                nc.sync.dma_start(out=words.bitcast(I32), in_=oc[k, t][:].bitcast(I32))
+            nc.sync.dma_start(out=out_0[k, t, P * i : P * (i + 1), :], in_=corr[k, t, i][:])
 
-        def c_scales(k):
-            rows = out_2.rearrange("g q m -> (g q) m")
-            for q in range(4):
+        def round_corr(k, t, i):
+            corr_bf[k, t, i] = work.tile([P, 512], BF16, name="corr_bf", tag="corr_bf", bufs=4)
+            nc.scalar.copy(
+                out=corr_bf[k, t, i][:].rearrange("a (u q v) -> a u q v", u=2, v=2),
+                in_=corr[k, t, i][:].rearrange("a (q u v) -> a u q v", u=2, v=2),
+            )
+
+        def turn_pair(k, t, pair, tag):
+            turn_bank[k, t, pair] = bank(tag)
+            for x in range(4):
+                i, u = 2 * pair + x // 2, x % 2
+                nc.tensor.transpose(
+                    turn_bank[k, t, pair][:, P * x : P * (x + 1)],
+                    corr_bf[k, t, i][:].bitcast(F32)[:, P * u : P * (u + 1)],
+                    ident[:],
+                )
+
+        def plane_copy(k, t, pair, engine):
+            if pair == 0:
+                plane_stage[k, t] = stage_tile("plane_stage%d%d" % (k, t))
+            words = plane_stage[k, t][:].bitcast(F32).rearrange("q (i a u) -> q i a u", i=TILES, u=2)
+            out = words[:, 2 * pair : 2 * pair + 2]
+            turned = turn_bank[k, t, pair][:].rearrange("q (i u a) -> q i a u", i=2, u=2)
+            if engine == "scalar":
+                nc.scalar.copy(out=out, in_=turned)
+            else:
+                nc.vector.tensor_copy(out=out, in_=turned)
+
+        def plane_quantise(k, t, pair_0, pair_1):
+            if pair_0 == 0:
+                plane_codes[k, t] = work.tile([P, D], U32, name="plane_codes", tag="plane_codes", bufs=2, align_bytes=64)
+            x0, x1 = 256 * pair_0, 256 * pair_1
+            quantise(
+                plane_codes[k, t][:, x0:x1],
+                plane_scales[k][:, D * t + x0 : D * t + x1],
+                plane_stage[k, t][:, 4 * x0 : 4 * x1],
+            )
+            if pair_1 == 2:
+                m0 = (NS * k + t) * D
+                words = out_1.rearrange("g q m e -> (g q) (m e)")[:, 4 * m0 : 4 * (m0 + D)]
+                nc.sync.dma_start(out=words.bitcast(I32), in_=plane_codes[k, t][:].bitcast(I32))
+
+        def store_scales(k):
+            rows = out_2.rearrange("g x m -> (g x) m")
+            for x in range(4):
                 nc.sync.dma_start(
-                    out=rows[4 * q : 4 * q + 4, 1024 * k : 1024 * (k + 1)].bitcast(I32),
-                    in_=osc[k][32 * q : 32 * q + 4, :].bitcast(I32),
+                    out=rows[4 * x : 4 * x + 4, NS * D * k : NS * D * (k + 1)].bitcast(I32),
+                    in_=plane_scales[k][32 * x : 32 * x + 4, :].bitcast(I32),
                 )
 
-        small_constants_0()
-        v_part(0, 0, 0, 4, "v")
-        small_constants()
-        v_quant(0, 0)
-        v_part(0, 1, 0, 4, "v")
-        lenv_pe(1)
-        lenv_evac(1)
-        small_constants_2()
-        lenv_quant(1, 0, 128)
-        lenv_quant(1, 128, 192)
-        v_quant(0, 1)
-        lenv_quant(1, 192, 704)
-        lenv_quant(1, 704, 768)
-        nc.gpsimd.memset(ones[:], 1.0)
-        lenv_pe(0)
-        lenv0_evac()
-        quant(lc0[:], ls0[:], lst[0][:])
-        lenv0_pair()
-        later_loads()
+        lenv_zeros(1)
+        zero_first_columns(1)
+        make_selectors()
+        nc.vector.tensor_copy(out=gl_f[:], in_=gl_in[:])
+        v_on_scalar(0, 1)
+        v_on_vector(0, 0)
+        spread_w()
+        v_quantise(0, 0)
+        lenv_turn(1)
+        lenv_copy(1)
+        make_mixer()
+        v_interleave(0, 1)
+        lenv_quantise(1, 0, 2)
+        v_quantise(0, 1)
+        lenv_quantise(1, 2, 4)
+        lenv_quantise(1, 4, STRIPS)
+        nc.gpsimd.memset(minus_ones[:], -1.0)
+        for i in (0, 2, 3):
+            zero_first_columns(i)
+        lenv_turn(0)
+        lenv0_copy()
+        quantise(lenv0_codes[:], lenv0_scales[:], lenv_stage[0][:])
+        load_second_part()
 
-        waiting = {"pe": [], "s0": [], "s": [], "g0": [], "g": [], "v0": [], "v": []}
-        state = {"round": 0, "h": True, "f": 0, "em": 0, "final": 0, "turned": 0, "t": True, "r": 0, "v": 0, "tail": False}
-        hq = []
+        tasks, index = [], {}
 
-        def push(engine, delay, cost, fn, *args):
-            waiting[engine].append((state["round"] + delay, cost, fn, args))
+        def task(name, engine, number, length, after, fn, *args, earliest=0):
+            index[name] = len(tasks)
+            tasks.append((name, engine, number, length, [x for x in after if x is not None], earliest, fn, args))
 
-        def drain(engine, budget):
-            for item in list(waiting[engine]):
-                if budget <= 0:
-                    break
-                if item[0] <= state["round"] and item[2](*item[3]) != "wait":
-                    waiting[engine].remove(item)
-                    budget -= item[1]
-            return budget
+        def before(kind, x, back):
+            return (kind, x - back) if x >= back else None
 
-        def stage_end(k, i):
-            z_tiles(k, i)
-            z_quant(k, i, 0, 1024)
-            push("pe", LAG_M3, 1, product_request, k, i)
+        last_strip = {}
+        for n, (k, i, j) in enumerate(strips):
+            last_strip[k, i] = n
+        n_last = len(strips) - 1
 
-        def product_request(k, i):
-            hq.extend([(k, i, 0), (k, i, 1)])
+        for i, number in ((2, 3), (3, 6)):
+            second = i == 3
+            task(("lenv zeros", i), "gpsimd", number, 900, [("z", 0), ("lenv quantise", 2)] if second else [], lenv_zeros, i)
+            task(
+                ("lenv turn", i), "tensor", number, 930, [("lenv copy", 2)] if second else [], lenv_turn, i,
+                earliest=13000 if second else 0,
+            )
+            task(("lenv copy", i), "scalar", number, 1000, [("lenv turn", i), ("lenv zeros", i)], lenv_copy, i)
+            task(("lenv quantise", i), "vector", number + 1, 930, [("lenv copy", i)], lenv_quantise, i, 0, STRIPS)
+        task("lenv 0 strips", "gpsimd", 4, 700, [], lenv0_strips_copy)
+        task(("lenv quantise", 0), "vector", 6, 260, ["lenv 0 strips"], lenv0_strips_quantise)
 
-        def product():
-            if hq and state["h"] and state["r"] == NC:
-                k, i, t = hq.pop(0)
-                m3(k, i, t, "h")
-                state["h"] = False
-                push("v", LAG_U, 450, u_and_more, k, i, t)
-
-        free = {"u": 3, "pq": 2, "cb": 4, "part": 2}
-
-        def u_and_more(k, i, t):
-            if free["u"] == 0:
-                return "wait"
-            ep_u(k, i, t)
-            state["h"] = True
-            if state["tail"]:
-                ep_q(k, i, t, "v")
-                ep_sum_v(k, i, t)
-                return
-            free["u"] -= 1
-            push("g", LAG_Q, 960, q_and_more, k, i, t)
-
-        def q_and_more(k, i, t):
-            ep_q(k, i, t, "g")
-            free["u"] += 1
-            push("g", 0, 960, p_and_more, k, i, t)
-
-        def p_and_more(k, i, t):
-            if free["pq"] == 0:
-                return "wait"
-            free["pq"] -= 1
-            ep_p(k, i, t)
-            push("s", LAG_SUM, 450, sum_and_more, k, i, t)
-
-        done = {0: 0, 1: 0}
-
-        def sum_and_more(k, i, t):
-            ep_sum(k, i, t)
-            free["pq"] += 1
-            done[k] += 1
-            if k == 0 and done[0] == NG:
-                push("v", 2, 100, overlap_a)
-
-        def overlap_a():
-            overlap_v1(0)
-            push("pe", 1, 50, overlap_b)
-
-        def overlap_b():
-            if not state["t"]:
-                return "wait"
-            state["t"] = False
-            overlap_pe(0)
-            push("v", 0, 300, overlap_c)
-
-        def overlap_c():
-            overlap_v2(0)
-            state["t"] = True
-            for x in range(NG):
-                push(CORR[0], 1 + x, CORR[1], corr_and_more, x)
-
-        def corr_and_more(x):
-            t, i = divmod(x, NT)
-            c_corr(0, t, i, CORR[0])
-            push(CAST[0], LAG_CAST, CAST[1], cast_and_more, t, i)
-
-        def cast_and_more(t, i):
-            if NT // 2 * t + i // 2 > state["turned"] + 1:
-                return "wait"
-            c_cast(0, t, i, CAST[0])
-            if i % 2 == 1:
-                push("pe", LAG_TURN, 420, turn_and_more, t, i // 2)
-
-        def turn_and_more(t, h):
-            if not state["t"]:
-                return "wait"
-            c_turn(0, t, 2 * h, "t")
-            c_turn(0, t, 2 * h + 1, "t")
-            state["turned"] += 1
-            c_evac(0, t, h, "s")
-            if h == 1:
-                push("v", 2, 470, c_quant, 0, t, 0, 2)
-                if t == 1:
-                    push("v", 3, 50, c_scales, 0)
-
-        fmas = [(k, q, g) for k in range(NK) for q in range(NB * NS) for g in range(NG)]
-        ems = [(k, q) for k in range(NK) for q in range(NB * NS)]
-
-        def em_ahead():
-            at = state["f"] // NG
-            into = state["f"] % NG
-            allowed = at + (2 if into >= EM_AT or at % NG == 0 else 1)
-            if (
-                state["round"] >= EM_FROM
-                and state["em"] < min(len(ems), allowed)
-                and (ems[state["em"]][0] == 0 or state["v"] == NS)
-            ):
-                em(*ems[state["em"]])
-                state["em"] += 1
-
-        def fma_next():
-            k, q, g = fmas[state["f"]]
-            if NB * NS * k + q >= state["em"] or (
-                q == 0 and k == 1 and (0, g) not in finals
-            ):
-                return False
-            if 0 < q < SG_INPUTS:
-                if free["part"] == 0:
-                    return False
-                free["part"] -= 1
-            part = fma(k, q, g)
-            if part is not None:
-                push("g0", 0, 860, part_end, k, g, part)
-            state["f"] += 1
-            if q == NB * NS - 1:
-                push(FINAL[g % 2][0] + "0", 1, 850, e_last, k, g, FINAL[g % 2])
-            return True
-
-        finals = set()
-
-        def part_end(k, g, part):
-            fma_add(k, g, part)
-            free["part"] += 1
-
-        def e_last(k, g, engine):
-            e_final(k, g, engine)
-            finals.add((k, g))
-            state["final"] += 1
-            if state["final"] == NG * (k + 1):
-                push("v", LAG_ZE, 900, stage_end, k, 0)
-
-        def rd_all(t, i):
-            push("s", 0, 450, rd_first, t, i)
-            push("s", 0, 450, rd_second, t, i)
-            push("s", 0, 450, rd_and_more, t, i)
-
-        def rd_and_more(t, i):
-            rd_third(t, i)
-            push("g", 2, 960, rd_g, t, i)
-
-        def prep(i):
-            if not (state["h"] and state["t"]):
-                return "wait"
-            lenv_pe(i)
-            lenv_evac(i)
-            push("v", 2, 480, lenv_quant, i, 0, 512)
-            push("v", 2, 250, lenv_quant, i, 512, 768)
-
-        def r_prep(c, eng):
-            for part in range(4):
-                push(eng, 0, 520, r_part, c, part, eng)
-
-        def r_part(c, part, eng):
-            r_copy(c, part, eng)
-            if part == 3:
-                push("v", LAG_R, 470, r_end, c)
-
-        def r_end(c):
-            r_quant(c)
-            state["r"] += 1
-
-        def v_prep(s):
-            for t in range(4):
-                push("g", 0, 960, v_next, s, t)
-
-        def v_next(s, t):
-            v_part(1, s, t, t + 1, "g")
-            if t == 3:
-                push("v", 2, 470, v_end, s)
-
-        def v_end(s):
-            v_quant(1, s)
-            state["v"] += 1
-
-        def square_and_more(k, t, i):
-            psi_square(k, t, i)
-            if (t, i) == (NS - 1, NT - 1):
-                push("v", 3, 100, norm_all, k)
-
-        def norm_all(k):
-            norm_a(k)
-            push("pe", 1, 50, norm_pe, k)
-
-        def norm_pe(k):
-            if not state["t"]:
-                return "wait"
-            state["t"] = False
-            norm_b(k)
-            push("v", 0, 200, norm_end, k)
-
-        def norm_end(k):
-            norm_c(k)
-            state["t"] = True
-
-        ready = {}
-
-        def at(step, fn, *args):
-            ready.setdefault(step, []).append((fn, args))
-
-        at(3, push, "v", 0, 230, lenv0_quant)
-        at(PREP_AT[0], push, "pe", 0, 840, prep, 2)
         for c in range(NC):
-            at(R_AT[c], r_prep, c, R_ENG[c])
-        at(3, more_loads)
-        at(LAST_AT, last_loads)
-        at(PREP_AT[1], push, "pe", 0, 840, prep, 3)
-        for x, (t, i) in enumerate([(0, 1), (1, 1), (0, 2), (1, 2), (0, 3), (1, 3), (0, 0), (1, 0)]):
-            at((10, 11, 14, 15, 18, 19, 20, 21)[x], rd_all, t, i)
-        at(V_AT, v_prep, 0)
-        at(V_AT, v_prep, 1)
-        for k in range(NK):
-            for t in range(NS):
-                for i in range(NT):
-                    at(SQ[k] + t * NT + i, push, "s", 0, 450, square_and_more, k, t, i)
+            engine = "scalar" if c == 1 else "gpsimd"
+            for part in range(4):
+                row = ("renv part", c, part - 1) if part else ("renv part", c - 1, 0) if c else None
+                task(
+                    ("renv part", c, part), engine, 3 + c, 560, [row, "lenv 0 strips" if c == 3 else None],
+                    renv_interleave, c, part, engine, earliest=8000 + 1000 * c,
+                )
+            task(("renv quantise", c), "vector", 5 + c, 490, [("renv part", c, 3)], renv_quantise, c)
 
-        pair_of = {n: x for x, m in enumerate(members) for n in m}
-        m1(0)
-        e1(0, 0)
-        e1(0, 1)
-        issued, half = 1, []
-        for n in range(nblocks):
-            state["round"] = n
-            x = pair_of[n]
-            if x >= issued:
-                m1(x)
-                e1(x, 0)
-                e1(x, 1)
-                issued += 1
-            product()
-            em_ahead()
-            for fn, args in ready.pop(n, []):
-                fn(*args)
-            drain("pe", 500)
-            m2(n)
-            for y in half:
-                e1(y, 1)
-            half = []
-            if issued < len(pairs) and issued <= x + AHEAD:
-                m1(issued)
-                e1(issued, 0)
-                half = [issued]
-                issued += 1
-            sb = S_BUDGET
-            while sb > 0 and state["f"] < len(fmas) and fmas[state["f"]][1] < SG_INPUTS and fma_next():
-                sb -= 450
-            drain("s", drain("s0", sb))
-            left = V_BUDGET
-            if n > 0:
-                e2(n - 1)
-                left -= 450
-                k, i, j = blocks[n - 1]
-                if i > 0 and last_of[k, i] == n - 1 and (k, i) != (1, 3):
-                    push("v", 0, 900, stage_end, k, i)
-            left = drain("v", drain("v0", left))
-            while (
-                left > 0
-                and state["f"] < min(len(fmas), int(PACE * (n - 1)) + NG)
-                and fmas[state["f"]][1] >= SG_INPUTS
-                and fma_next()
-            ):
-                left -= 380
-            drain("g", drain("g0", G_BUDGET))
-        assert state["f"] == len(fmas), state["f"]
-        state["round"], state["tail"] = nblocks + 20, True
-        e2(nblocks - 1)
-        z_tiles(1, 3)
-        z_quant(1, 3, 0, 512)
-        z_quant(1, 3, 512, 1024)
-        drain("pe", 2)
-        rest = hq + [(1, 3, 0), (1, 3, 1)]
-        assert len(rest) < 5
-        for x, (k, i, t) in enumerate(rest):
-            m3(k, i, t, "yyzz"[x + 4 - len(rest)])
-        drain("v0", 9999)
-        for item in list(waiting["v"]):
-            if item[2] == u_and_more:
-                waiting["v"].remove(item)
-                item[2](*item[3])
-        for k, i, t in rest:
-            ep_u(k, i, t)
-            ep_q(k, i, t, "v")
-            ep_sum_v(k, i, t)
-        for n in range(8):
-            state["round"] += 10
-            for engine in ("pe", "s0", "g0", "g", "s"):
-                drain(engine, 9999)
-        overlap_v1(1)
-        overlap_pe(1)
-        overlap_v2(1)
-        order = [(t, i) for t in range(NS) for i in range(NT)]
-        for x, (t, i) in enumerate(order):
-            c_corr(1, t, i, "v")
-            c_cast(1, t, i, TAIL_CAST[x])
-            c_turn(1, t, i, "ez"[t])
-            if x == 4:
-                c_evac(1, 0, 0, "s")
-        state["round"] += 10
-        drain("v", 9999)
-        drain("v", 9999)
-        c_evac(1, 0, 1, "v")
-        c_evac(1, 1, 0, "s")
-        c_quant(1, 0, 0, 2)
-        c_evac(1, 1, 1, "v")
-        c_quant(1, 1, 0, 1)
-        c_quant(1, 1, 1, 2)
-        c_scales(1)
-        assert not any(waiting.values()) and not ready, waiting
+        task("third loads", "sync", 0, 100, [("lenv turn", 2), ("renv part", 0, 3)], load_third_part)
+        for s in range(NS):
+            for e in range(4):
+                row = ("v part", s, e - 1) if e else ("v part", 0, 3) if s else ("renv quantise", 3)
+                task(
+                    ("v part", s, e), "gpsimd", 12 + 2 * s, 990, [row, ("renv quantise", s), "third loads"],
+                    v_on_gpsimd, 1, s, e, earliest=19000,
+                )
+            task(("v quantise", s), "vector", 15 + 2 * s, 490, [("v part", s, 3)], v_quantise, 1, s)
+        second_v = [("v quantise", s) for s in range(NS)]
+
+        for x, i in enumerate((1, 2, 3, 0)):
+            for t in range(NS):
+                number = 7 + 2 * (2 * x + t)
+                task(("root", t, i), "scalar", number, 460, [], inverse_root, t, i, earliest=14000)
+                task(("sign", t, i), "scalar", number, 460, [("root", t, i)], inverse_sign, t, i)
+                task(("square", t, i), "scalar", number, 460, [("sign", t, i)], inverse_square, t, i)
+                task(("inverse", t, i), "gpsimd", number + 1, 980, [("square", t, i)], inverse_join, t, i)
+
+        for k in range(NK):
+            number = (20, 30)[k]
+            for x in range(NG):
+                t, i = divmod(x, TILES)
+                task(("psi^2", k, x), "scalar", number + x, 500, [], psi_square, k, t, i, earliest=16000 + 6000 * k)
+            bank_free = ("plane copy", 3) if k else ("lenv copy", 3)
+            task(("norm partial", k), "vector", number + 10, 60, [("psi^2", k, x) for x in range(NG)], norm_partial, k)
+            task(("norm total", k), "tensor", number + 10, 100, [("norm partial", k), bank_free], norm_total, k)
+            task(("norm inverse", k), "vector", number + 10, 70, [("norm total", k)], norm_inverse, k)
+            task(("norm spread", k), "scalar", number + 11, 150, [("norm inverse", k)], norm_spread, k)
+
+        z_stage_free = {
+            (0, 1): [("lenv zeros", 2)],
+            (0, 2): [("z codes", 0, 1), ("lenv zeros", 3)],
+            (0, 3): [("lenv quantise", 3)],
+            (1, 1): [("z codes", 0, 2)],
+            (1, 2): [("z codes", 0, 3)],
+            (1, 0): [("z codes", 0, 0)],
+            (1, 3): [("z codes", 1, 1)],
+        }
+        for n, (k, i, j) in enumerate(strips):
+            inputs = ([("lenv quantise", i)] if i != 1 else []) + (second_v if k else [])
+            task(("y", n), "tensor", n - 1.5, 480, [before("y copy", n, 2)] + inputs, strip_y, n)
+            task(("y copy", n), "scalar", n - 5, 460, [("y", n), before("mix", n, 4)], strip_copy, n)
+            task(("mix", n), "tensor", n, 892, [("y copy", n), before("z", n, 2)], strip_mix, n)
+            room = z_stage_free.get((k, i), []) if n == 0 or strips[n - 1][:2] != (k, i) else []
+            task(("z", n), "vector", n - 1, 460, [("mix", n), before("z", n, 1)] + room, strip_z, n)
+
+        for f in range(NK * NG * NG):
+            x, g = divmod(f, NG)
+            k, n = divmod(x, NG)
+            number = 1 + f / 3
+            columns = 64 * V_STRIPS[k]
+            if g == 0:
+                bank_free = [("add", x - 2, y) for y in range(NG)] if x > 1 else []
+                task(("input", x), "tensor", number - 1, 290, bank_free + (second_v if k else []), input_y, k, n)
+            row = ("add", x - 1, g) if n else ("finish", 0, g) if k else None
+            task(
+                ("add", x, g), "vector" if n else "scalar", number, 0.84 * columns + 25, [("input", x), row],
+                add_input, k, n, g,
+            )
+            if n == NG - 1:
+                engine = "gpsimd" if g % 2 else "scalar"
+                length = 110 + 1.68 * columns if g % 2 else 400 + columns
+                room = ("z codes", 0, 0) if k else None
+                task(("finish", k, g), engine, number + 1, length, [("add", x, g), room], finish_output, k, g, engine)
+
+        order = [(0, 1), (0, 2), (0, 3), (0, 0), (1, 1), (1, 2), (1, 0), (1, 3)]
+        for m, (k, i) in enumerate(order):
+            last = m == len(order) - 1
+            number = last_strip[k, i] if i else last_strip[k, 3] + (2, -6)[k]
+            ready = [("z", n) for n, strip in enumerate(strips) if strip[:2] == (k, i)]
+            ready += [] if i else [("finish", k, g) for g in range(NG)]
+            ready += [("z codes",) + order[m - 1]] if m else []
+            ready += [("h", 2 * (m - 2)), ("h", 2 * (m - 2) + 1)] if m > 1 else []
+            if last:
+                task(("z codes", k, i), "vector", number, 10, ready, z_code_tiles, k, i)
+            else:
+                task(("z codes", k, i), "vector", number, 940, ready, z_quantise_tile, k, i)
+            for t in range(NS):
+                x, at = 2 * m + t, number + 1 + 1.5 * t
+                codes, bank_free = ("z codes", k, i), before("residual", x, 1) or ("lenv copy", 3)
+                if last:
+                    codes, bank_free = ("z half", t), ("y copy", n_last)
+                    half = NG * P // 2
+                    task(codes, "vector", number, 480, [("z codes", k, i)], z_quantise, k, i, half * t, half * (t + 1))
+                all_renv = [("renv quantise", c) for c in range(NC)] if m == 0 else []
+                task(("h", x), "tensor", at - 2, 920, [codes, bank_free] + all_renv, h_product, k, i, t, "y" if last else "h")
+                task(
+                    ("residual", x), "vector", at + 1, 460,
+                    [("h", x), before("residual", x, 1), before("precondition", x, 4)], residual, k, i, t,
+                )
+                engine = "vector" if last else "gpsimd"
+                task(
+                    ("precondition", x), engine, at + 2, 460 if last else 980,
+                    [("residual", x), ("inverse", t, i), before("precondition", x, 1)], precondition, k, i, t, engine,
+                )
+                if last:
+                    task(("overlap", x), "vector", at + 2, 520, [("precondition", x)], overlap_on_vector, k, i, t)
+                else:
+                    task(
+                        ("product", x), "gpsimd", at + 2, 980,
+                        [("precondition", x), before("product", x, 1), before("overlap", x, 2)], overlap_product, k, i, t,
+                    )
+                    task(("overlap", x), "scalar", at + 3, 500, [("product", x)], overlap_sum, k, i, t)
+
+        for k in range(NK):
+            number = n_last + 3 if k else last_strip[0, 3] + 8
+            known = [("overlap", NG * k + x) for x in range(NG)]
+            task(("overlap partial", k), "vector", number, 60, known, overlap_partial, k)
+            task(("overlap total", k), "tensor", number, 100, [("overlap partial", k), ("norm spread", k)], overlap_total, k)
+            if k == 0:
+                task("overlap copy", "vector", number, 60, [("overlap total", 0)], overlap_copy, 0)
+            for y in range(NG):
+                x, (t, i) = NG * k + y, divmod(y, TILES)
+                at = number + 1 + (1.5, 0.3)[k] * y
+                known = ("overlap total", 1) if k else "overlap copy"
+                task(
+                    ("correct", x), "vector", at, 460, [known, before("correct", x, 1), before("round", x, 4)],
+                    correct, k, t, i,
+                )
+                task(
+                    ("round", x), "scalar", at + 1, 460,
+                    [("correct", x), before("round", x, 1), before("turn", x // 2, 2)], round_corr, k, t, i,
+                )
+                if y % 2 == 0:
+                    continue
+                w, pair = x // 2, i // 2
+                if k:
+                    bank_free = [("z", n_last)] + [("add", 2 * NG - 1, g) for g in range(NG)]
+                else:
+                    bank_free = [before("plane copy", w, 1), "overlap copy", ("norm inverse", 0)]
+                task(
+                    ("turn", w), "tensor", at - 19 if k else at + 1, 500,
+                    [("round", x), ("round", x - 1), before("turn", w, 1)] + bank_free,
+                    turn_pair, k, t, pair, ("e", "z")[t] if k else "turn",
+                )
+                engine = "vector" if k and y != 3 else "scalar"
+                task(("plane copy", w), engine, at + 4 if k else at + 1, 450, [("turn", w)], plane_copy, k, t, pair, engine)
+            for t in range(NS):
+                w, at = NG // 2 * k + 2 * t, number + 6 + 5 * t
+                copies = [("plane copy", w), ("plane copy", w + 1)]
+                if k == 0:
+                    task(("planes", k, t), "vector", at, 490, copies, plane_quantise, k, t, 0, 2)
+                else:
+                    task(("half plane", t), "vector", at, 250, copies[:1] + [("planes", 0, t)], plane_quantise, k, t, 0, 1)
+                    task(("planes", k, t), "vector", at, 250, copies[1:] + [("half plane", t)], plane_quantise, k, t, 1, 2)
+            task(("scales", k), "sync", number + 12, 50, [("planes", k, t) for t in range(NS)], store_scales, k)
+
+        followers = [[] for x in tasks]
+        missing = [len(entry[4]) for entry in tasks]
+        for x, entry in enumerate(tasks):
+            for name in entry[4]:
+                followers[index[name]].append(x)
+        two_ports = (
+            "z codes", "z half", "lenv quantise", "renv quantise", "v quantise", "planes", "half plane",
+            "precondition", "overlap", "correct",
+        )
+
+        def takes_turns(x):
+            name, engine = tasks[x][0], tasks[x][1]
+            kind = name if isinstance(name, str) else name[0]
+            return engine == "gpsimd" and kind != "lenv zeros" or engine == "vector" and kind in two_ports
+
+        START, HOP, SAME_ENGINE, SCALAR_EXTRA = 7600, 260, 110, 80
+        clock = {"tensor": START, "scalar": START, "vector": START + 1000, "gpsimd": START, "sync": START, "turns": 0}
+        can_start = [max(START, entry[5]) for entry in tasks]
+        open_tasks = [x for x in range(len(tasks)) if missing[x] == 0]
+        plan = []
+        while open_tasks:
+            start, number, x = min(
+                (
+                    max(clock[tasks[x][1]], can_start[x], clock["turns"] if takes_turns(x) else 0),
+                    tasks[x][2],
+                    x,
+                )
+                for x in open_tasks
+            )
+            open_tasks.remove(x)
+            engine = tasks[x][1]
+            end = start + tasks[x][3] + (SCALAR_EXTRA if engine == "scalar" else 0)
+            clock[engine] = end
+            if takes_turns(x):
+                clock["turns"] = end
+            plan.append(x)
+            for y in followers[x]:
+                missing[y] -= 1
+                wait = HOP if tasks[y][1] != engine else 0 if engine == "tensor" else SAME_ENGINE
+                can_start[y] = max(can_start[y], end + wait)
+                if missing[y] == 0:
+                    open_tasks.append(y)
+        assert len(plan) == len(tasks)
+        for x in plan:
+            tasks[x][6](*tasks[x][7])

from contextlib import ExitStack

import concourse.mybir as mybir
from concourse.masks import make_identity

F32 = mybir.dt.float32
BF16 = mybir.dt.bfloat16
U32 = mybir.dt.uint32
I32 = mybir.dt.int32
U8 = mybir.dt.uint8
FP8X4 = mybir.dt.float8_e4m3fn_x4
ALU = mybir.AluOpType
ACT = mybir.ActivationFunctionType
AX = mybir.AxisListType

P = 128
NK, NS, NB, NC, D = 2, 2, 4, 4, 512
NG = NC * NS
TILES = D // P
STRIP = 16
STRIPS = P // STRIP
V_STRIPS = (7, 6)

FLOPS = 2 * 2 * 2048 * 2048 * 512 + 2 * 64 * 2 * 512 * 512


def tile_dmrgsinglesitempodavidsoncorrection_x1_kernel(
    tc, psi, gl, lenv, wmpo, gr, renv, d, out_0, out_1, out_2
):
    nc = tc.nc
    with ExitStack() as ctx:
        keep = ctx.enter_context(tc.tile_pool(name="keep", bufs=1))
        work = ctx.enter_context(tc.tile_pool(name="work", bufs=2))
        psum = ctx.enter_context(tc.psum_pool(name="psum", bufs=2))
        ctx.enter_context(tc.manual_schedule())

        banks_of = {"y": 2, "z": 2, "e": 2, "h": 1, "turn": 1}

        def bank(tag):
            return psum.tile([P, 512], F32, name="bank_" + tag, tag=tag, bufs=banks_of[tag])

        lenv_in, psi_lr, renv_in, d_in, psi_ap = {}, {}, {}, {}, {}

        def input_tile(name):
            return work.tile([P, 4, 512], BF16, name=name, tag="input", bufs=8, align_bytes=64)

        def load_lenv(i):
            lenv_in[i] = input_tile("lenv_in%d" % i)
            nc.sync.dma_start(
                out=lenv_in[i][:], in_=lenv[:, P * i : P * (i + 1), :].rearrange("b a l -> a b l")
            )

        def load_psi_lr(k, s):
            psi_lr[k, s] = input_tile("psi_lr%d%d" % (k, s))
            nc.sync.dma_start(out=psi_lr[k, s][:], in_=psi[k, s].rearrange("(q e) r -> q e r", e=4))

        def load_renv(c):
            renv_in[c] = input_tile("renv_in%d" % c)
            nc.sync.dma_start(out=renv_in[c][:], in_=renv[c].rearrange("(q e) p -> q e p", e=4))

        def load_psi_ap(k, t):
            psi_ap[k, t] = keep.tile([P, TILES, 512], BF16, name="psi_ap%d%d" % (k, t))
            nc.sync.dma_start(out=psi_ap[k, t][:], in_=psi[k, t].rearrange("(i a) p -> a i p", a=P))

        def load_d(t):
            d_in[t] = input_tile("d_in%d" % t)
            nc.sync.dma_start(out=d_in[t][:], in_=d[t].rearrange("(i a) p -> a i p", a=P))

        w_row = keep.tile([P, NG * NG], BF16, name="w_row")
        nc.vector.memset(w_row[:], 0.0)
        gl_in = keep.tile([P, 4], BF16, name="gl_in")
        nc.sync.dma_start(out=gl_in[:], in_=gl.rearrange("(q e) -> q e", e=4))
        load_psi_lr(0, 0)
        nc.sync.dma_start(out=w_row[0:1, :], in_=wmpo.rearrange("b s c t -> (b s c t)").unsqueeze(0))
        load_psi_lr(0, 1)
        load_lenv(1)
        gr_in = keep.tile([P, NC, 4], BF16, name="gr_in")
        nc.sync.dma_start(out=gr_in[:], in_=gr.rearrange("c (q e) -> q c e", e=4))
        load_lenv(0)
        load_lenv(2)
        load_renv(0)

        def load_second_part():
            for c in range(1, NC):
                load_renv(c)
            load_lenv(3)
            for t in range(NS):
                load_d(t)
                load_psi_ap(0, t)

        def load_third_part():
            for s in range(NS):
                load_psi_lr(1, s)
            for t in range(NS):
                load_psi_ap(1, t)

        ident = keep.tile([P, P], F32, name="ident")
        make_identity(nc, ident[:])
        one = keep.tile([P, 1], F32, name="one")
        nc.vector.memset(one[:], 1.0)
        table_load = keep.tile([P, 1], F32, name="table_load")
        nc.scalar.activation(table_load[:], one[:], ACT.Abs_reciprocal_sqrt)
        minus_ones = keep.tile([P, P], F32, name="minus_ones")
        ones = keep.tile([P, P], BF16, name="ones")
        nc.vector.memset(ones[:], 1.0)

        gl_f = keep.tile([P, 4], F32, name="gl_f")
        w_all = keep.tile([P, NG, NG], F32, name="w_all")
        same_a = keep.tile([P, STRIP], F32, name="same_a")
        same_sb = keep.tile([P, NG], F32, name="same_sb")
        w_pick = keep.tile([P, NG, NG], F32, name="w_pick")
        w_own = keep.tile([P, NG], F32, name="w_own")
        mixer = keep.tile([P, P], F32, name="mixer")
        gr_all = keep.tile([P, NG, 4], F32, name="gr_all")

        def make_selectors():
            split = ident[:].rearrange("x (sb a) -> x sb a", a=STRIP)
            nc.vector.tensor_reduce(
                out=same_a[:], in_=split.rearrange("x sb a -> x a sb"), axis=AX.X, op=ALU.add
            )
            nc.vector.tensor_reduce(out=same_sb[:], in_=split, axis=AX.X, op=ALU.add)

        def spread_w():
            spread = bank("e")
            nc.tensor.matmul(spread[:, 0 : NG * NG], ones[:], w_row[:], start=True, stop=True)
            nc.vector.tensor_copy(
                out=w_all[:].rearrange("x bs (t c) -> x bs t c", t=NS),
                in_=spread[:, 0 : NG * NG].rearrange("x (bs c t) -> x bs t c", bs=NG, t=NS),
            )

        def make_mixer():
            nc.vector.tensor_copy(
                out=gr_all[:].rearrange("q (t c) e -> q t (c e)", t=NS),
                in_=gr_in[:].rearrange("q c e -> q (c e)").unsqueeze(1).to_broadcast([P, NS, 4 * NC]),
            )
            nc.vector.tensor_tensor(
                out=w_pick[:].rearrange("x g (s b) -> x g s b", s=NS),
                in0=w_all[:].rearrange("x (b s) g -> x g s b", s=NS),
                in1=same_sb[:].rearrange("x (s b) -> x s b", s=NS).unsqueeze(1).to_broadcast([P, NG, NS, NB]),
                op=ALU.mult,
            )
            nc.vector.tensor_reduce(out=w_own[:], in_=w_pick[:], axis=AX.X, op=ALU.add)
            nc.vector.tensor_tensor(
                out=mixer[:].rearrange("x (g a) -> x g a", a=STRIP),
                in0=w_own[:].unsqueeze(2).to_broadcast([P, NG, STRIP]),
                in1=same_a[:].unsqueeze(1).to_broadcast([P, NG, STRIP]),
                op=ALU.mult,
            )

        def stage_tile(name):
            return work.tile([P, 2048], BF16, name=name, tag="stage", bufs=4, align_bytes=64)

        def quantise(codes, scales, values):
            nc.vector.quantize_mx(out=codes.bitcast(FP8X4), scales=scales, in_=values)

        HELD = (2, STRIPS, STRIPS, STRIPS)
        lenv_codes, lenv_scales, lenv_stage, lenv_banks = {}, {}, {}, {}
        for i in range(TILES):
            n = 64 + P * HELD[i]
            lenv_codes[i] = keep.tile([P, n], U32, name="lenv_codes%d" % i, align_bytes=64)
            lenv_scales[i] = keep.tile([P, n], U8, name="lenv_scales%d" % i, align_bytes=64)
        lenv0_codes = keep.tile([P, 512], U32, name="lenv0_codes", align_bytes=64)
        lenv0_scales = keep.tile([P, 512], U8, name="lenv0_scales", align_bytes=64)
        lenv0_strips = keep.tile([P, 2, 2, 256], BF16, name="lenv0_strips", align_bytes=64)

        def zero_first_columns(i):
            nc.gpsimd.memset(lenv_codes[i][:, 0:64], 0)
            nc.gpsimd.memset(lenv_scales[i][:, 0:64].bitcast(I32), 0)

        def zero_halves(values, strips):
            words = values.rearrange("q k z x -> q (k z x)").bitcast(U32)
            nc.gpsimd.memset(words.rearrange("q (k z x) -> q k z x", k=strips, z=2)[:, :, 1], 0)

        def lenv_zeros(i):
            lenv_stage[i] = work.tile(
                [P, STRIPS, 2, 256], BF16, name="lenv_stage%d" % i, tag="z_stage", bufs=2, align_bytes=64
            )
            zero_halves(lenv_stage[i][:], STRIPS)

        def lenv_turn(i):
            words = lenv_in[i][:].rearrange("a b l -> a (b l)").bitcast(F32)
            for half, tag in enumerate(("h", "turn")):
                lenv_banks[i, half] = bank(tag)
                for x in range(4):
                    b, u = 2 * half + x // 2, x % 2
                    nc.tensor.transpose(
                        lenv_banks[i, half][:, P * x : P * (x + 1)],
                        words[:, 256 * b + u : 256 * (b + 1) : 2],
                        ident[:],
                    )

        def lenv_bank(i, b):
            return lenv_banks[i, b // 2][:, 256 * (b % 2) : 256 * (b % 2 + 1)]

        def lenv_copy(i):
            words = lenv_stage[i][:].rearrange("q k z x -> q (k z x)").bitcast(F32)
            out = words.rearrange("q (k z b a u) -> q k z b a u", k=STRIPS, z=2, b=NB, a=STRIP)
            for b in range(NB):
                nc.scalar.copy(
                    out=out[:, :, 0, b], in_=lenv_bank(i, b).rearrange("q (u k a) -> q k a u", u=2, k=STRIPS)
                )

        def lenv_quantise(i, strip_0, strip_1):
            x0, x1 = 64 + P * strip_0, 64 + P * strip_1
            values = lenv_stage[i][:].rearrange("q k z x -> q (k z x)")
            quantise(lenv_codes[i][:, x0:x1], lenv_scales[i][:, x0:x1], values[:, 512 * strip_0 : 512 * strip_1])

        def lenv0_copy():
            lenv_stage[0] = stage_tile("lenv_stage0")
            out = lenv_stage[0][:].bitcast(F32).rearrange("q (b a u) -> q b a u", b=NB, a=P)
            for b in range(NB):
                nc.scalar.copy(out=out[:, b], in_=lenv_bank(0, b).rearrange("q (u a) -> q a u", u=2))

        def lenv0_strips_copy():
            zero_halves(lenv0_strips[:], 2)
            out = lenv0_strips[:].rearrange("q k z (b x) -> q k z b x", b=NB)[:, :, 0]
            values = lenv_stage[0][:].rearrange("q (b k x) -> q k b x", b=NB, k=STRIPS)
            nc.gpsimd.tensor_copy(out=out, in_=values[:, STRIPS - 2 :])

        def lenv0_strips_quantise():
            values = lenv0_strips[:].rearrange("q k z x -> q (k z x)")
            quantise(lenv_codes[0][:, 64 : 64 + 2 * P], lenv_scales[0][:, 64 : 64 + 2 * P], values)

        v_codes, v_scales, v_stage, scaled = {}, {}, {}, {}
        for k in range(NK):
            for s in range(NS):
                v_codes[k, s] = keep.tile([P, 512], U32, name="v_codes%d%d" % (k, s), align_bytes=64)
                v_scales[k, s] = keep.tile([P, 512], U8, name="v_scales%d%d" % (k, s), align_bytes=64)

        def v_out(k, s):
            return v_stage[k, s][:].rearrange("m (e q f) -> m e q f", e=4, f=4)

        def v_in(k, s):
            return psi_lr[k, s][:].rearrange("m f (q e) -> m e q f", e=4)

        def v_on_vector(k, s):
            v_stage[k, s] = stage_tile("v_stage%d%d" % (k, s))
            nc.vector.tensor_tensor(
                out=v_out(k, s),
                in0=v_in(k, s),
                in1=gl_in[:].unsqueeze(1).unsqueeze(1).to_broadcast([P, 4, P, 4]),
                op=ALU.mult,
            )

        def v_on_gpsimd(k, s, e):
            if e == 0:
                v_stage[k, s] = stage_tile("v_stage%d%d" % (k, s))
            nc.gpsimd.tensor_tensor(
                out=v_out(k, s)[:, e],
                in0=v_in(k, s)[:, e],
                in1=gl_in[:].unsqueeze(1).to_broadcast([P, P, 4]),
                op=ALU.mult,
            )

        def v_on_scalar(k, s):
            scaled[k, s] = stage_tile("scaled")
            for f in range(4):
                nc.scalar.activation(
                    scaled[k, s][:, 512 * f : 512 * (f + 1)], psi_lr[k, s][:, f, :], ACT.Copy, scale=gl_f[:, f : f + 1]
                )

        def v_interleave(k, s):
            v_stage[k, s] = stage_tile("v_stage%d%d" % (k, s))
            nc.vector.tensor_copy(
                out=v_out(k, s), in_=scaled[k, s][:].rearrange("m (f q e) -> m e q f", f=4, e=4)
            )

        def v_quantise(k, s):
            quantise(v_codes[k, s][:], v_scales[k, s][:], v_stage[k, s][:])

        renv_codes, renv_scales, renv_stage = {}, {}, {}
        for c in range(NC):
            renv_codes[c] = keep.tile([P, 512], U32, name="renv_codes%d" % c, align_bytes=64)
            renv_scales[c] = keep.tile([P, 512], U8, name="renv_scales%d" % c, align_bytes=64)

        def renv_interleave(c, part, engine):
            if part == 0:
                renv_stage[c] = stage_tile("renv_stage%d" % c)
            cols = slice(P * part, P * (part + 1))
            out = renv_stage[c][:].rearrange("q (p e) -> q p e", e=4)[:, cols]
            values = renv_in[c][:].rearrange("q e p -> q p e")[:, cols]
            if engine == "scalar":
                nc.scalar.copy(out=out, in_=values)
            else:
                nc.gpsimd.tensor_scalar(out, values, 1.0, 0.0, ALU.mult, ALU.add)

        def renv_quantise(c):
            quantise(renv_codes[c][:], renv_scales[c][:], renv_stage[c][:])

        inverse, sign = {}, {}
        for t in range(NS):
            for i in range(TILES):
                inverse[t, i] = keep.tile([P, 512], F32, name="inverse%d%d" % (t, i))

        def inverse_root(t, i):
            nc.scalar.activation(
                inverse[t, i][:], d_in[t][:, i, :], ACT.Abs_reciprocal_sqrt, bias=one[:, 0:1]
            )

        def inverse_sign(t, i):
            sign[t, i] = work.tile([P, 512], BF16, name="sign", tag="sign", bufs=8)
            nc.scalar.activation(sign[t, i][:], d_in[t][:, i, :], ACT.Sign, bias=one[:, 0:1])

        def inverse_square(t, i):
            nc.scalar.activation(inverse[t, i][:], inverse[t, i][:], ACT.Square)

        def inverse_join(t, i):
            nc.gpsimd.tensor_tensor(out=inverse[t, i][:], in0=inverse[t, i][:], in1=sign[t, i][:], op=ALU.mult)

        sums, norm, norm_bank, scaled_ones = {}, {}, {}, {}
        for k in range(NK):
            sums[k] = keep.tile([P, 2, NG], F32, name="sums%d" % k)
            norm[k] = keep.tile([P, 2], F32, name="norm%d" % k)
            scaled_ones[k] = keep.tile([P, P], F32, name="scaled_ones%d" % k)

        def psi_square(k, t, i):
            unused = work.tile([P, 512], BF16, name="unused", tag="unused", bufs=2)
            j = t * TILES + i
            nc.scalar.activation(unused[:], psi_ap[k, t][:, i, :], ACT.Square, accum_out=sums[k][:, 1, j : j + 1])

        def norm_partial(k):
            nc.vector.tensor_reduce(out=norm[k][:, 0:1], in_=sums[k][:, 1, :], axis=AX.X, op=ALU.add)

        def norm_total(k):
            norm_bank[k] = bank("turn")
            nc.tensor.matmul(norm_bank[k][:, 0:1], minus_ones[:], norm[k][:, 0:1], start=True, stop=True)

        def norm_inverse(k):
            nc.vector.reciprocal(out=norm[k][:, 1:2], in_=norm_bank[k][:, 0:1])

        def norm_spread(k):
            nc.scalar.activation(scaled_ones[k][:], ones[:], ACT.Copy, scale=norm[k][:, 1:2])

        strips = [
            (k, i, j)
            for k in range(NK)
            for i in (1, 2, 0, 3)
            for j in range(STRIPS)
            if i > 0 or j >= V_STRIPS[k]
        ]
        y_bank, y_sb, z_bank, z_stage, z_codes, z_scales = {}, {}, {}, {}, {}, {}

        def strip_y(n):
            k, i, j = strips[n]
            y_bank[n] = bank("y")
            for s in range(NS):
                x0 = 64 + P * (j - STRIPS + HELD[i]) - 64 * s
                nc.tensor.matmul_mx(
                    out=y_bank[n][:],
                    lhsT=lenv_codes[i][:, x0 : x0 + P].bitcast(FP8X4),
                    lhsT_scale=lenv_scales[i][:, x0 : x0 + P],
                    rhs=v_codes[k, s][:].bitcast(FP8X4),
                    rhs_scale=v_scales[k, s][:],
                    start=(s == 0),
                    stop=(s == NS - 1),
                )

        def strip_copy(n):
            y_sb[n] = work.tile([P, 512], F32, name="y_sb", tag="y_sb", bufs=4)
            nc.scalar.copy(out=y_sb[n][:], in_=y_bank[n][:])

        def strip_mix(n):
            z_bank[n] = bank("z")
            for e in range(4):
                nc.tensor.matmul(
                    z_bank[n][:, P * e : P * (e + 1)], y_sb[n][:, P * e : P * (e + 1)], mixer[:], start=True, stop=True
                )

        def z_tile(k, i):
            if (k, i) not in z_stage:
                tag, bufs = ("z_stage", 2) if i else ("z_stage0", 1)
                z_stage[k, i] = work.tile([P, NG, P, 4], BF16, name=tag, tag=tag, bufs=bufs, align_bytes=64)
            return z_stage[k, i]

        def strip_z(n):
            k, i, j = strips[n]
            nc.vector.tensor_tensor(
                out=z_tile(k, i)[:, :, STRIP * j : STRIP * (j + 1), :],
                in0=z_bank[n][:].rearrange("q (e g a) -> q g a e", e=4, g=NG),
                in1=gr_all[:].unsqueeze(2).to_broadcast([P, NG, STRIP, 4]),
                op=ALU.mult,
            )

        e_bank, acc = {}, {}

        def input_y(k, n):
            b, s = divmod(n, NS)
            e_bank[k, n] = bank("e")
            for e in range(4):
                nc.tensor.matmul_mx(
                    out=e_bank[k, n][:, P * e : P * (e + 1)],
                    lhsT=v_codes[k, s][:, P * e : P * (e + 1)].bitcast(FP8X4),
                    lhsT_scale=v_scales[k, s][:, P * e : P * (e + 1)],
                    rhs=lenv0_codes[:, P * b : P * (b + 1)].bitcast(FP8X4),
                    rhs_scale=lenv0_scales[:, P * b : P * (b + 1)],
                    start=True,
                    stop=True,
                )

        def add_input(k, n, g):
            width = STRIP * V_STRIPS[k]
            y = e_bank[k, n][:].rearrange("q (e a) -> q e a", e=4)[:, :, 0:width]
            w = w_all[:, n, g : g + 1]
            if n == 0:
                acc[k, g] = work.tile([P, 4, width], F32, name="acc%d" % g, tag="acc%d" % g, bufs=1)
                nc.scalar.activation(acc[k, g][:], y, ACT.Copy, scale=w)
            else:
                nc.vector.scalar_tensor_tensor(
                    out=acc[k, g][:], in0=y, scalar=w, in1=acc[k, g][:], op0=ALU.mult, op1=ALU.add
                )

        def finish_output(k, g, engine):
            width = STRIP * V_STRIPS[k]
            out = z_tile(k, 0)[:, g, 0:width, :]
            if engine == "scalar":
                for e in range(4):
                    nc.scalar.activation(out[:, :, e], acc[k, g][:, e, :], ACT.Copy, scale=gr_all[:, g, e : e + 1])
            else:
                nc.gpsimd.tensor_tensor(
                    out=out,
                    in0=acc[k, g][:].rearrange("q e a -> q a e"),
                    in1=gr_all[:, g : g + 1, :].to_broadcast([P, width, 4]),
                    op=ALU.mult,
                )

        h_bank, minus_u, q_tile, psi_q = {}, {}, {}, {}

        def z_code_tiles(k, i):
            z_codes[k, i] = work.tile([P, NG * P], U32, name="z_codes", tag="z_codes", bufs=2, align_bytes=64)
            z_scales[k, i] = work.tile([P, NG * P], U8, name="z_scales", tag="z_scales", bufs=2, align_bytes=64)

        def z_quantise(k, i, x0, x1):
            values = z_stage[k, i][:].rearrange("q g a e -> q (g a e)")
            quantise(z_codes[k, i][:, x0:x1], z_scales[k, i][:, x0:x1], values[:, 4 * x0 : 4 * x1])

        def z_quantise_tile(k, i):
            z_code_tiles(k, i)
            z_quantise(k, i, 0, NG * P)

        def h_product(k, i, t, tag):
            h_bank[k, i, t] = bank(tag)
            for c in range(NC):
                x0 = (NC * t + c) * P
                nc.tensor.matmul_mx(
                    out=h_bank[k, i, t][:],
                    lhsT=z_codes[k, i][:, x0 : x0 + P].bitcast(FP8X4),
                    lhsT_scale=z_scales[k, i][:, x0 : x0 + P],
                    rhs=renv_codes[c][:].bitcast(FP8X4),
                    rhs_scale=renv_scales[c][:],
                    start=(c == 0),
                    stop=(c == NC - 1),
                )

        def residual(k, i, t):
            minus_u[k, i, t] = work.tile([P, 512], F32, name="minus_u", tag="minus_u", bufs=4)
            nc.vector.scalar_tensor_tensor(
                out=minus_u[k, i, t][:],
                in0=h_bank[k, i, t][:],
                scalar=-1.0,
                in1=psi_ap[k, t][:, i, :],
                op0=ALU.mult,
                op1=ALU.subtract,
            )

        def precondition(k, i, t, engine):
            q_tile[k, i, t] = inverse[t, i] if k else work.tile([P, 512], F32, name="q", tag="q", bufs=8)
            e = nc.vector if engine == "vector" else nc.gpsimd
            e.tensor_tensor(out=q_tile[k, i, t][:], in0=minus_u[k, i, t][:], in1=inverse[t, i][:], op=ALU.mult)

        def overlap_product(k, i, t):
            psi_q[k, i, t] = work.tile([P, 512], F32, name="psi_q", tag="psi_q", bufs=2)
            nc.gpsimd.tensor_tensor(
                out=psi_q[k, i, t][:], in0=q_tile[k, i, t][:], in1=psi_ap[k, t][:, i, :], op=ALU.mult
            )

        def overlap_sum(k, i, t):
            j = t * TILES + i
            nc.scalar.activation(
                psi_q[k, i, t][:], psi_q[k, i, t][:], ACT.Copy, accum_out=sums[k][:, 0, j : j + 1]
            )

        def overlap_on_vector(k, i, t):
            j = t * TILES + i
            nc.vector.scalar_tensor_tensor(
                out=minus_u[k, i, t][:],
                in0=q_tile[k, i, t][:],
                scalar=1.0,
                in1=psi_ap[k, t][:, i, :],
                op0=ALU.mult,
                op1=ALU.mult,
                accum_out=sums[k][:, 0, j : j + 1],
            )

        partial, ov_bank, minus_ov = {}, {}, {}
        corr, corr_bf, turn_bank, plane_stage, plane_codes, plane_scales = {}, {}, {}, {}, {}, {}
        for k in range(NK):
            plane_scales[k] = keep.tile([P, NS * D], U8, name="plane_scales%d" % k, align_bytes=64)

        def overlap_partial(k):
            partial[k] = keep.tile([P, 1], F32, name="partial%d" % k)
            nc.vector.tensor_reduce(out=partial[k][:], in_=sums[k][:, 0, :], axis=AX.X, op=ALU.add)

        def overlap_total(k):
            ov_bank[k] = bank("turn")
            nc.tensor.matmul(ov_bank[k][:, 0:1], scaled_ones[k][:], partial[k][:], start=True, stop=True)
            minus_ov[k] = ov_bank[k][:, 0:1]

        def overlap_copy(k):
            minus_ov[k] = keep.tile([P, 1], F32, name="minus_ov%d" % k)
            nc.vector.tensor_copy(out=minus_ov[k][:], in_=ov_bank[k][:, 0:1])

        def correct(k, t, i):
            corr[k, t, i] = work.tile([P, 512], F32, name="corr", tag="corr", bufs=4)
            nc.vector.scalar_tensor_tensor(
                out=corr[k, t, i][:],
                in0=psi_ap[k, t][:, i, :],
                scalar=minus_ov[k][:, 0:1],
                in1=q_tile[k, i, t][:],
                op0=ALU.mult,
                op1=ALU.add,
            )
            nc.sync.dma_start(out=out_0[k, t, P * i : P * (i + 1), :], in_=corr[k, t, i][:])

        def round_corr(k, t, i):
            corr_bf[k, t, i] = work.tile([P, 512], BF16, name="corr_bf", tag="corr_bf", bufs=4)
            nc.scalar.copy(
                out=corr_bf[k, t, i][:].rearrange("a (u q v) -> a u q v", u=2, v=2),
                in_=corr[k, t, i][:].rearrange("a (q u v) -> a u q v", u=2, v=2),
            )

        def turn_pair(k, t, pair, tag):
            turn_bank[k, t, pair] = bank(tag)
            for x in range(4):
                i, u = 2 * pair + x // 2, x % 2
                nc.tensor.transpose(
                    turn_bank[k, t, pair][:, P * x : P * (x + 1)],
                    corr_bf[k, t, i][:].bitcast(F32)[:, P * u : P * (u + 1)],
                    ident[:],
                )

        def plane_copy(k, t, pair, engine):
            if pair == 0:
                plane_stage[k, t] = stage_tile("plane_stage%d%d" % (k, t))
            words = plane_stage[k, t][:].bitcast(F32).rearrange("q (i a u) -> q i a u", i=TILES, u=2)
            out = words[:, 2 * pair : 2 * pair + 2]
            turned = turn_bank[k, t, pair][:].rearrange("q (i u a) -> q i a u", i=2, u=2)
            if engine == "scalar":
                nc.scalar.copy(out=out, in_=turned)
            else:
                nc.vector.tensor_copy(out=out, in_=turned)

        def plane_quantise(k, t, pair_0, pair_1):
            if pair_0 == 0:
                plane_codes[k, t] = work.tile([P, D], U32, name="plane_codes", tag="plane_codes", bufs=2, align_bytes=64)
            x0, x1 = 256 * pair_0, 256 * pair_1
            quantise(
                plane_codes[k, t][:, x0:x1],
                plane_scales[k][:, D * t + x0 : D * t + x1],
                plane_stage[k, t][:, 4 * x0 : 4 * x1],
            )
            if pair_1 == 2:
                m0 = (NS * k + t) * D
                words = out_1.rearrange("g q m e -> (g q) (m e)")[:, 4 * m0 : 4 * (m0 + D)]
                nc.sync.dma_start(out=words.bitcast(I32), in_=plane_codes[k, t][:].bitcast(I32))

        def store_scales(k):
            rows = out_2.rearrange("g x m -> (g x) m")
            for x in range(4):
                nc.sync.dma_start(
                    out=rows[4 * x : 4 * x + 4, NS * D * k : NS * D * (k + 1)].bitcast(I32),
                    in_=plane_scales[k][32 * x : 32 * x + 4, :].bitcast(I32),
                )

        lenv_zeros(1)
        zero_first_columns(1)
        make_selectors()
        nc.vector.tensor_copy(out=gl_f[:], in_=gl_in[:])
        v_on_scalar(0, 1)
        v_on_vector(0, 0)
        spread_w()
        v_quantise(0, 0)
        lenv_turn(1)
        lenv_copy(1)
        make_mixer()
        v_interleave(0, 1)
        lenv_quantise(1, 0, 2)
        v_quantise(0, 1)
        lenv_quantise(1, 2, 4)
        lenv_quantise(1, 4, STRIPS)
        nc.gpsimd.memset(minus_ones[:], -1.0)
        for i in (0, 2, 3):
            zero_first_columns(i)
        lenv_turn(0)
        lenv0_copy()
        quantise(lenv0_codes[:], lenv0_scales[:], lenv_stage[0][:])
        load_second_part()

        tasks, index = [], {}

        def task(name, engine, number, length, after, fn, *args, earliest=0):
            index[name] = len(tasks)
            tasks.append((name, engine, number, length, [x for x in after if x is not None], earliest, fn, args))

        def before(kind, x, back):
            return (kind, x - back) if x >= back else None

        last_strip = {}
        for n, (k, i, j) in enumerate(strips):
            last_strip[k, i] = n
        n_last = len(strips) - 1

        for i, number in ((2, 3), (3, 6)):
            second = i == 3
            task(("lenv zeros", i), "gpsimd", number, 900, [("z", 0), ("lenv quantise", 2)] if second else [], lenv_zeros, i)
            task(
                ("lenv turn", i), "tensor", number, 930, [("lenv copy", 2)] if second else [], lenv_turn, i,
                earliest=13000 if second else 0,
            )
            task(("lenv copy", i), "scalar", number, 1000, [("lenv turn", i), ("lenv zeros", i)], lenv_copy, i)
            task(("lenv quantise", i), "vector", number + 1, 930, [("lenv copy", i)], lenv_quantise, i, 0, STRIPS)
        task("lenv 0 strips", "gpsimd", 4, 700, [], lenv0_strips_copy)
        task(("lenv quantise", 0), "vector", 6, 260, ["lenv 0 strips"], lenv0_strips_quantise)

        for c in range(NC):
            engine = "scalar" if c == 1 else "gpsimd"
            for part in range(4):
                row = ("renv part", c, part - 1) if part else ("renv part", c - 1, 0) if c else None
                task(
                    ("renv part", c, part), engine, 3 + c, 560, [row, "lenv 0 strips" if c == 3 else None],
                    renv_interleave, c, part, engine, earliest=8000 + 1000 * c,
                )
            task(("renv quantise", c), "vector", 5 + c, 490, [("renv part", c, 3)], renv_quantise, c)

        task("third loads", "sync", 0, 100, [("lenv turn", 2), ("renv part", 0, 3)], load_third_part)
        for s in range(NS):
            for e in range(4):
                row = ("v part", s, e - 1) if e else ("v part", 0, 3) if s else ("renv quantise", 3)
                task(
                    ("v part", s, e), "gpsimd", 12 + 2 * s, 990, [row, ("renv quantise", s), "third loads"],
                    v_on_gpsimd, 1, s, e, earliest=19000,
                )
            task(("v quantise", s), "vector", 15 + 2 * s, 490, [("v part", s, 3)], v_quantise, 1, s)
        second_v = [("v quantise", s) for s in range(NS)]

        for x, i in enumerate((1, 2, 3, 0)):
            for t in range(NS):
                number = 7 + 2 * (2 * x + t)
                task(("root", t, i), "scalar", number, 460, [], inverse_root, t, i, earliest=14000)
                task(("sign", t, i), "scalar", number, 460, [("root", t, i)], inverse_sign, t, i)
                task(("square", t, i), "scalar", number, 460, [("sign", t, i)], inverse_square, t, i)
                task(("inverse", t, i), "gpsimd", number + 1, 980, [("square", t, i)], inverse_join, t, i)

        for k in range(NK):
            number = (20, 30)[k]
            for x in range(NG):
                t, i = divmod(x, TILES)
                task(("psi^2", k, x), "scalar", number + x, 500, [], psi_square, k, t, i, earliest=16000 + 6000 * k)
            bank_free = ("plane copy", 3) if k else ("lenv copy", 3)
            task(("norm partial", k), "vector", number + 10, 60, [("psi^2", k, x) for x in range(NG)], norm_partial, k)
            task(("norm total", k), "tensor", number + 10, 100, [("norm partial", k), bank_free], norm_total, k)
            task(("norm inverse", k), "vector", number + 10, 70, [("norm total", k)], norm_inverse, k)
            task(("norm spread", k), "scalar", number + 11, 150, [("norm inverse", k)], norm_spread, k)

        z_stage_free = {
            (0, 1): [("lenv zeros", 2)],
            (0, 2): [("z codes", 0, 1), ("lenv zeros", 3)],
            (0, 3): [("lenv quantise", 3)],
            (1, 1): [("z codes", 0, 2)],
            (1, 2): [("z codes", 0, 3)],
            (1, 0): [("z codes", 0, 0)],
            (1, 3): [("z codes", 1, 1)],
        }
        for n, (k, i, j) in enumerate(strips):
            inputs = ([("lenv quantise", i)] if i != 1 else []) + (second_v if k else [])
            task(("y", n), "tensor", n - 1.5, 480, [before("y copy", n, 2)] + inputs, strip_y, n)
            task(("y copy", n), "scalar", n - 5, 460, [("y", n), before("mix", n, 4)], strip_copy, n)
            task(("mix", n), "tensor", n, 892, [("y copy", n), before("z", n, 2)], strip_mix, n)
            room = z_stage_free.get((k, i), []) if n == 0 or strips[n - 1][:2] != (k, i) else []
            task(("z", n), "vector", n - 1, 460, [("mix", n), before("z", n, 1)] + room, strip_z, n)

        for f in range(NK * NG * NG):
            x, g = divmod(f, NG)
            k, n = divmod(x, NG)
            number = 1 + f / 3
            columns = 64 * V_STRIPS[k]
            if g == 0:
                bank_free = [("add", x - 2, y) for y in range(NG)] if x > 1 else []
                task(("input", x), "tensor", number - 1, 290, bank_free + (second_v if k else []), input_y, k, n)
            row = ("add", x - 1, g) if n else ("finish", 0, g) if k else None
            task(
                ("add", x, g), "vector" if n else "scalar", number, 0.84 * columns + 25, [("input", x), row],
                add_input, k, n, g,
            )
            if n == NG - 1:
                engine = "gpsimd" if g % 2 else "scalar"
                length = 110 + 1.68 * columns if g % 2 else 400 + columns
                room = ("z codes", 0, 0) if k else None
                task(("finish", k, g), engine, number + 1, length, [("add", x, g), room], finish_output, k, g, engine)

        order = [(0, 1), (0, 2), (0, 3), (0, 0), (1, 1), (1, 2), (1, 0), (1, 3)]
        for m, (k, i) in enumerate(order):
            last = m == len(order) - 1
            number = last_strip[k, i] if i else last_strip[k, 3] + (2, -6)[k]
            ready = [("z", n) for n, strip in enumerate(strips) if strip[:2] == (k, i)]
            ready += [] if i else [("finish", k, g) for g in range(NG)]
            ready += [("z codes",) + order[m - 1]] if m else []
            ready += [("h", 2 * (m - 2)), ("h", 2 * (m - 2) + 1)] if m > 1 else []
            if last:
                task(("z codes", k, i), "vector", number, 10, ready, z_code_tiles, k, i)
            else:
                task(("z codes", k, i), "vector", number, 940, ready, z_quantise_tile, k, i)
            for t in range(NS):
                x, at = 2 * m + t, number + 1 + 1.5 * t
                codes, bank_free = ("z codes", k, i), before("residual", x, 1) or ("lenv copy", 3)
                if last:
                    codes, bank_free = ("z half", t), ("y copy", n_last)
                    half = NG * P // 2
                    task(codes, "vector", number, 480, [("z codes", k, i)], z_quantise, k, i, half * t, half * (t + 1))
                all_renv = [("renv quantise", c) for c in range(NC)] if m == 0 else []
                task(("h", x), "tensor", at - 2, 920, [codes, bank_free] + all_renv, h_product, k, i, t, "y" if last else "h")
                task(
                    ("residual", x), "vector", at + 1, 460,
                    [("h", x), before("residual", x, 1), before("precondition", x, 4)], residual, k, i, t,
                )
                engine = "vector" if last else "gpsimd"
                task(
                    ("precondition", x), engine, at + 2, 460 if last else 980,
                    [("residual", x), ("inverse", t, i), before("precondition", x, 1)], precondition, k, i, t, engine,
                )
                if last:
                    task(("overlap", x), "vector", at + 2, 520, [("precondition", x)], overlap_on_vector, k, i, t)
                else:
                    task(
                        ("product", x), "gpsimd", at + 2, 980,
                        [("precondition", x), before("product", x, 1), before("overlap", x, 2)], overlap_product, k, i, t,
                    )
                    task(("overlap", x), "scalar", at + 3, 500, [("product", x)], overlap_sum, k, i, t)

        for k in range(NK):
            number = n_last + 3 if k else last_strip[0, 3] + 8
            known = [("overlap", NG * k + x) for x in range(NG)]
            task(("overlap partial", k), "vector", number, 60, known, overlap_partial, k)
            task(("overlap total", k), "tensor", number, 100, [("overlap partial", k), ("norm spread", k)], overlap_total, k)
            if k == 0:
                task("overlap copy", "vector", number, 60, [("overlap total", 0)], overlap_copy, 0)
            for y in range(NG):
                x, (t, i) = NG * k + y, divmod(y, TILES)
                at = number + 1 + (1.5, 0.3)[k] * y
                known = ("overlap total", 1) if k else "overlap copy"
                task(
                    ("correct", x), "vector", at, 460, [known, before("correct", x, 1), before("round", x, 4)],
                    correct, k, t, i,
                )
                task(
                    ("round", x), "scalar", at + 1, 460,
                    [("correct", x), before("round", x, 1), before("turn", x // 2, 2)], round_corr, k, t, i,
                )
                if y % 2 == 0:
                    continue
                w, pair = x // 2, i // 2
                if k:
                    bank_free = [("z", n_last)] + [("add", 2 * NG - 1, g) for g in range(NG)]
                else:
                    bank_free = [before("plane copy", w, 1), "overlap copy", ("norm inverse", 0)]
                task(
                    ("turn", w), "tensor", at - 19 if k else at + 1, 500,
                    [("round", x), ("round", x - 1), before("turn", w, 1)] + bank_free,
                    turn_pair, k, t, pair, ("e", "z")[t] if k else "turn",
                )
                engine = "vector" if k and y != 3 else "scalar"
                task(("plane copy", w), engine, at + 4 if k else at + 1, 450, [("turn", w)], plane_copy, k, t, pair, engine)
            for t in range(NS):
                w, at = NG // 2 * k + 2 * t, number + 6 + 5 * t
                copies = [("plane copy", w), ("plane copy", w + 1)]
                if k == 0:
                    task(("planes", k, t), "vector", at, 490, copies, plane_quantise, k, t, 0, 2)
                else:
                    task(("half plane", t), "vector", at, 250, copies[:1] + [("planes", 0, t)], plane_quantise, k, t, 0, 1)
                    task(("planes", k, t), "vector", at, 250, copies[1:] + [("half plane", t)], plane_quantise, k, t, 1, 2)
            task(("scales", k), "sync", number + 12, 50, [("planes", k, t) for t in range(NS)], store_scales, k)

        followers = [[] for x in tasks]
        missing = [len(entry[4]) for entry in tasks]
        for x, entry in enumerate(tasks):
            for name in entry[4]:
                followers[index[name]].append(x)
        two_ports = (
            "z codes", "z half", "lenv quantise", "renv quantise", "v quantise", "planes", "half plane",
            "precondition", "overlap", "correct",
        )

        def takes_turns(x):
            name, engine = tasks[x][0], tasks[x][1]
            kind = name if isinstance(name, str) else name[0]
            return engine == "gpsimd" and kind != "lenv zeros" or engine == "vector" and kind in two_ports

        START, HOP, SAME_ENGINE, SCALAR_EXTRA = 7600, 260, 110, 80
        clock = {"tensor": START, "scalar": START, "vector": START + 1000, "gpsimd": START, "sync": START, "turns": 0}
        can_start = [max(START, entry[5]) for entry in tasks]
        open_tasks = [x for x in range(len(tasks)) if missing[x] == 0]
        plan = []
        while open_tasks:
            start, number, x = min(
                (
                    max(clock[tasks[x][1]], can_start[x], clock["turns"] if takes_turns(x) else 0),
                    tasks[x][2],
                    x,
                )
                for x in open_tasks
            )
            open_tasks.remove(x)
            engine = tasks[x][1]
            end = start + tasks[x][3] + (SCALAR_EXTRA if engine == "scalar" else 0)
            clock[engine] = end
            if takes_turns(x):
                clock["turns"] = end
            plan.append(x)
            for y in followers[x]:
                missing[y] -= 1
                wait = HOP if tasks[y][1] != engine else 0 if engine == "tensor" else SAME_ENGINE
                can_start[y] = max(can_start[y], end + wait)
                if missing[y] == 0:
                    open_tasks.append(y)
        assert len(plan) == len(tasks)
        for x in plan:
            tasks[x][6](*tasks[x][7])
